import numpy as np, ml_dtypes
CORES = [51,54,179,182]
N = 4
BF = ml_dtypes.bfloat16
def gentries(a):
    return np.ascontiguousarray(a.reshape(8, 16, -1).transpose(0, 2, 1)).reshape(8, -1)
def gtable(e):
    e = np.asarray(e); return np.ascontiguousarray(e.reshape(8, -1, 16).transpose(0, 2, 1)).reshape(128, -1).astype(np.int32)
V, G, L, SH, RO = 512, 256, 4096, 4, 2
W = V + (N - 1) * G; NV = N * V; TOP = 32640; END = 2 ** 23
def place(x, r):
    d = (r - x // V) % N
    return np.where(d == 0, x % V, V + (d - 1) * G + x % V)
def rising(x, n):
    x = np.sort(x, axis=-1); x[..., 1:] = np.where(x[..., 1:] == x[..., :-1], NV, x[..., 1:]); x = np.sort(x, axis=-1)
    return np.where((np.arange(4) < n[..., None]) & (x < NV), x, -1)
def counts(rng):
    return rng.choice(np.array([0, 1, 2, 2, 3, 3, 4]), (N, 8, 3, V))
def parts(rng, size, share, n):
    nets = rng.integers(0, W, (N, 8, 2 * V)); lv = np.zeros((N, 8, 3, V, 4), np.int64); r = np.arange(N)[:, None]
    for g in range(8):
        p = int(size[g])
        if p <= N * G // 2:
            x = rng.permutation(N * G)[:p]; pool = np.sort(x // G * V + x % G)
            nets[:, g] = np.where(rng.random((N, 2 * V)) < share, place(pool[rng.integers(0, p, (N, 2 * V))], r), nets[:, g])
        else:
            pool = np.sort(rng.permutation(NV)[:p])
        lv[:, g] = pool[rng.integers(0, p, (N, 3, V, 4))]
    tb = rng.integers(0, 65536, (N, 8, 3, V))
    return nets, rising(lv, n), tb, rng.integers(0, TOP + 1, (N, 8, 16, L)), rng.integers(0, 20001, (N, 8, 16, V))
def pack(nets, lv, tb, ce, rq):
    return {"fan": np.stack([gtable(x) for x in nets]), "cells": ce.reshape(N, 128, L).astype(np.float32).astype(BF), "req": rq.reshape(N, 128, V).astype(np.float32).astype(BF),
            "leaf0": np.ascontiguousarray(lv.transpose(0, 1, 2, 4, 3)).reshape(N, 8, 12 * V).astype(np.int32), "tab0": tb.reshape(N, 8, 3 * V).astype(np.int32)}
def setup_inputs(rng):
    return pack(*parts(rng, rng.permutation(np.array([4, 6, 8, 12, 20, 28, 200, NV])), 0.4, counts(rng)))
def setup_inputs_ties(rng):
    nets, lv, tb, ce, rq = parts(rng, rng.permutation(np.array([4, 5, 6, 8, 10, 12, 16, 24])), 0.5, counts(rng))
    ce = 256 * rng.integers(0, 3, ce.shape); rq = 256 * rng.integers(0, 2, rq.shape)
    g = rng.permutation(8); ce[:, g[0]] = 1024; rq[:, g[0]] = 0
    for i in (1, 2): ce[:, g[i]] = rng.integers(0, 2, ce[:, g[i]].shape); rq[:, g[i]] = 0
    rq = np.where(rng.random((N, 8, 1, V)) < 0.1, TOP, rq)
    return pack(nets, lv, tb, ce, rq)
def setup_inputs_bare(rng):
    n = counts(rng); n[:, ::2] = 0; n[:, 5] = rng.integers(0, 2, (N, 3, V)); n[rng.integers(0, N)] = 0
    nets, lv, tb, ce, rq = parts(rng, rng.permutation(np.array([4, 6, 8, 12, 20, 28, 200, NV])), 0.4, n)
    nets[:, 1] = np.tile(np.arange(V), 2); nets[:, 3, V:] = nets[:, 3, :V]; nets[:, 4, V::2] = nets[:, 4, :V:2]
    return pack(nets, lv, tb, ce, rq)
def setup_inputs_ends(rng):
    nets, lv, tb, ce, rq = parts(rng, np.full(8, 8), 0.0, counts(rng))
    for g in range(8):
        p = (4, 5, 6, 8)[g % 4]
        pool = np.sort(np.concatenate([np.array([0, NV - 1]), 1 + rng.permutation(NV - 2)[:p - 2]]))
        lv[:, g] = rising(pool[np.argsort(rng.random((N, 3, V, p)), axis=-1)[..., :4]], np.full((N, 3, V), 4))
        if g % 2 == 1: nets[:, g] = rng.choice(np.array([0, V - 1, V, W - 1]), (N, 2 * V))
    tb = np.where(rng.random(tb.shape) < 0.6, rng.choice(np.array([0, 65535, 1, 32768, 43690, 65534]), tb.shape), tb)
    ce = np.where(rng.random(ce.shape) < 0.4, TOP * rng.integers(0, 2, ce.shape), ce); ce[:, :, :, 0] = rng.integers(0, TOP + 1, (N, 8, 16)); ce[:, 7] = np.where(rng.random((N, 16, L)) < 0.98, TOP, ce[:, 7])
    rq = np.where(rng.random(rq.shape) < 0.2, rng.choice(np.array([0, 1, TOP]), rq.shape), rq); rq = np.where(rng.random((N, 8, 1, V)) < 0.1, 0, rq)
    return pack(nets, lv, tb, ce, rq)
def setup_inputs_alike(rng):
    nets, lv, tb, ce, rq = parts(rng, rng.integers(3, 7, 8), 1.0, counts(rng))
    lv[:, ::2, 1:] = lv[:, ::2, :1]; tb[:, ::2, 1:] = tb[:, ::2, :1]
    return pack(nets, lv, tb, ce, rq)
def setup_inputs_spread(rng):
    nets, lv, tb, ce, rq = parts(rng, rng.permutation(np.array([4, 6, 8, 12, 20, 28, 200, NV])), 0.4, counts(rng))
    ce = np.minimum(np.floor(np.exp2(15 * rng.random((N, 8, 1, L))) * rng.random((N, 8, 16, L))), TOP)
    rq = np.minimum(np.floor(np.exp2(15 * rng.random((N, 8, 1, V))) * rng.random((N, 8, 16, V))), TOP)
    w = rng.random(tb.shape); t2 = rng.integers(0, 65536, tb.shape); t3 = rng.integers(0, 65536, tb.shape)
    tb = np.where(w < 0.3, tb & t2 & t3, np.where(w < 0.6, tb | t2 | t3, tb))
    nets[:, ::2] = np.where(rng.random((N, 4, 2 * V)) < 0.5, np.floor(W * rng.random((N, 4, 2 * V)) ** 3).astype(np.int64), nets[:, ::2])
    return pack(nets, lv, tb, ce, rq)
def check_inputs(d):
    bad = []
    for k, lo, hi in (("fan", 0, W - 1), ("cells", 0, TOP), ("req", 0, TOP), ("leaf0", -1, NV - 1), ("tab0", 0, 65535)):
        x = np.asarray(d[k]).astype(np.float32)
        if not (np.all(x >= lo) and np.all(x <= hi) and np.all(np.floor(x) == x)): bad.append("range of " + k)
    x = np.asarray(d["leaf0"]).reshape(-1, 4, V); a, b = x[:, :-1], x[:, 1:]
    if not np.all((b == -1) | ((a >= 0) & (b > a))): bad.append("order of leaf0")
    return bad
def old_rows():
    o = np.zeros((16, 16), np.int32)
    for s in range(16):
        k = 0
        for p in range(4):
            if (s >> p) & 1:
                o[s] |= (((np.arange(16) >> p) & 1) << k).astype(np.int32); k += 1
    return o
OLD = old_rows()
def turned(x, u, t):
    p = np.sum(u[..., None, :] < x[..., :, None], axis=-1)
    s = np.sum(np.where((x < NV) & (p < 4), 1 << np.minimum(p, 3), 0), axis=-1)
    return (t[..., None] >> OLD[s]) & 1
def reference(fan, cells, req, leaf0, tab0):
    lv = leaf0.astype(np.int32).reshape(N, 8, 3, 4, V).transpose(0, 1, 2, 4, 3); lv = np.where(lv < 0, np.int32(NV), lv)
    tb = tab0.astype(np.int32).reshape(N, 8, 3, V); co = np.full((N, 8, 3, V), -1, np.int32)
    nets = np.stack([gentries(x) for x in fan]).astype(np.int64).reshape(N, 8, 2, V)
    ce = cells.astype(np.float32).astype(np.int32).reshape(N, 8, 16, L); rq = req.astype(np.float32).astype(np.int32).reshape(N, 8, 16, V)
    own = np.full((N, 8, 1, V, 4), NV, np.int32); own[..., 0] = np.arange(NV, dtype=np.int32).reshape(N, 1, 1, V)
    triv = np.full((N, 8, 1, V), 43690, np.int32); bits = np.arange(16, dtype=np.int32)
    for rnd in range(RO):
        al = np.concatenate([lv, own], axis=2); at = np.concatenate([tb, triv], axis=2)
        lv = np.full_like(lv, NV); tb = np.zeros_like(tb); co = np.full_like(co, -1)
        for r in range(N):
            wl = np.concatenate([al[r]] + [al[(r - d) % N][:, :, :G] for d in range(1, N)], axis=2)
            wt = np.concatenate([at[r]] + [at[(r - d) % N][:, :, :G] for d in range(1, N)], axis=2)
            ia = nets[r, :, 0][:, None, :]; ib = nets[r, :, 1][:, None, :]
            xa = np.repeat(np.take_along_axis(wl, ia[..., None], 2), 4, axis=1); ta = np.repeat(np.take_along_axis(wt, ia, 2), 4, axis=1)
            xb = np.tile(np.take_along_axis(wl, ib[..., None], 2), (1, 4, 1, 1)); tc = np.tile(np.take_along_axis(wt, ib, 2), (1, 4, 1))
            both = np.sort(np.concatenate([xa, xb], axis=-1), axis=-1)
            both[..., 1:] = np.where(both[..., 1:] == both[..., :-1], np.int32(NV), both[..., 1:]); both = np.sort(both, axis=-1)
            u = both[..., :4]; void = (both[..., 4] < NV) | (xa[..., 0] == NV) | (xb[..., 0] == NV)
            t = (65535 - np.sum((turned(xa, u, ta) & turned(xb, u, tc)) << bits, axis=-1)).astype(np.int32)
            c1 = ((t + 29 * (t >> 5)) & (L - 1)).reshape(8, 1, 16 * V); c2 = (t >> SH).reshape(8, 1, 16 * V)
            e = np.minimum(np.take_along_axis(ce[r], c1, 2), np.take_along_axis(ce[r], c2, 2)).reshape(8, 16, 16, V)
            cost = np.sum(np.maximum(e - rq[r][:, :, None, :], 0), axis=1)
            key = np.where(void, END, 16 * cost + np.arange(16)[None, :, None])
            for c in range(3):
                k = np.min(key, axis=1); full = k < END; i = (k & 15)[:, None, :]
                lv[r, :, c] = np.where(full[..., None], np.take_along_axis(u, i[..., None], 1)[:, 0], NV)
                tb[r, :, c] = np.where(full, np.take_along_axis(t, i, 1)[:, 0], 0); co[r, :, c] = np.where(full, k >> 4, -1)
                key = np.where((key >> 4) == (k >> 4)[:, None, :], END, key)
    yl = np.where(lv == NV, -1, lv).transpose(0, 1, 2, 4, 3)
    return {"yl": np.ascontiguousarray(yl).reshape(N, 8, 12 * V).astype(np.float32), "yt": tb.reshape(N, 8, 3 * V).astype(np.float32), "yc": co.reshape(N, 8, 3 * V).astype(np.float32)}

@@ -1,0 +1,611 @@
+import numpy as np
+from concourse.bass import DstId, RemoteDMATransfer
+from concourse.mybir import AluOpType as AL, ActivationFunctionType as AF
+
+V, NR, BORD, WN = 512, 4, 256, 1280
+w, WB, GW, QS = 256, 128, 64, 4
+NCH, NS = V // w, w // 16
+LUTW, VOID = 6144, 9008
+WW = LUTW + 3 * WN
+N_ = None
+P16 = list(range(16))
+KK = [p >> 2 for p in P16]
+LL = [p & 3 for p in P16]
+MARG, OVH, PEC, GC = 0.2, 0.06, 0.5e-3, 1.56
+
+
+def _old(s):
+    o, k = [0] * 16, 0
+    for p in range(4):
+        if s >> p & 1:
+            o = [o[m] | (((m >> p) & 1) << k) for m in P16]
+            k += 1
+    return o
+
+
+WC1 = [((1 << m) + (29 * (1 << (m - 5)) if m >= 5 else 0)) % 4096 for m in P16]
+WC1 = [x - 4096 * (x > 2048) for x in WC1]
+HZ, HK, W3 = [0, 1, 1, 2, 2, 2], [0, 0, 1, 0, 1, 2], [256, 512, -256]
+_bh = [128 + 768 * HK[c] + 256 * HZ[c] for c in range(6)]
+VEC = [{
+    "bR": [3, 6, 9, 3, 6, 9, 0, 0] * 2, "bVoid": [[-12, -3, -6][(KK[p] == 3) + (LL[p] == 3)] for p in P16], "bX": [0, -2048] * 8,
+    "bIa": [256 * (18 + 5 * KK[p]) if KK[p] < 3 else 170 for p in P16],
+    "bIb": [256 * (18 + 5 * LL[p]) if LL[p] < 3 else 170 for p in P16],
+    "wV": [7 / 2048, -1 / 2048, -1 / 2048, -1 / 2048] * 4, "wP": [[0, 1, 1, -(18 + 5 * KK[p]) / 8][LL[p]] for p in P16],
+    "valo": W3 + [0] * 13, "vahi": [0] * 8 + W3 + [0] * 5, "vblo": [0] * 3 + W3 + [0] * 10, "vbhi": [0] * 11 + W3 + [0] * 2,
+    "w3": (W3 + [0]) * 3 + [256, 0, 0, 0], "wb": [0, 0, 0, 256] * 3 + [0, 256, 0, 0],
+}, {
+    "is12": [0] * 12 + [1, 0, 0, 0], "nwc1": [-x for x in WC1], "zrow": HZ * 2 + [9] * 4, "u3": [1] * 12 + [-1] * 4,
+    "ua": [1] * 4 + [0] * 12, "bU": [2048, 6144, 10240, -18432] * 3 + [0] * 4, "padAB": [2048] * 4 + [-4096] * 4 + [0] * 8,
+    "bAB3": [0, 2048, 2048, 2048, 0, -4096, -4096, -4096] + [0] * 8, "thr": [2048] * 13 + [131072] * 3,
+    "bH": _bh + [x - 4096 for x in _bh] + [-896] * 4,
+}]
+VN = list(VEC[0]) + list(VEC[1])
+NV0, NVT = len(VEC[0]), len(VN)
+PHI = {}
+for _i in range(6):
+    PHI["S" + "AB"[_i // 3] + str(_i % 3)] = [4 * (_i % 3) + x for x in (KK, LL)[_i // 3]]
+PHI.update({"COL": P16, "RID": [12] * 16, "XC": [N_, N_, 12, N_] * 3 + [N_] * 4,
+            "XL": [N_, N_, N_, 13, N_, N_, N_, 14, N_, N_, N_, 15] + [N_] * 4,
+            "XP": [N_, N_, 3, 3, N_, N_, 7, 7, N_, N_, 11, 11] + [N_] * 4, "XA": [2 * x for x in KK], "XB": [2 * x + 1 for x in LL]})
+for _i in range(4):
+    PHI["SEL%d" % _i] = [N_] * 4 + ([4 * _i + x for x in range(4)] if _i < 3 else [12, N_, N_, N_]) + [N_] * 8
+PHI.update({"HB": [N_] * 6 + [4 + x for x in HK] + [4, 5, 6, 7], "HA": HK + [N_] * 10, "CK": KK, "CL": LL,
+            "VT1": [N_, N_, N_, 0, N_, N_, N_, 1, N_, N_, N_, 2, N_, N_, N_, 3], "VT2": [N_] * 12 + [0, 1, 2, N_]})
+for _i, _m in enumerate([8, 12, 10, 9, 14, 13, 7, 11]):
+    PHI["LUT%d" % _i] = _old(_m)
+PN = list(PHI)
+FM = [["SA0", "SA1", "SA2", "SB0", "SB1", "SB2", "COL", "RID"], ["XC", "XL", "XP", "XLn", "XA", "XB", "VPa", "VPb", "PA3", "PB3"],
+      ["SEL0", "SEL1", "SEL2", "SEL3", "HB", "HA", "UH", "UA", "E12"]]
+BM = [["LUT%d" % i for i in range(8)], ["Zs", "Ze", "T1s", "T2s", "Te", "VT1", "VT2", "Zp1", "A1", "B1", "A4", "B4", "T1a", "T1b", "T2a", "T2b"],
+      ["Zc1", "Zc2", "IV", "Zm1", "ONE", "Hs", "He", "BH", "Zlb", "ZT"]]
+FN, BN = sum(FM, []), sum(BM, [])
+f32, f16, b16, i32, u16 = "float32", "float16", "bfloat16", "int32", "uint16"
+_S = [("fanI", 64, i32), ("fanU", 64, u16), ("LI", V, i32), ("IDI", V, i32), ("TR", 3 * V, i32), ("CE", VOID + 16, b16), ("RQ", V, b16),
+      ("Gw0", WN, f32), ("Gw1", WN, f32), ("W0", WW, b16), ("W1", WW, b16), ("WF", 3 * V, b16), ("IW", WN, f32), ("Gc", 2 * V, f16),
+      ("IDf", V, f16), ("PI", 8, i32), ("PJ", 8, i32), ("PF", 8, f32), ("GI", 8, f32), ("GM", 8, f32), ("HC", 2, f32), ("PM", 4, f32),
+      ("VAL", 16 * NVT, f32), ("OHI", 16 * NVT, f32), ("OH", 16 * NVT, f32), ("VC", 16 * NVT, f32), ("RST", 256, f32),
+      ("POWR", 48, f32), ("POWC", 32, f32), ("TWO", 32, f32), ("PW2", 4, f32), ("TM", 96, f32),
+      ("D0", 128, f32), ("SW", 512, f32), ("KC", 128, b16), ("KI", 128, f32), ("ON", 512, b16), ("BYI", 256, i32), ("BYB", 256, b16),
+      ("NI", 256, i32), ("NL", 256, u16), ("BCI", 16, i32), ("BC", 16, u16), ("VNI", 3 * NS, f32), ("VNN", 3 * NS, f32),
+      ("Y", V, f32), ("YP", w, f32), ("YC", V, f32), ("CB", w, f32),
+      ("SG", 11 * w, b16), ("NE", 11 * w, b16), ("RR", 7 * w, b16), ("XX", w, f16), ("AG", 16 * w, b16), ("CG", 16 * w, b16),
+      ("XM", 16 * w, b16), ("NK", 3 * w, f32), ("KP", w, f32), ("SC", 3 * w, f32), ("CA", 3 * w, f16), ("CN", 3 * w, f16),
+      ("S2", 3 * w, b16), ("E2", 3 * w, b16), ("HH", 3 * w, f16), ("TT", 3 * NS, i32), ("Q", 21 * NS, f32), ("QI", 3 * NS, i32),
+      ("LV", 9 * NS, f32), ("LU", 9 * NS, u16)]
+for _h in range(NCH):
+    _S += [("GG%d" % _h, 5 * w, f16), ("VD%d" % _h, w, b16), ("IX%d" % _h, 4 * w, u16), ("AN%d" % _h, 16 * w + 16, b16), ("AB%d" % _h, 4 * w + 8, f32)]
+SCRATCH = {n: ("sbuf", [128, k], d) for n, k, d in _S}
+SCRATCH.update({"PH": ("sbuf", [128, len(PN), 16], f32), "MF": ("sbuf", [128, len(FN), 16], f16), "MB": ("sbuf", [128, len(BN), 16], b16),
+                "BF": ("sbuf", [128, len(FN), 144], f16), "BB": ("sbuf", [128, len(BN), 144], b16)})
+for _b in range(8):
+    SCRATCH["ps%d" % _b] = ("psum", [128, 512], f32)
+SEMAPHORES = ["sv", "sa", "st", "sg", "loc"] + ["d%d" % i for i in range(12)] + ["ar%d" % i for i in range(4)]
+EST = []
+
+
+def _cover(L):
+    out, s = [], 0
+    while s < len(L):
+        best, base = None, (L[s] if L[s] is not None else -1)
+        for n1 in range(1, min(16, len(L) - s) + 1):
+            for s1 in ({L[s + 1] - base} if n1 > 1 and L[s + 1] is not None else {0, 100}):
+                for s2 in ({0, L[s + n1] - base} if s + n1 < len(L) and L[s + n1] is not None else {0, 100}):
+                    n2 = 0
+                    if max(abs(s1), abs(s2)) > 32767: continue
+                    while s + (n2 + 1) * n1 <= len(L) and all(
+                            (not 0 <= base + n2 * s2 + j * s1 <= 15) if L[s + n2 * n1 + j] is None else base + n2 * s2 + j * s1 == L[s + n2 * n1 + j]
+                            for j in range(n1)):
+                        n2 += 1
+                    if n2 and (best is None or n1 * n2 > best[0]): best = (n1 * n2, [[s2, n2], [s1, n1]], base)
+        out.append((s,) + best); s += best[0]
+    return out
+
+
+def _prog(L):
+    out = []
+    for x in sorted(set(L) - {0}):
+        rest = {i for i, y in enumerate(L) if y == x}
+        while rest:
+            best = None
+            for a in sorted(rest):
+                for st in [1] + [b - a for b in sorted(rest) if b > a]:
+                    n = 1
+                    while a + n * st in rest and n < 32: n += 1
+                    if best is None or n > best[2]: best = (a, st, n)
+            out.append(best + (float(x),)); rest -= {best[0] + k * best[1] for k in range(best[2])}
+    return out
+
+
+def rank_program(g, core, T, topo):
+    rank = T.rank_of(core)
+    if rank is None:
+        return
+    ops, lastw, readers = [], {}, {}
+    vec, act, ten = g.vector, g.scalar, g.tensor
+    CY = 0.83e-3
+
+    def add(alts, R, Wr, lat=0.0, sem=None, cnt=1):
+        i, deps, eng = len(ops), set(), "".join(alts)
+        for t in list(R) + list(Wr):
+            if t in lastw: deps.add(lastw[t])
+            if t.startswith("ps") and t != "ps7": deps.update(j for j in readers.get(t, ()) if ops[j]["e"] != eng or len(eng) > 1)
+        for t in Wr: deps.update(readers.get(t, ()))
+        for t in R: readers.setdefault(t, []).append(i)
+        for t in Wr: lastw[t] = i; readers[t] = []
+        deps.discard(i)
+        ops.append({"e": eng, "a": alts, "d": deps, "l": lat, "s": sem, "n": cnt, "k": (list(Wr) + ["-"])[0]})
+        return i
+
+    def nel(ap): return int(np.prod(ap.shape[1:]))
+
+    def cv(out, cy): return OVH + max(64, nel(out) * cy) * CY
+
+    def vts(out, in0, s1, s2, o0, o1, cy=1.0):
+        if o1 is None: return (lambda: vec.tensor_scalar(out, in0, s1, None, o0)), cv(out, cy)
+        return (lambda: vec.tensor_scalar(out, in0, s1, s2, o0, o1)), cv(out, cy)
+
+    def vcp(out, a, cy=1.0): return (lambda: vec.tensor_copy(out, a)), cv(out, cy)
+
+    def aac(out, a, fn, bias=0.0, scale=1.0, cy=1.0): return (lambda: act.activation(out, a, fn, bias, scale)), cv(out, cy) + 0.02
+
+    def ts(out, in0, s1, s2, o0, o1, R, Wr, cy=1.0): add({"v": vts(out, in0, s1, s2, o0, o1, cy)}, R, Wr)
+
+    def tt(out, a, b, o, R, Wr, cy=2.0): add({"v": (lambda: vec.tensor_tensor(out, a, b, o), cv(out, cy))}, R, Wr)
+
+    def cp(out, a, R, Wr, cy=1.0): add({"v": vcp(out, a, cy)}, R, Wr)
+
+    def fcp(out, a, R, Wr, cy=1.0): add({"v": vcp(out, a, cy), "a": aac(out, a, AF.Copy, cy=cy)}, R, Wr)
+
+    def faff(out, a, sc, bi, R, Wr, cy=1.0, cyv=None):
+        add({"v": vts(out, a, sc, bi, AL.mult, AL.add, cyv or cy), "a": aac(out, a, AF.Identity, bi, sc, cy)}, R, Wr)
+
+    def frelu(out, a, bi, R, Wr): add({"v": vts(out, a, bi, 0.0, AL.add, AL.max), "a": aac(out, a, AF.Relu, bi)}, R, Wr)
+
+    def fsign(out, a, R, Wr): add({"v": vts(out, a, -1.0, 1.0, AL.max, AL.min), "a": aac(out, a, AF.Sign)}, R, Wr)
+
+    def fne(out, a, R, Wr): add({"v": vts(out, a, 0.0, None, AL.not_equal, None, 0.5), "a": aac(out, a, AF.Abs)}, R, Wr)
+
+    def ms(out, c, Wr, cy=1.0): add({"v": (lambda: vec.memset(out, c), cv(out, cy))}, [], Wr)
+
+    def scan(out, d0, d1, init, o0, o1, R, Wr): add({"v": (lambda: vec.tensor_tensor_scan(out, d0, d1, init, o0, o1), cv(out, 1))}, R, Wr)
+
+    def tr(out, a, R, Wr): add({"v": (lambda: vec.transpose(out, a), cv(out, 1))}, R, Wr)
+
+    def ac(out, a, R, Wr): add({"a": aac(out, a, AF.Copy, cy=GC)}, R, Wr)
+
+    def mm(out, pairs, R, Wr, k=1, st=True, sp=True):
+        def f():
+            for n, (l, r) in enumerate(pairs): x = ten.matmul(out, l, r, st and n == 0, sp and n == len(pairs) - 1)
+            return x
+        add({"t": (f, 0.05 + len(pairs) * (0.01 + max(64, nel(out)) * k * PEC))}, R, Wr)
+
+    def mms(out, parts, Wr):
+        for n, (pairs, R) in enumerate(parts): mm(out, pairs, R, Wr, 1, n == 0, n == len(parts) - 1)
+
+    def io(out, pat, base, cm, Wr, fl=True):
+        if fl: f = lambda: g.iota(out, pat, base, cm, allow_small_or_imprecise_dtypes=True)
+        else: f = lambda: g.iota(out, pat, base, cm)
+        add({"g": (f, 0.13 + 2 * nel(out) * CY)}, [], Wr)
+    nd = [0]
+
+    def dma(q, prs, R, Wr, lat=2.5):
+        s, eng = "d%d" % nd[0], {"s": g.sync, "a": g.scalar}[q]
+        nd[0] += 1
+
+        def f():
+            for o, i in prs: eng.dma_start(o, i).then_inc(T.sem[s], 16)
+        add({q: (f, 0.06 * len(prs))}, R, Wr, lat, s, 16 * len(prs))
+
+    def deal(src):
+        ds = [c for c in T.cores if c != src]
+        far = [c for c in ds if c not in topo.cores_of(src)]
+        used, res = set(), {}
+        for c in far + [c for c in ds if c not in far]:
+            pool = [e for e in topo.engines(src, c) if e not in used]
+            share, n = len(pool) // (len([x for x in far if x not in res]) if c in far else 1), 1
+            while 2 * n <= min(share, 4): n *= 2
+            res[c] = pool[:n]; used.update(pool[:n])
+        return res
+    mine = deal(core)
+    inc_in = sum(len(deal(c)[core]) for c in T.cores if c != core)
+    locn = [0]
+
+    def send(buf, offs, sem, R, Wr, lat):
+        def f():
+            for o in offs:
+                trs = []
+                for d in range(1, NR):
+                    c = T.cores[(rank + d) % NR]
+                    rid, pid = topo.addr(c, core)
+                    trs.append(RemoteDMATransfer(dst_ids=[DstId(rid=rid, pnc=pid)], dma_engine_mask=sum(1 << e for e in mine[c]), remote_sem=T.sem[sem],
+                                                 src=buf[:, o:o + BORD], dst=buf[:, o + V + (d - 1) * BORD:o + V + d * BORD]))
+                g.remote_dma_fused(trs, local_sem=T.sem.loc)
+        locn[0] += len(offs) * sum(len(x) for x in mine.values())
+        i = add({"g": (f, 0.3 * len(offs))}, R, [], 0.0, "loc", 0)
+        ops[add({"x": (None, 0.0)}, [], Wr, lat, sem, inc_in * len(offs))]["o"] = i
+
+    def send_g(r): send(T["Gw%d" % r], [0], "ar%d" % (2 * r), ["Gw%d_0" % r], ["Gw%dr" % r], 4.0)
+
+    def send_b(r): send(T["W%d" % r], [LUTW + WN * c for c in range(3)], "ar%d" % (2 * r + 1), ["W%d_0_%d" % (r, c) for c in range(3)], ["W%dr" % r], 5.0)
+
+    dma("s", [(T.LI[f::16, :], T.leaf0[:, f * V:(f + 1) * V]) for f in range(8)], [], ["LIa"])
+    dma("a", [(T.LI[f::16, :], T.leaf0[:, f * V:(f + 1) * V]) for f in range(8, 12)] +
+        [(T.LI[13 + c::16, :], T.tab0[:, c * V:(c + 1) * V]) for c in range(3)] + [(T.fanI[:], T.fan[:])], [], ["LIb", "fanI"])
+    io(T.PI[:, 0:1], [[0, 1]], 0, 1, ["PI"], False)
+    io(T.IDI[:], [[1, V]], V * rank, 0, ["IDI"], False)
+    dma("s", [(T.LI[12::16, :], T.IDI[12::16, :])], ["IDI"], ["LIc"], 2.0)
+    dma("s", [(T.TR[m::16, :], T.tab0[:]) for m in range(16)], [], ["TR"], 3.0)
+    dma("s", [(T.RQ[:], T.req[:]), (T.CE[:, 0:4096], T.cells[:]), (T.CE[:, 4096:8192], T.cells[:]), (T.CE[:, 8192:VOID], T.cells[:, 0:VOID - 8192])],
+        ["TR"], ["RQ", "CEa"], 12.0)
+    ms(T.CE[:, VOID:], 65536.0, ["CEb"])
+
+    for n, (sh, an) in enumerate([(0, 15), (2, 3), (0, 3), (1, 7), (4, 7), (4, 1), (0, 31)]):
+        ts(T.PJ[:, n:n + 1], T.PI[:, 0:1], sh, an, AL.logical_shift_right, AL.bitwise_and, ["PI"], ["PJ%d" % n])
+    cp(T.PF[:, 0:7], T.PJ[:, 0:7], ["PJ%d" % n for n in range(7)], ["PF"])
+    p16, kc, lc, q2, gc_, hc, c32 = [T.PF[:, n:n + 1] for n in range(7)]
+    io(T.GI[:], [[1, 8]], 0, 0, ["GI"])
+    ts(T.GM[:], T.GI[:], gc_, None, AL.is_equal, None, ["GI", "PF"], ["GM"])
+    ts(T.HC[:], T.GI[:, 0:2], hc, None, AL.is_equal, None, ["GI", "PF"], ["HC"])
+    io(T.OHI[:], [[0, NVT], [1, 16]], 0, 0, ["OHI"])
+    ms(T.RST[:], 1.0, ["RST"]); ms(T.RST[:, 0::16], 0.0, ["RST"]); ms(T.VAL[:, 0:16 * NV0], 0.0, ["VAL"])
+    ms(T.TWO[:, 0:16], 2.0, ["TWO"]); ms(T.TWO[:, 16:32], 0.5, ["TWO"]); ms(T.POWR[:, 32:48], 0.0, ["ZR"])
+    for b, (a0, a1) in enumerate([(0, 16 * NV0), (16 * NV0, 16 * NVT)]):
+        tk, L = [], [x for y in VEC[b].values() for x in y]
+        for s, n, pat, base in (_cover(L) if b else []):
+            tk.append("VAL%d_%d" % (b, s)); io(T.VAL[:, a0 + s:a0 + s + n], pat, base, 0, [tk[-1]])
+        for s, st, n, x in ([] if b else _prog(L)):
+            o = T.VAL[:, a0 + s:a0 + s + (n - 1) * st + 1:st]
+            tk.append("VAL%d_%d" % (b, s))
+            add({"v": (lambda o=o, x=x: vec.memset(o, x), cv(o, 1)), "a": aac(o, T.TWO[:, 0:n], AF.Identity, x, 0.0)}, ["VAL", "TWO"], [tk[-1]])
+        ts(T.OH[:, a0:a1], T.OHI[:, a0:a1], p16, None, AL.is_equal, None, ["OHI", "PF"], ["OH%d" % b])
+        tt(T.OHI[:, a0:a1], T.OH[:, a0:a1], T.VAL[:, a0:a1], AL.mult, tk + ["OH%d" % b], ["OP%d" % b])
+        scan(T.VC[:, a0:a1], T.RST[:, 0:a1 - a0], T.OHI[:, a0:a1], 0.0, AL.mult, AL.add, ["OP%d" % b, "RST"], ["VC%d" % b])
+
+    def vc(n): return T.VC[:, 16 * VN.index(n) + 15:16 * VN.index(n) + 16]
+    V0, V1 = "VC0", "VC1"
+    scan(T.POWR[:, 0:16], T.TWO[:, 0:16], T.POWR[:, 32:48], 0.5, AL.mult, AL.add, ["TWO", "ZR"], ["PWa"])
+    scan(T.POWR[:, 16:32], T.TWO[:, 16:32], T.POWR[:, 32:48], 65536.0, AL.mult, AL.add, ["TWO", "ZR"], ["PWb"])
+    tt(T.POWC[:], T.POWR[:, 0:32], T.OH[:, 0:32], AL.mult, ["PWa", "PWb", "OH0"], ["PWc"])
+    scan(T.POWR[:, 0:32], T.RST[:, 0:32], T.POWC[:], 0.0, AL.mult, AL.add, ["PWc", "RST"], ["PWa", "PWb"])
+    w2m, w15 = T.POWR[:, 15:16], T.POWR[:, 31:32]
+    ts(T.PW2[:, 0:1], w2m, 16.0, w2m, AL.is_ge, AL.mult, ["PWa"], ["PW2a"])
+    ts(T.PW2[:, 1:2], w2m, 200.0, w2m, AL.is_le, AL.mult, ["PWa"], ["PW2b"])
+
+    ts(T.PM[:, 0:1], p16, 13.0, 15.0, AL.is_ge, AL.mult, ["PF"], ["PM"])
+    ts(T.PM[:, 1:2], T.PM[:, 0:1], 1.0, None, AL.add, None, ["PM"], ["PM1"])
+    ts(T.PM[:, 2:3], T.PM[:, 0:1], -1 / 16, 1.0, AL.mult, AL.add, ["PM"], ["PM2"])
+    ts(T.PM[:, 3:4], p16, 8.0, vc("bR"), AL.is_lt, AL.mult, ["PF", V0], ["PM3"])
+    for h in range(NCH):
+        x = T.LI[:, h * w:(h + 1) * w]
+        ts(x, x, T.PM[:, 1:2], None, AL.mult, None, ["LIa", "LIb", "LIc", "PM1"], ["LI%d" % h])
+        ts(x, x, 4095, None, AL.bitwise_and, None, ["LI%d" % h], ["LI%d" % h])
+        ts(T.Gw0[:, h * w:(h + 1) * w], x, T.PM[:, 2:3], 2048.0, AL.mult, AL.min, ["LI%d" % h, "PM2"], ["Gw0_%d" % h])
+    send_g(0)
+    for c in range(3):
+        x = T.TR[:, c * V:(c + 1) * V]
+        ts(x, x, w15, None, AL.mult, None, ["TR", "PWa"], ["TR%d" % c])
+        ts(x, x, 32768, None, AL.bitwise_and, None, ["TR%d" % c], ["TR%d" % c])
+        ts(T.W0[:, LUTW + WN * c:LUTW + WN * c + V], x, 0.0, None, AL.is_gt, None, ["TR%d" % c], ["W0_%d_%d" % (h, c) for h in range(NCH)])
+    send_b(0)
+    cp(T.fanU[:], T.fanI[:], ["fanI"], ["fanU"])
+    cp(T.IDf[:], T.IDI[:], ["IDI"], ["IDf"])
+    io(T.IW[:], [[1, WN]], 0, 0, ["IW"])
+    fcp(T.Gc[:], T.IW[:].indirect(T.fanU[:]), ["IW", "fanU"], ["Gc"], GC)
+    cp(T.ps7[:], T.RQ[:], ["RQ"], ["ps7"])
+
+    for k, n in enumerate(PN):
+        for s, x, pat, base in _cover(PHI[n]): io(T.PH[:, k, s:s + x], pat, base, 0, ["PH%s_%d" % (n, s)])
+
+    def P_(n, a=0, b=16): return T.PH[:, PN.index(n), a:b], ["PH%s_%d" % (n, y[0]) for y in _cover(PHI[n])]
+
+    def mf(n, a=0, b=16, st=1): return T.MF[:, FN.index(n), a:b:st], "MF" + n
+
+    def mb(n, a=0, b=16, st=1): return T.MB[:, BN.index(n), a:b:st], "MB" + n
+
+    def tm(a, n): return T.TM[:, a:a + n], "TM%d" % a
+
+    def eqm(dst, phi, feat, x, tok=()): ts(dst[0], phi[0], feat, x, AL.is_equal, AL.mult, phi[1] + ["PF"] + list(tok), [dst[1]])
+
+    def col(dst, z, tok, sc=1.0): faff(dst[0], z, sc, 0.0, [tok], [dst[1]])
+
+    def ramp(dst, phi, feat, tmp, top):
+        ts(tmp[0], phi[0], feat, 1.0, AL.subtract, AL.add, phi[1] + ["PF"], [tmp[1]])
+        ts(tmp[0], tmp[0], -top / 2, 0.0, AL.mult, AL.min, [tmp[1]], [tmp[1]])
+        ts(dst[0], tmp[0], -top, None, AL.max, None, [tmp[1]], [dst[1]])
+    add({"v": (lambda: vec.memset(T.MF[:], 0.0), 0.3)}, [], ["MF" + n for n in FN])
+    add({"v": (lambda: vec.memset(T.MB[:], 0.0), 0.3)}, [], ["MB" + n for n in BN])
+    ms(T.BF[:, :, 128:144], 0.0, ["BFz"], 0.5); ms(T.BB[:, :, 128:144], 0.0, ["BBz"], 0.5)
+    for M, N, ns, ft in ((T.MF, FN, FM[0], p16), (T.MF, FN, FM[1][:3], p16), (T.MF, FN, FM[1][4:6], q2), (T.MF, FN, FM[2][:5], p16), (T.MB, BN, BM[0], p16)):
+        a0, b0 = N.index(ns[0]), PN.index(ns[0])
+        ts(M[:, a0:a0 + len(ns), :], T.PH[:, b0:b0 + len(ns), :], ft, None, AL.is_equal, None, sum([P_(n)[1] for n in ns], ["PF"]),
+           [("MF" if N is FN else "MB") + n for n in ns])
+    eqm(mf("XLn"), P_("XL"), p16, -1.0); eqm(mf("HA"), P_("HA"), p16, -1.0)
+    x = mf("XP", 0, 16, 2); ts(x[0], x[0], -1.0, None, AL.mult, None, [x[1]], [x[1]])
+    for n, pn, vn in [("VPa", "CK", "wV"), ("VPb", "CL", "wV"), ("PA3", "CK", "wP"), ("PB3", "CL", "wP")]: eqm(mf(n), P_(pn), kc, vc(vn), [V0])
+    eqm(mf("E12"), P_("COL"), p16, vc("is12"), [V1]); eqm(mf("UH", 8, 11), P_("COL", 0, 3), vc("zrow"), -1.0, [V1])
+    col(mf("UH", 11, 12), vc("u3"), V1); col(mf("UA", 11, 12), vc("ua"), V1)
+    eqm(mb("Zs", 8, 11), P_("COL", 0, 3), kc, -0.5); eqm(mb("Zs", 11, 14), P_("COL", 0, 3), lc, 0.5)
+    ramp(mb("Ze", 8, 11), P_("COL", 0, 3), kc, tm(0, 3), 1.0); ramp(mb("Ze", 11, 14), P_("COL", 0, 3), lc, tm(3, 3), 1.0)
+    eqm(mb("T1s", 0, 13), P_("COL", 0, 13), p16, -0.5); eqm(mb("T1s", 3, 12, 4), P_("COL", 0, 3), kc, 0.5)
+    eqm(mb("T1s", 13, 14), P_("RID", 0, 1), p16, 0.5); col(mb("T2s"), *mb("T1s"), -1.0)
+    ramp(tm(16, 12), P_("CL", 0, 12), lc, tm(16, 12), 1.0); eqm(tm(32, 12), P_("CK", 0, 12), kc, 1.0)
+    tt(mb("Te", 0, 12)[0], tm(16, 12)[0], tm(32, 12)[0], AL.mult, ["TM16", "TM32"], ["MBTe"])
+    eqm(mb("Te", 3, 12, 4), P_("COL", 0, 3), kc, -0.5); eqm(mb("Te", 12, 14), P_("RID", 0, 2), p16, -0.5)
+    eqm(mb("VT1"), P_("VT1"), kc, 1.0); eqm(mb("VT2"), P_("VT2"), kc, 1.0)
+    for n, a0, x in (("Zp1", 15, 1.0), ("Zm1", 15, -1.0), ("ONE", 0, 1.0)): ms(mb(n, a0)[0], x, ["MB" + n])
+    for n, c0, c1, lo, hi in [("A1", 14, 15, "valo", "vahi"), ("B1", 14, 15, "vblo", "vbhi"), ("A4", 2, 6, "valo", "vahi"), ("B4", 2, 6, "vblo", "vbhi")]:
+        col(mb(n, c0, c0 + 1), vc(lo), V0); col(mb(n, c1, c1 + 1), vc(hi), V0)
+    for n, pn, vn in [("T1a", "VT1", "w3"), ("T1b", "VT1", "wb"), ("T2a", "VT2", "wb"), ("T2b", "VT2", "w3")]: eqm(mb(n), P_(pn), kc, vc(vn), [V0])
+    col(mb("Zc1", 15), vc("nwc1"), V1); col(mb("Zc2", 15), T.PW2[:, 0:1], "PW2a", -1 / 16)
+    col(mb("Zlb", 15), T.PW2[:, 1:2], "PW2b"); col(mb("ZT", 15), w2m, "PWa")
+    eqm(mb("IV"), P_("COL"), p16, 16384.0); col(mb("BH"), T.VAL[:, 16 * NVT - 16:], "OP1")
+    eqm(mb("Hs", 0, 6), P_("HA", 0, 6), kc, -2048.0); eqm(mb("Hs", 6, 12), P_("HA", 0, 6), lc, 2048.0)
+    ramp(mb("He", 0, 6), P_("HA", 0, 6), kc, tm(48, 6), 4096.0); ramp(tm(54, 6), P_("HA", 0, 6), lc, tm(54, 6), 4096.0)
+    eqm(tm(60, 6), P_("HA", 0, 6), lc, 16384.0)
+    tt(mb("He", 6, 12)[0], tm(54, 6)[0], tm(60, 6)[0], AL.add, ["TM54", "TM60"], ["MBHe"])
+    eqm(mb("He", 12, 16), P_("COL", 0, 4), lc, 4096.0)
+    TK = {}
+    for tag, grp, M, B in (("F", FM, T.MF, T.BF), ("B", BM, T.MB, T.BB)):
+        o = 0
+        for gi, ns in enumerate(grp):
+            for q in range(8):
+                faff(B[:, o:o + len(ns), 16 * q:16 * q + 16], M[:, o:o + len(ns), :], T.GM[:, q:q + 1], 0.0, ["GM"] + ["M" + tag + n for n in ns],
+                     ["B%s%d_%d" % (tag, gi, q)], 1.0, 0.5)
+            TK[tag + str(gi)] = ["B%s%d_%d" % (tag, gi, q) for q in range(8)] + ["B%sz" % tag]
+            o += len(ns)
+
+    def LF(n, s=0): return T.BF[:, FN.index(n), s:s + 128]
+
+    def LB(n, s=0): return T.BB[:, BN.index(n), s:s + 128]
+    F0, F1, F2, B0, B1, B2 = [TK[x] for x in ("F0", "F1", "F2", "B0", "B1", "B2")]
+    io(T.D0[:], [[-1, 128]], 0, 1, ["D0"])
+    for u in range(4):
+        ts(T.SW[:, u * 128:(u + 1) * 128], T.D0[:], 16.0 * (u // 2 - u % 2), T.HC[:, u // 2:u // 2 + 1], AL.is_equal, AL.mult, ["D0", "HC"], ["SW%d" % u])
+    io(T.KI[0:2, :], [[0, 8], [-1, 16]], 0, 0, ["KI"])
+    ts(T.KC[0:2, :], T.KI[0:2, :], 1 / 16, None, AL.mult, None, ["KI"], ["KC"]); ms(T.KC[0:1, :], 524288.0, ["KC"])
+    ms(T.ON[:], 1.0, ["ON"], 0.5); ms(T.CB[:], 0.0, ["CB"])
+    io(T.BCI[:], [[1, 16]], 0, 0, ["BCI"], False); cp(T.BC[:], T.BCI[:], ["BCI"], ["BC"])
+    io(T.VNI[:], [[0, 3], [32, w // 32], [0, 2]], 0, 0, ["VNI"])
+    ts(T.VNN[:], T.VNI[:], c32, None, AL.add, None, ["VNI", "PF"], ["VNN"])
+    for h in range(NCH):
+        ms(T["AN%d" % h][:, 16 * w:], 1.0, ["ANp%d" % h])
+        faff(T["AB%d" % h][:, 4 * w:], T.GI[:], 0.0, vc("padAB"), ["GI", V1], ["ABp%d" % h])
+
+    io(T.BYI[:], [[1, 256]], 0, 0, ["BYI"], False)
+    ts(T.BYI[:], T.BYI[:], w15, None, AL.mult, None, ["BYI", "PWa"], ["BYI"])
+    ts(T.BYI[:], T.BYI[:], 32768, None, AL.bitwise_and, None, ["BYI"], ["BYI"])
+    ts(T.BYB[:], T.BYI[:], 0.0, None, AL.is_gt, None, ["BYI"], ["BYB"])
+    for q in range(4):
+        pb = "ps%d" % (3 + q)
+        for u in range(2): mm(T[pb][:, 256 * u:256 * u + 256], [(LB("LUT%d" % (2 * q + u)), T.BYB[:])], B0 + ["BYB"], [pb])
+        fcp(T.W0[:, 512 * q:512 * q + 512], T[pb][:], [pb], ["LUT%d" % q])
+    io(T.NI[:], [[0, 2], [256, 8], [0, 16]], 0, 0, ["NI"], False)
+    ts(T.TM[:, 80:81], p16, 17.0, None, AL.mult, None, ["PF"], ["TM80"]); ts(T.TM[:, 81:82], lc, 85.0, None, AL.mult, None, ["PF"], ["TM81"])
+    for u in range(2):
+        ts(T.NL[:, 128 * u:128 * u + 128], T.NI[:, 128 * u:128 * u + 128], T.TM[:, 80 + u:81 + u], None, AL.add, None, ["NI", "TM%d" % (80 + u)], ["NL%d" % u])
+        for x in range(2):
+            fcp(T.W0[:, 2048 * (u + 1) + 1024 * x:2048 * (u + 1) + 1024 * (x + 1)], T.W0[:, 0:2048].indirect(T.NL[:, 128 * u + 64 * x:128 * u + 64 * (x + 1)]),
+                ["NL%d" % u] + ["LUT%d" % q for q in range(4)], ["LUT%d" % (4 + 2 * u + x)], GC)
+    LUT0 = ["LUT%d" % q for q in range(8)]
+    dma("s", [(T.W1[:, 0:LUTW], T.W0[:, 0:LUTW])], LUT0, ["LUTc"], 10.0)
+
+    FULL = [0, 1, 4, 5, 8, 9, 2, 6, 10]
+    rot = {}
+    BAS, BC_, BE = ((1, 2, 3, 4, 5, 6, 0), (1, 2, 0, 5, 6)), (3, 4), (5, 6, 0, 1, 2)
+
+    def bank(lst):
+        rot[lst] = rot.get(lst, -1) + 1
+        return "ps%d" % lst[rot[lst] % len(lst)]
+
+    def blk(buf, x, n=1): return buf[:, x * w:(x + n) * w]
+
+    def tk(n, xs): return ["%s_%d" % (n, x) for x in xs]
+
+    def stage_a(r, h):
+        Gw, v0, SG, NE, RR, BA = T["Gw%d" % r], h * w, T.SG, T.NE, T.RR, BAS[h]
+        Ga, Gn, Gb, Pa, Pb = [blk(T["GG%d" % h], x) for x in range(5)]
+        ga, gn, gb, pa, pb_ = ["G%d_%d" % (x, h) for x in range(5)]
+        gw = ["Gw%d_%d" % (r, x) for x in range(NCH)] + ["Gw%dr" % r, "fanU"]
+        fcp(Ga, Gw[:].indirect(T.fanU[:, v0 // 16:(v0 + w) // 16]), gw, [ga], GC)
+        faff(Gb, Gw[:].indirect(T.fanU[:, (V + v0) // 16:(V + v0 + w) // 16]), -1.0, 0.0, gw, [gb], GC)
+        ts(Pb, Gb, -2048.0, 2048.0, AL.is_le, AL.mult, [gb], [pb_], 0.5)
+        tt(Gn, Gb, Pb, AL.subtract, [gb, pb_], [gn])
+        ts(Pa, Ga, 2048.0, 2048.0, AL.is_ge, AL.mult, [ga], [pa], 0.5)
+        for b0 in range(0, 11, 2):
+            bs, pb = list(range(b0, min(11, b0 + 2))), bank(BA)
+            for u, bl in enumerate(bs):
+                l = ("SA%d" % (FULL[bl] >> 2), "SB%d" % (FULL[bl] & 3)) if bl < 9 else (("COL", "RID") if bl == 9 else ("RID", "COL"))
+                mm(blk(T[pb], u), [(LF(l[0]), Ga), (LF(l[1]), Gn)], F0 + [ga, gn], [pb])
+            fsign(blk(SG, b0, len(bs)), blk(T[pb], 0, len(bs)), [pb], tk("SG", bs))
+            fne(blk(NE, b0, len(bs)), blk(SG, b0, len(bs)), tk("SG", bs), tk("NE", bs))
+        pb = bank(BA)
+        mm(blk(T[pb], 0), [(LF("XC", 2), T.Gc[:, v0:v0 + w]), (LF("XC"), T.Gc[:, V + v0:V + v0 + w]), (LF("XL", 2), Ga), (LF("XLn"), Gn),
+                           (LF("XP", 2), Pa), (LF("XP"), Pb)], F1 + ["Gc", ga, gn, pa, pb_], [pb])
+        frelu(T.XX[:], blk(T[pb], 0), vc("bX"), [pb, V0], ["XX"])
+        src = [[0, 1], [2, 3], [4, 5], [6, 7], [8], [9], [10]]
+        for grp, bi in [([0, 1], vc("bR")), ([2, 3], vc("bR")), ([4], T.PM[:, 3:4]), ([5, 6], 3.0)]:
+            pb = bank(BA)
+            for u, t in enumerate(grp):
+                pr = []
+                for n, x in enumerate(src[t]):
+                    l = (LB("Zs", 8 - 8 * n), LB("Ze", 8 - 8 * n)) if x < 9 else (LB("T%ds" % (x - 8)), LB("Te"))
+                    pr += [(l[0], blk(SG, x)), (l[1], blk(NE, x))]
+                mm(blk(T[pb], u), pr, B1 + tk("SG", src[t]) + tk("NE", src[t]), [pb])
+            frelu(blk(RR, grp[0], len(grp)), blk(T[pb], 0, len(grp)), bi, [pb, V0, "PM3"], tk("RR", grp))
+        for u, (x, P) in enumerate((("a", Pa), ("b", Pb))):
+            m1, pb = x.upper() + "1", bank(BA)
+            l = [LB(m1, 14), LB(m1, 10), LB(m1, 6), LB(x.upper() + "4"), LB(m1, 4), LB("T1" + x), LB("T2" + x)]
+            mms(blk(T[pb], 0), [([(LF("X" + x.upper()), T.XX[:]), (LF("P%s3" % x.upper()), P)] * (k == 0) + [(l[t], blk(RR, t)) for t in grp],
+                                 B1 + F1 + tk("RR", grp) + ["XX", pa, pb_]) for k, grp in enumerate((range(4), range(4, 7)))], [pb])
+            ts(blk(T["IX%d" % h], u), blk(T[pb], 0), vc("bI" + x), float(WW - 1), AL.add, AL.min, [pb, V0], ["IX%d_%d" % (h, u)])
+        pb = bank(BA)
+        mm(blk(T[pb], 0), [(LF("VPa"), Pa), (LF("VPb"), Pb)] + [(LB("Zp1", 15 - FULL[x]), blk(NE, x)) for x in range(9)] +
+           [(LB("VT1"), blk(NE, 9)), (LB("VT2"), blk(NE, 10))], B1 + F1 + tk("NE", range(11)) + [pa, pb_], [pb])
+        frelu(T["VD%d" % h][:], blk(T[pb], 0), vc("bVoid"), [pb, V0], ["VD%d" % h])
+        AB = T["AB%d" % h]
+        for i0 in (0, 2):
+            pb = bank(BA)
+            for u in range(2): mm(blk(T[pb], u), [(LF("SEL%d" % (i0 + u), 4), Ga), (LF("SEL%d" % (i0 + u)), Gn)], F2 + [ga, gn], [pb])
+            fcp(blk(AB, i0, 2 - i0 // 2), blk(T[pb], 0, 2 - i0 // 2), [pb], ["AB%d_%d" % (h, i0)])
+        faff(blk(AB, 3), blk(T[pb], 1), 1.0, vc("bAB3"), [pb, V1], ["AB%d_3" % h])
+
+    def stage_b(r, h):
+        Wt, IX, AN = T["W%d" % r], T["IX%d" % h], T["AN%d" % h]
+        wt = ["W%d_%d_%d" % (r, x, c) for x in range(NCH) for c in range(3)] + ["W%dr" % r] + (LUT0 if r == 0 else ["LUTc"])
+        for u in range(w // GW):
+            s = slice(16 * GW * u, 16 * GW * (u + 1))
+            ac(T.AG[:, s], Wt[:].indirect(IX[:, GW * u:GW * (u + 1)]), wt + ["IX%d_0" % h], ["AG_%d" % u])
+            tt(AN[:, s], Wt[:].indirect(IX[:, w + GW * u:w + GW * (u + 1)]), T.AG[:, s], AL.mult, wt + ["IX%d_1" % h, "AG_%d" % u], ["AN%d_%d" % (h, u)], GC)
+        for c0 in range(0, w, WB):
+            for u, (zm, bi) in enumerate((("Zc2", 4095.0), ("Zc1", sum(WC1) + 4096.0))):
+                pb = bank(BC_)
+                mm(T[pb][:, 0:WB], [(LB("IV"), T["VD%d" % h][:, c0:c0 + WB])] + [(LB(zm, 15 - q), AN[:, 16 * c0 + q:16 * (c0 + WB):16]) for q in range(16)],
+                   B2 + tk("AN%d" % h, range(c0 // GW, (c0 + WB) // GW)) + ["VD%d" % h], [pb])
+                ts(IX[:, (2 + u) * w + c0:(2 + u) * w + c0 + WB], T[pb][:, 0:WB], bi, float(VOID), AL.add, AL.min, [pb], ["CX%d_%d_%d" % (h, u, c0 // WB)])
+
+    def stage_c(r, h):
+        IX, v0, XM, xm = T["IX%d" % h], h * w, T.XM, tk("XM", range(16))
+        for u in range(w // GW):
+            s = slice(16 * GW * u, 16 * GW * (u + 1))
+            ac(T.CG[:, s], T.CE[:].indirect(IX[:, 2 * w + GW * u:2 * w + GW * (u + 1)]), ["CEa", "CEb", "CX%d_0_%d" % (h, u * GW // WB)], ["CG_%d" % u])
+            tt(XM[:, s], T.CE[:].indirect(IX[:, 3 * w + GW * u:3 * w + GW * (u + 1)]), T.CG[:, s], AL.min,
+               ["CEa", "CEb", "CX%d_1_%d" % (h, u * GW // WB), "CG_%d" % u] + xm, ["XG_%d" % u], GC)
+        for q in range(16): tt(XM[:, q::16], XM[:, q::16], T.ps7[:, v0:v0 + w], AL.max, ["ps7"] + tk("XG", range(w // GW)), [xm[q]], 1.0)
+        pb = bank(BC_)
+        mms(blk(T[pb], 0), [([(T.KC[0:2, :], T.ON[0:2, 0:w]), (LB("ONE"), T.RQ[:, v0:v0 + w])] * (q0 == 0) +
+            [(LB("Zm1", 15 - q), XM[:, q::16]) for q in range(q0, q0 + QS)],
+            B2 + ["KC", "ON", "RQ"] + xm[q0:q0 + QS] + tk("XG", range(w // GW))) for q0 in range(0, 16, QS)], [pb])
+        tr(blk(T.NK, 0), blk(T[pb], 0), [pb], ["NK_0"])
+
+    def stage_d(r, h):
+        NK, SC, TT, KP, LV, LU, QI, n3 = T.NK, T.SC, T.TT, T.KP[:], T.LV, T.LU, T.QI[:], 3 * NS
+        nk, sc, tn = [tk(n, range(3)) for n in ("NK", "SC", "TT")]
+        for c in range(3):
+            scan(blk(SC, c), T.RST[:, 0:w], blk(NK, c), 0.0, AL.mult, AL.max, ["RST", nk[c]], [sc[c]])
+            ts(TT[:, c * NS:(c + 1) * NS], SC[:, c * w + 15:(c + 1) * w:16], -0.53125, None, AL.add, None, [sc[c]], [tn[c]])
+            if c < 2:
+                tt(KP, TT[:, c * NS:(c + 1) * NS].indirect(T.BC[:, 0:NS]), blk(NK, c), AL.is_ge, [tn[c], "BC", nk[c]], ["KP"], GC)
+                tt(blk(NK, c + 1), KP, blk(NK, c), AL.mult, ["KP", nk[c]], [nk[c + 1]])
+        M, Q, q, lv = SC[:, 15::16], [T.Q[:, n * n3:(n + 1) * n3] for n in range(7)], tk("Q", range(8)), tk("LV", range(3))
+        tt(Q[0], TT[:], M, AL.subtract, sc + tn, [q[0]])
+        ts(Q[1], M, 0.0, 8192.0, AL.is_le, AL.mult, sc, [q[1]])
+        ts(QI, Q[0], 4.0, 3.625, AL.mult, AL.add, [q[0]], [q[7]])
+        tt(Q[2], Q[1], T.VNN[:], AL.add, [q[1], "VNN"], [q[2]])
+        ts(Q[3], Q[0], 16.0 * w, 16.0 * w, AL.mult, AL.add, [q[0]], [q[3]])
+        tt(Q[4], Q[0], Q[2], AL.add, [q[0], q[2]], [q[4]])
+        ts(Q[5], QI, float(w), None, AL.mult, None, [q[7]], [q[5]])
+        ts(Q[6], QI, -4.0 * w, None, AL.mult, None, [q[7]], [q[6]])
+        tt(Q[3], Q[3], Q[2], AL.add, [q[3], q[2]], [q[3]])
+        ts(LV[:, 2 * n3:], Q[4], 16.0, 16.0, AL.mult, AL.add, [q[4]], [lv[2]])
+        tt(LV[:, 0:n3], Q[5], Q[2], AL.add, [q[5], q[2]], [lv[0]])
+        tt(LV[:, n3:2 * n3], Q[6], Q[3], AL.add, [q[6], q[3]], [lv[1]])
+        pb = bank(BE)
+        for h1 in range(2):
+            mm(T[pb][:, h1:3 * n3:2], [(T.SW[:, (2 * h1 + x) * 128:(2 * h1 + x + 1) * 128], LV[:, x::2]) for x in range(2)],
+               lv + ["SW%d" % x for x in range(4)], [pb], 4)
+        ts(LU[:, 0:2 * n3], T[pb][:, 0:2 * n3], 4.0 * w, None, AL.min, None, [pb], ["LU"])
+        ts(LU[:, 2 * n3:], T[pb][:, 2 * n3:3 * n3], 16.0 * w, None, AL.min, None, [pb], ["LW"])
+        if r == 1:
+            ts(Q[5], TT[:], -1.0, 524287.0, AL.mult, AL.add, tn, [q[5]])
+            ts(Q[6], M, 0.0, -524289.0, AL.is_le, AL.mult, sc, [q[6]])
+            for c in range(3):
+                a0 = c * NS
+                tt(T.CB[:, c::16], T.Q[:, 5 * n3 + a0:5 * n3 + a0 + NS], T.Q[:, 6 * n3 + a0:6 * n3 + a0 + NS], AL.add, [q[5], q[6]], ["CB"])
+            tr(blk(T.YC, h), T.CB[:], ["CB"], ["YC%d" % h])
+
+    def stage_e(r, h):
+        v0, AB, Wn, LU, CA, CN, S2, E2, HH = h * w, T["AB%d" % h], (T.WF if r else T.W1), T.LU, T.CA, T.CN, T.S2, T.E2, T.HH
+        n3, (w0, w1) = 3 * NS, ((0, V) if r else (LUTW, WN))
+        ab = tk("AB%d" % h, (0, 2, 3)) + ["ABp%d" % h, "LU"]
+        fcp(CA[:], AB[:].indirect(LU[:, 0:n3]), ab, ["CA"], GC)
+        fcp(CN[:], AB[:].indirect(LU[:, n3:2 * n3]), ab, ["CN"], GC)
+        wn = ["W%d_%d_%d" % (1 + r, h, c) for c in range(3)]
+        for c in range(3):
+            o = w0 + w1 * c + v0
+            faff(Wn[:, o:o + w], T["AN%d" % h][:].indirect(LU[:, 2 * n3 + c * NS:2 * n3 + (c + 1) * NS]), -1.0, 1.0,
+                 tk("AN%d" % h, range(w // GW)) + ["ANp%d" % h, "LW"], [wn[c]], GC)
+        if r == 0 and h == 0: send_b(1)
+        for a0, n in ((0, 512), (512, 256)):
+            s, y, pb = slice(a0, a0 + n), str(a0), bank(BE)
+            mm(T[pb][:, 0:n], [(LF("SA0"), CA[:, s]), (LF("SB1"), CN[:, s])], F0 + ["CA", "CN"], [pb])
+            fsign(S2[:, s], T[pb][:, 0:n], [pb], ["S2" + y]); fne(E2[:, s], S2[:, s], ["S2" + y], ["E2" + y])
+            pb = bank(BE)
+            mms(T[pb][:, 0:n], [([(LB("BH"), T.ON[:, 0:n]), (LF("HA"), CA[:, s]), (LF("HB"), CN[:, s])], F2 + B2 + ["ON", "CA", "CN"]),
+                                ([(LB("Hs"), S2[:, s])], ["S2" + y]), ([(LB("He"), E2[:, s])], ["E2" + y])], [pb])
+            ts(HH[:, s], T[pb][:, 0:n], 0.0, 4096.0, AL.max, AL.min, [pb], ["HH" + y])
+        pb, pr = bank(BE), [(LF("E12"), T.IDf[:, v0:v0 + w])]
+        for c in range(3):
+            o = w0 + w1 * c + v0
+            pr += [(LB("ZT" if r else "Zlb", 2 - c), Wn[:, o:o + w]), (LF("UA", 8 - 4 * c), blk(CA, c))]
+        mms(blk(T[pb], 0), [(pr, F2 + B2 + ["IDf", "CA"] + wn), ([(LF("UH", 8 - 4 * c), blk(HH, c)) for c in range(3)], ["HH0", "HH512"])], [pb])
+        if r == 0:
+            faff(blk(T.Gw1, h), blk(T[pb], 0), 1.0, vc("bU"), [pb, V1], ["Gw1_%d" % h])
+            if h == 0: send_g(1)
+        else:
+            Y = blk(T.Y, h)
+            faff(Y, blk(T[pb], 0), 1.0, vc("bU"), [pb, V1], ["Y%d" % h])
+            ts(T.YP[:], Y, vc("thr"), -2049.0, AL.is_ge, AL.mult, ["Y%d" % h, V1], ["YP"])
+            tt(Y, Y, T.YP[:], AL.add, ["Y%d" % h, "YP"], ["Y%d" % h])
+    for r in range(2):
+        for s in range(NCH + 3):
+            for k, sts in ((3, (stage_d, stage_e)), (2, (stage_c,)), (1, (stage_b,)), (0, (stage_a,))):
+                if 0 <= s - k < NCH:
+                    for st in sts: st(r, s - k)
+    ys = ["Y%d" % h for h in range(NCH)]
+    dma("s", [(T.yc[:, c * V:(c + 1) * V], T.YC[c::16, :]) for c in range(3)], ["YC%d" % h for h in range(NCH)], [])
+    dma("s", [(T.yl[:, f * V:(f + 1) * V], T.Y[f::16, :]) for f in range(8)], ys, [])
+    dma("a", [(T.yl[:, f * V:(f + 1) * V], T.Y[f::16, :]) for f in range(8, 12)] +
+        [(T.yt[:, c * V:(c + 1) * V], T.Y[13 + c::16, :]) for c in range(3)], ys, [])
+
+    n = len(ops)
+    succ, pl, rdy = [[] for _ in range(n)], [0.0] * n, [0.0] * n
+    for i, o in enumerate(ops):
+        o["dd"] = set(o["d"]) | ({o["o"]} if "o" in o else set())
+        for d in o["dd"]: succ[d].append(i)
+    for i in range(n - 1, -1, -1):
+        pl[i] = max(c for f, c in ops[i]["a"].values()) + ops[i]["l"] + 0.06 + max([pl[j] for j in succ[i]], default=0.0)
+    for i in range(n): pl[i] += 20.0 * (ops[i]["k"] in ("VAL", "TWO"))
+    left, free, order = [len(o["dd"]) for o in ops], {e: 0.0 for e in "atgsxv"}, []
+    pool = {i for i in range(n) if left[i] == 0}
+    while pool:
+        best = None
+        for i in pool:
+            al = ops[i]["a"]
+            e = min(al, key=lambda e: max(free[e], rdy[i]) + al[e][1] + (MARG if e == "v" else 0.0))
+            key = (round(max(free[e], rdy[i]), 6), -pl[i], i, e)
+            if best is None or key < best: best = key
+        t0, i, e = best[0], best[2], best[3]
+        soon = [j for j in pool if ops[j]["e"] == e and rdy[j] < t0 + 0.5 * ops[i]["a"][e][1] and pl[j] > pl[i] + 1.0]
+        if soon:
+            i = max(soon, key=lambda j: (pl[j], j)); t0 = max(free[e], rdy[i])
+        pool.remove(i); order.append(i)
+        ops[i].update({"e": e, "t": t0, "c": ops[i]["a"][e][1]})
+        free[e] = t0 + ops[i]["c"]
+        for j in succ[i]:
+            rdy[j] = max(rdy[j], free[e] + ops[i]["l"] + 0.06); left[j] -= 1
+            if left[j] == 0: pool.add(j)
+    EST[:] = [free, ops, order]
+    qs = {"v": vec, "a": act, "t": ten, "g": g, "s": g.sync}
+    cnt, seen, final = {"v": 0, "a": 0, "t": 0, "g": 0}, {}, {}
+    for i in order:
+        o = ops[i]
+        e = o["e"]
+        if o["s"] is None:
+            cnt[e] += 1; o["w"] = ("s" + e, cnt[e])
+        else:
+            o["w"] = (o["s"], o["n"])
+        if o["s"] != "loc": final[o["w"][0]] = o["w"][1]
+        if e == "x": continue
+        need = {}
+        for d in o["d"]:
+            if e == "t" and ops[d]["e"] == "t": continue
+            s, c = ops[d]["w"]
+            need[s] = max(need.get(s, 0), c)
+        for s, c in need.items():
+            if seen.get((e, s), 0) < c:
+                qs[e].wait_ge(T.sem[s], c); seen[(e, s)] = c
+        x = o["a"][e][0]()
+        if o["s"] is None: x.then_inc(T.sem[o["w"][0]], 1)
+    final["loc"] = locn[0]
+    for s, c in final.items(): g.wait_ge(T.sem[s], c)

@@ -3,15 +3,21 @@ from concourse.bass import DstId, RemoteDMATransfer
 from concourse.mybir import AluOpType as AL, ActivationFunctionType as AF
 
 V, NR, BORD, WN = 512, 4, 256, 1280
-w, WB, GW, QS = 256, 128, 64, 4
-NCH, NS = V // w, w // 16
-LUTW, VOID = 6144, 9008
+CH = [[128] * 4, [128] * 4]
+GW, QS = 64, 4
+LUTW = 14 * 256
 WW = LUTW + 3 * WN
+CEW, CE0 = 7792, 2880
+MG, DL = 12582912.0, 1 / 128
 N_ = None
 P16 = list(range(16))
 KK = [p >> 2 for p in P16]
 LL = [p & 3 for p in P16]
-MARG, OVH, PEC, GC = 0.2, 0.06, 0.5e-3, 1.56
+SI = [0, 0, 3, 0, 1, 1, 3, 1, 2, 2, 3, 2, 0, 1, 2, 3]
+SJ = [0, 1, 0, 3, 0, 1, 1, 3, 0, 1, 2, 3, 2, 2, 2, 3]
+FULL = [q for q in P16 if SI[q] < 3 and SJ[q] < 3]
+PLACINGS = [7, 11, 13, 3, 14, 5, 6, 9, 10, 12, 1, 2, 4, 8]
+MARG, OVH, PEC, GC, HOP, AHEAD, SOON = 20.0, 0.06, 0.43e-3, 1.4, 0.08, 0.02, 0.3
 
 
 def _old(s):
@@ -25,133 +31,127 @@ def _old(s):
 
 WC1 = [((1 << m) + (29 * (1 << (m - 5)) if m >= 5 else 0)) % 4096 for m in P16]
 WC1 = [x - 4096 * (x > 2048) for x in WC1]
-HZ, HK, W3 = [0, 1, 1, 2, 2, 2], [0, 0, 1, 0, 1, 2], [256, 512, -256]
-_bh = [128 + 768 * HK[c] + 256 * HZ[c] for c in range(6)]
-VEC = [{
-    "bR": [3, 6, 9, 3, 6, 9, 0, 0] * 2, "bVoid": [[-12, -3, -6][(KK[p] == 3) + (LL[p] == 3)] for p in P16], "bX": [0, -2048] * 8,
-    "bIa": [256 * (18 + 5 * KK[p]) if KK[p] < 3 else 170 for p in P16],
-    "bIb": [256 * (18 + 5 * LL[p]) if LL[p] < 3 else 170 for p in P16],
-    "wV": [7 / 2048, -1 / 2048, -1 / 2048, -1 / 2048] * 4, "wP": [[0, 1, 1, -(18 + 5 * KK[p]) / 8][LL[p]] for p in P16],
-    "valo": W3 + [0] * 13, "vahi": [0] * 8 + W3 + [0] * 5, "vblo": [0] * 3 + W3 + [0] * 10, "vbhi": [0] * 11 + W3 + [0] * 2,
-    "w3": (W3 + [0]) * 3 + [256, 0, 0, 0], "wb": [0, 0, 0, 256] * 3 + [0, 256, 0, 0],
-}, {
-    "is12": [0] * 12 + [1, 0, 0, 0], "nwc1": [-x for x in WC1], "zrow": HZ * 2 + [9] * 4, "u3": [1] * 12 + [-1] * 4,
-    "ua": [1] * 4 + [0] * 12, "bU": [2048, 6144, 10240, -18432] * 3 + [0] * 4, "padAB": [2048] * 4 + [-4096] * 4 + [0] * 8,
-    "bAB3": [0, 2048, 2048, 2048, 0, -4096, -4096, -4096] + [0] * 8, "thr": [2048] * 13 + [131072] * 3,
-    "bH": _bh + [x - 4096 for x in _bh] + [-896] * 4,
-}]
-VN = list(VEC[0]) + list(VEC[1])
-NV0, NVT = len(VEC[0]), len(VN)
+HZ, HK = [0, 1, 1, 2, 2, 2], [0, 0, 1, 0, 1, 2]
+A1, A2, N1, N2 = [.5, 1, 0, 0], [.5, -.5, .5, 0], [2.5, 1, 0, 0], [.5, .5, .5, 0]
+TRIV = 10 + 1 / 128
+V8 = {"A1": A1 * 2, "A2": A2 * 2, "N1": N1 * 2, "N2": N2 * 2,
+      "cA0": [-24, 19, -3, 14, TRIV, 0, 0, 0], "cA1": [-18, 19, -3, 14, -16, 0, 0, 0], "cBf": [6, -26, 16, 0, 0, 0, 0, 0],
+      "cBt": [9, -26, 16, 0, TRIV, 0, 0, 0], "cV": [-7, 1, 1, 1, 5, 0, 0, 0], "bU": [0, -4096, -8192, 12288, 0, 0, 0, 0]}
+V16 = {"zrow": HZ * 2 + [9] * 4, "nwc1": [-x for x in WC1]}
+V2_ = {"mul": (13, -1, 16), "off": (13, -1, 0), "sub": (13, 2047, 0), "dcol": (12, DL, 0), "bRa": (13, -4096, DL - 4096),
+       "bRb": (13, -4096, 2), "u3": (12, -1, 1), "sY": (13, -1, 1), "thr": (13, 2047.5, 70000), "tY": (13, 2048, 0)}
+CN = list(V2_) + ["f12", "f13", "c8", "t5", "cAf", "cAt", "bX", "lo2", "hi2", "bY", "le12", "le12n", "is13", "is14", "is0", "is1", "bM",
+                  "p256", "w2hi", "w2lo", "nA1", "nA2"]
+_hc = [2048 * (HZ[c] - HK[c]) + 8192 * HK[c] for c in range(6)]
 PHI = {}
 for _i in range(6):
     PHI["S" + "AB"[_i // 3] + str(_i % 3)] = [4 * (_i % 3) + x for x in (KK, LL)[_i // 3]]
-PHI.update({"COL": P16, "RID": [12] * 16, "XC": [N_, N_, 12, N_] * 3 + [N_] * 4,
-            "XL": [N_, N_, N_, 13, N_, N_, N_, 14, N_, N_, N_, 15] + [N_] * 4,
-            "XP": [N_, N_, 3, 3, N_, N_, 7, 7, N_, N_, 11, 11] + [N_] * 4, "XA": [2 * x for x in KK], "XB": [2 * x + 1 for x in LL]})
-for _i in range(4):
-    PHI["SEL%d" % _i] = [N_] * 4 + ([4 * _i + x for x in range(4)] if _i < 3 else [12, N_, N_, N_]) + [N_] * 8
-PHI.update({"HB": [N_] * 6 + [4 + x for x in HK] + [4, 5, 6, 7], "HA": HK + [N_] * 10, "CK": KK, "CL": LL,
-            "VT1": [N_, N_, N_, 0, N_, N_, N_, 1, N_, N_, N_, 2, N_, N_, N_, 3], "VT2": [N_] * 12 + [0, 1, 2, N_]})
-for _i, _m in enumerate([8, 12, 10, 9, 14, 13, 7, 11]):
+PHI.update({"COL": P16, "RID": [12] * 16})
+for _i, _m in enumerate(PLACINGS):
     PHI["LUT%d" % _i] = _old(_m)
+PHI.update({"CK": KK, "CL": LL, "HK": HK + [N_] * 10, "HC": _hc + [x - 24576 for x in _hc] + [-8192] * 4})
 PN = list(PHI)
-FM = [["SA0", "SA1", "SA2", "SB0", "SB1", "SB2", "COL", "RID"], ["XC", "XL", "XP", "XLn", "XA", "XB", "VPa", "VPb", "PA3", "PB3"],
-      ["SEL0", "SEL1", "SEL2", "SEL3", "HB", "HA", "UH", "UA", "E12"]]
-BM = [["LUT%d" % i for i in range(8)], ["Zs", "Ze", "T1s", "T2s", "Te", "VT1", "VT2", "Zp1", "A1", "B1", "A4", "B4", "T1a", "T1b", "T2a", "T2b"],
-      ["Zc1", "Zc2", "IV", "Zm1", "ONE", "Hs", "He", "BH", "Zlb", "ZT"]]
+FM = [["SA0", "SA1", "SA2", "SB0", "SB1", "SB2", "I13", "R13", "I12", "R12"], ["XC", "XL", "XP", "XA", "XB", "I256"],
+      ["J13", "RMa", "RMb", "EA", "EB", "HA", "HB", "Hs", "He", "UH", "UA", "UE", "E12", "LP"]]
+BM = [["LUT%d" % i for i in range(14)], ["Zc1", "Zc2", "IV", "ONE", "KC", "Zlb", "ZT"]]
 FN, BN = sum(FM, []), sum(BM, [])
 f32, f16, b16, i32, u16 = "float32", "float16", "bfloat16", "int32", "uint16"
-_S = [("fanI", 64, i32), ("fanU", 64, u16), ("LI", V, i32), ("IDI", V, i32), ("TR", 3 * V, i32), ("CE", VOID + 16, b16), ("RQ", V, b16),
-      ("Gw0", WN, f32), ("Gw1", WN, f32), ("W0", WW, b16), ("W1", WW, b16), ("WF", 3 * V, b16), ("IW", WN, f32), ("Gc", 2 * V, f16),
-      ("IDf", V, f16), ("PI", 8, i32), ("PJ", 8, i32), ("PF", 8, f32), ("GI", 8, f32), ("GM", 8, f32), ("HC", 2, f32), ("PM", 4, f32),
-      ("VAL", 16 * NVT, f32), ("OHI", 16 * NVT, f32), ("OH", 16 * NVT, f32), ("VC", 16 * NVT, f32), ("RST", 256, f32),
-      ("POWR", 48, f32), ("POWC", 32, f32), ("TWO", 32, f32), ("PW2", 4, f32), ("TM", 96, f32),
-      ("D0", 128, f32), ("SW", 512, f32), ("KC", 128, b16), ("KI", 128, f32), ("ON", 512, b16), ("BYI", 256, i32), ("BYB", 256, b16),
-      ("NI", 256, i32), ("NL", 256, u16), ("BCI", 16, i32), ("BC", 16, u16), ("VNI", 3 * NS, f32), ("VNN", 3 * NS, f32),
-      ("Y", V, f32), ("YP", w, f32), ("YC", V, f32), ("CB", w, f32),
-      ("SG", 11 * w, b16), ("NE", 11 * w, b16), ("RR", 7 * w, b16), ("XX", w, f16), ("AG", 16 * w, b16), ("CG", 16 * w, b16),
-      ("XM", 16 * w, b16), ("NK", 3 * w, f32), ("KP", w, f32), ("SC", 3 * w, f32), ("CA", 3 * w, f16), ("CN", 3 * w, f16),
-      ("S2", 3 * w, b16), ("E2", 3 * w, b16), ("HH", 3 * w, f16), ("TT", 3 * NS, i32), ("Q", 21 * NS, f32), ("QI", 3 * NS, i32),
-      ("LV", 9 * NS, f32), ("LU", 9 * NS, u16)]
-for _h in range(NCH):
-    _S += [("GG%d" % _h, 5 * w, f16), ("VD%d" % _h, w, b16), ("IX%d" % _h, 4 * w, u16), ("AN%d" % _h, 16 * w + 16, b16), ("AB%d" % _h, 4 * w + 8, f32)]
+_S = [("fanI", 64, i32), ("fanU", 64, u16), ("LI", V, i32), ("IDI", V, i32), ("TR", 3 * V, i32), ("CE", CEW, b16), ("RQ", V, b16),
+      ("Gw0", WN, f32), ("Gw1", WN, f32), ("W0", WW, b16), ("W1", WW, b16), ("IW", WN, f32), ("Gc", 2 * V, f16),
+      ("IDf", V, f16), ("PI", 8, i32), ("PJ", 8, i32), ("PF", 8, f32), ("GI", 32, f32), ("GM", 8, f32), ("GN", 8, b16), ("CO", len(CN), f32),
+      ("VAL", 112, f32), ("OHI", 80, f32), ("OH", 176, f32), ("PR", 176, f32), ("VC", 176, f32), ("RST", 256, f32), ("RS8", 112, f32),
+      ("POWR", 48, f32), ("POWC", 32, f32), ("TWO", 32, f32), ("TM", 128, f32), ("ONF", 128, f32), ("IDN", 128, f32),
+      ("ON", 128, b16), ("ONH", 128, f16), ("BYI", 256, i32), ("BYB", 256, b16), ("BCI", 16, i32), ("BC", 16, u16), ("CV", 96, f16),
+      ("PIW", 128, f32), ("PJW", 128, f32), ("PA", 512, f16), ("PB", 256, f16), ("PAV", 128, f16), ("PBV", 128, f16),
+      ("W2", 72, f16), ("W9", 224, f16),
+      ("GG", 2 * V, f16), ("PP", 2 * V, f16), ("SG", 11 * V, f16), ("NE", 11 * V, f16), ("XX", V, f16), ("XT", 4 * V, f16), ("VT", V, b16),
+      ("IX", 2 * V, u16), ("CX", 2 * V, u16), ("AG", 16 * V, b16), ("AN", 16 * V, b16), ("XG", 16 * V, b16),
+      ("NK0", V, f32), ("NK1", V, f32), ("NKN", 2 * V, f32), ("KP", 2 * V, f32), ("SC", 3 * V, f32), ("MT", 3 * V, f16), ("MK", 3 * V, f16),
+      ("LU", 3 * V // 16, u16), ("RA", 3 * V, f16), ("RB", 3 * V, f16), ("S2", 3 * V, f16), ("E2", 3 * V, f16), ("HH", 3 * V, f16),
+      ("Y", V, f32), ("YP", V, f32), ("TT", 96, i32), ("Q5", 96, f32), ("Q6", 96, f32), ("YC", V, f32)]
 SCRATCH = {n: ("sbuf", [128, k], d) for n, k, d in _S}
-SCRATCH.update({"PH": ("sbuf", [128, len(PN), 16], f32), "MF": ("sbuf", [128, len(FN), 16], f16), "MB": ("sbuf", [128, len(BN), 16], b16),
+SCRATCH.update({"TR": ("sbuf", [128, 3, V], i32), "PH": ("sbuf", [128, len(PN), 16], f32), "MF": ("sbuf", [128, len(FN), 16], f16), "MB": ("sbuf", [128, len(BN), 16], b16),
                 "BF": ("sbuf", [128, len(FN), 144], f16), "BB": ("sbuf", [128, len(BN), 144], b16)})
 for _b in range(8):
     SCRATCH["ps%d" % _b] = ("psum", [128, 512], f32)
-SEMAPHORES = ["sv", "sa", "st", "sg", "loc"] + ["d%d" % i for i in range(12)] + ["ar%d" % i for i in range(4)]
+SEMAPHORES = ["sv", "sa", "st", "sg", "loc"] + ["d%d" % i for i in range(32)] + ["ar%d" % i for i in range(4)]
 EST = []
 
 
 def _cover(L):
+    def ok(v, x): return (not 0 <= v <= 15) if x is None else v == x
     out, s = [], 0
     while s < len(L):
-        best, base = None, (L[s] if L[s] is not None else -1)
+        base = L[s] if L[s] is not None else -1
+        best = (1, [[0, 1]], base)
+
+        def steps(o): return [x for x in ({0, L[s + o] - base} if s + o < len(L) and L[s + o] is not None else {0, 100}) if abs(x) < 32768]
         for n1 in range(1, min(16, len(L) - s) + 1):
-            for s1 in ({L[s + 1] - base} if n1 > 1 and L[s + 1] is not None else {0, 100}):
-                for s2 in ({0, L[s + n1] - base} if s + n1 < len(L) and L[s + n1] is not None else {0, 100}):
-                    n2 = 0
-                    if max(abs(s1), abs(s2)) > 32767: continue
-                    while s + (n2 + 1) * n1 <= len(L) and all(
-                            (not 0 <= base + n2 * s2 + j * s1 <= 15) if L[s + n2 * n1 + j] is None else base + n2 * s2 + j * s1 == L[s + n2 * n1 + j]
-                            for j in range(n1)):
-                        n2 += 1
-                    if n2 and (best is None or n1 * n2 > best[0]): best = (n1 * n2, [[s2, n2], [s1, n1]], base)
+            for s1 in (steps(1) if n1 > 1 else [0]):
+                if not all(ok(base + j * s1, L[s + j]) for j in range(n1)): continue
+                for s2 in steps(n1):
+                    n2 = 1
+                    while True:
+                        m = n1 * n2
+                        for s3 in steps(m):
+                            n3 = 1
+                            while s + (n3 + 1) * m <= len(L) and all(ok(base + n3 * s3 + j // n1 * s2 + j % n1 * s1, L[s + n3 * m + j]) for j in range(m)): n3 += 1
+                            if m * n3 > best[0]: best = (m * n3, [[s3, n3], [s2, n2], [s1, n1]], base)
+                        if s + (n2 + 1) * n1 <= len(L) and all(ok(base + n2 * s2 + j * s1, L[s + n2 * n1 + j]) for j in range(n1)): n2 += 1
+                        else: break
         out.append((s,) + best); s += best[0]
     return out
 
 
-def _prog(L):
-    out = []
-    for x in sorted(set(L) - {0}):
-        rest = {i for i, y in enumerate(L) if y == x}
-        while rest:
-            best = None
-            for a in sorted(rest):
-                for st in [1] + [b - a for b in sorted(rest) if b > a]:
-                    n = 1
-                    while a + n * st in rest and n < 32: n += 1
-                    if best is None or n > best[2]: best = (a, st, n)
-            out.append(best + (float(x),)); rest -= {best[0] + k * best[1] for k in range(best[2])}
-    return out
+COVER = {n: _cover(x) for n, x in PHI.items()}
+VCOVER = [_cover([int(x * 128) for y in list(V8.values())[:9] for x in y]), _cover(V8["bU"]), _cover(sum(V16.values(), []))]
 
 
 def rank_program(g, core, T, topo):
     rank = T.rank_of(core)
     if rank is None:
         return
-    ops, lastw, readers = [], {}, {}
+    ops, lastw, readers, users, bankof = [], {}, {}, {}, {}
     vec, act, ten = g.vector, g.scalar, g.tensor
     CY = 0.83e-3
 
     def add(alts, R, Wr, lat=0.0, sem=None, cnt=1):
-        i, deps, eng = len(ops), set(), "".join(alts)
+        i, deps, eng, new = len(ops), set(), "".join(alts), None
         for t in list(R) + list(Wr):
             if t in lastw: deps.add(lastw[t])
-            if t.startswith("ps") and t != "ps7": deps.update(j for j in readers.get(t, ()) if ops[j]["e"] != eng or len(eng) > 1)
+            if t[0] == "#":
+                deps.update(j for j in readers.get(t, ()) if ops[j]["e"] != eng or len(eng) > 1)
+                if t not in users: new = t
+                users.setdefault(t, set()).add(i)
         for t in Wr: deps.update(readers.get(t, ()))
         for t in R: readers.setdefault(t, []).append(i)
         for t in Wr: lastw[t] = i; readers[t] = []
         deps.discard(i)
-        ops.append({"e": eng, "a": alts, "d": deps, "l": lat, "s": sem, "n": cnt, "k": (list(Wr) + ["-"])[0]})
+        ops.append({"e": eng, "a": alts, "d": deps, "l": lat, "s": sem, "n": cnt, "new": new, "ps": [t for t in set(R) | set(Wr) if t[0] == "#"]})
         return i
 
-    def nel(ap): return int(np.prod(ap.shape[1:]))
+    def tile():
+        return "#%d" % len(ops)
+
+    def ps(t, a, b, st=1, rows=128): return (t, a, b, st, rows)
+
+    def rs(x): return T["ps%d" % bankof[x[0]]][0:x[4], x[1]:x[2]:x[3]] if isinstance(x, tuple) else x
+
+    def nel(x): return len(range(x[1], x[2], x[3])) if isinstance(x, tuple) else int(np.prod(x.shape[1:]))
 
     def cv(out, cy): return OVH + max(64, nel(out) * cy) * CY
 
     def vts(out, in0, s1, s2, o0, o1, cy=1.0):
-        if o1 is None: return (lambda: vec.tensor_scalar(out, in0, s1, None, o0)), cv(out, cy)
-        return (lambda: vec.tensor_scalar(out, in0, s1, s2, o0, o1)), cv(out, cy)
+        if o1 is None: return (lambda: vec.tensor_scalar(rs(out), rs(in0), s1, None, o0)), cv(out, cy)
+        return (lambda: vec.tensor_scalar(rs(out), rs(in0), s1, s2, o0, o1)), cv(out, cy)
 
-    def vcp(out, a, cy=1.0): return (lambda: vec.tensor_copy(out, a)), cv(out, cy)
+    def vcp(out, a, cy=1.0): return (lambda: vec.tensor_copy(rs(out), rs(a))), cv(out, cy)
 
-    def aac(out, a, fn, bias=0.0, scale=1.0, cy=1.0): return (lambda: act.activation(out, a, fn, bias, scale)), cv(out, cy) + 0.02
+    def aac(out, a, fn, bias=0.0, scale=1.0, cy=1.0): return (lambda: act.activation(rs(out), rs(a), fn, bias, scale)), cv(out, cy) + 0.015
 
     def ts(out, in0, s1, s2, o0, o1, R, Wr, cy=1.0): add({"v": vts(out, in0, s1, s2, o0, o1, cy)}, R, Wr)
 
-    def tt(out, a, b, o, R, Wr, cy=2.0): add({"v": (lambda: vec.tensor_tensor(out, a, b, o), cv(out, cy))}, R, Wr)
+    def tt(out, a, b, o, R, Wr, cy=2.0): add({"v": (lambda: vec.tensor_tensor(rs(out), rs(a), rs(b), o), cv(out, cy))}, R, Wr)
 
     def cp(out, a, R, Wr, cy=1.0): add({"v": vcp(out, a, cy)}, R, Wr)
 
@@ -162,26 +162,21 @@ def rank_program(g, core, T, topo):
 
     def frelu(out, a, bi, R, Wr): add({"v": vts(out, a, bi, 0.0, AL.add, AL.max), "a": aac(out, a, AF.Relu, bi)}, R, Wr)
 
-    def fsign(out, a, R, Wr): add({"v": vts(out, a, -1.0, 1.0, AL.max, AL.min), "a": aac(out, a, AF.Sign)}, R, Wr)
+    def sign(out, a, R, Wr): add({"v": vts(out, a, -1.0, 1.0, AL.max, AL.min), "a": aac(out, a, AF.Sign)}, R, Wr)
 
     def fne(out, a, R, Wr): add({"v": vts(out, a, 0.0, None, AL.not_equal, None, 0.5), "a": aac(out, a, AF.Abs)}, R, Wr)
 
     def ms(out, c, Wr, cy=1.0): add({"v": (lambda: vec.memset(out, c), cv(out, cy))}, [], Wr)
 
-    def scan(out, d0, d1, init, o0, o1, R, Wr): add({"v": (lambda: vec.tensor_tensor_scan(out, d0, d1, init, o0, o1), cv(out, 1))}, R, Wr)
+    def scan(out, d0, d1, init, o0, o1, R, Wr): add({"v": (lambda: vec.tensor_tensor_scan(out, d0, rs(d1), init, o0, o1), cv(out, 1))}, R, Wr)
 
-    def tr(out, a, R, Wr): add({"v": (lambda: vec.transpose(out, a), cv(out, 1))}, R, Wr)
+    def ac(out, a, R, Wr, fn=AF.Copy, bias=0.0, cy=1.0): add({"a": aac(out, a, fn, bias, 1.0, cy)}, R, Wr)
 
-    def ac(out, a, R, Wr): add({"a": aac(out, a, AF.Copy, cy=GC)}, R, Wr)
-
-    def mm(out, pairs, R, Wr, k=1, st=True, sp=True):
+    def mm(trips, R, Wr, st=True, sp=True, k=1):
         def f():
-            for n, (l, r) in enumerate(pairs): x = ten.matmul(out, l, r, st and n == 0, sp and n == len(pairs) - 1)
+            for n, (o, l, r) in enumerate(trips): x = ten.matmul(rs(o), l, r, st and n == 0, sp and n == len(trips) - 1)
             return x
-        add({"t": (f, 0.05 + len(pairs) * (0.01 + max(64, nel(out)) * k * PEC))}, R, Wr)
-
-    def mms(out, parts, Wr):
-        for n, (pairs, R) in enumerate(parts): mm(out, pairs, R, Wr, 1, n == 0, n == len(parts) - 1)
+        add({"t": (f, 0.03 + sum(0.012 + max(64, nel(o)) * k * PEC for o, l, r in trips))}, R, Wr, 0.05)
 
     def io(out, pat, base, cm, Wr, fl=True):
         if fl: f = lambda: g.iota(out, pat, base, cm, allow_small_or_imprecise_dtypes=True)
@@ -222,12 +217,14 @@ def rank_program(g, core, T, topo):
                                                  src=buf[:, o:o + BORD], dst=buf[:, o + V + (d - 1) * BORD:o + V + d * BORD]))
                 g.remote_dma_fused(trs, local_sem=T.sem.loc)
         locn[0] += len(offs) * sum(len(x) for x in mine.values())
-        i = add({"g": (f, 0.3 * len(offs))}, R, [], 0.0, "loc", 0)
+        i = add({"g": (f, 0.4 * len(offs))}, R, [], 0.0, "loc", 0)
         ops[add({"x": (None, 0.0)}, [], Wr, lat, sem, inc_in * len(offs))]["o"] = i
 
-    def send_g(r): send(T["Gw%d" % r], [0], "ar%d" % (2 * r), ["Gw%d_0" % r], ["Gw%dr" % r], 4.0)
+    def tk(n, xs): return ["%s_%d" % (n, x) for x in xs]
 
-    def send_b(r): send(T["W%d" % r], [LUTW + WN * c for c in range(3)], "ar%d" % (2 * r + 1), ["W%d_0_%d" % (r, c) for c in range(3)], ["W%dr" % r], 5.0)
+    def send_g(r): send(T["Gw%d" % r], [0], "ar%d" % (2 * r), tk("Gw%d" % r, (0, 1)), ["Gw%dr" % r], 5.0)
+
+    def send_b(r): send(T["W%d" % r], [LUTW + WN * c for c in range(3)], "ar%d" % (2 * r + 1), tk("W%d" % r, range(6)), ["W%dr" % r], 5.0)
 
     dma("s", [(T.LI[f::16, :], T.leaf0[:, f * V:(f + 1) * V]) for f in range(8)], [], ["LIa"])
     dma("a", [(T.LI[f::16, :], T.leaf0[:, f * V:(f + 1) * V]) for f in range(8, 12)] +
@@ -235,69 +232,93 @@ def rank_program(g, core, T, topo):
     io(T.PI[:, 0:1], [[0, 1]], 0, 1, ["PI"], False)
     io(T.IDI[:], [[1, V]], V * rank, 0, ["IDI"], False)
     dma("s", [(T.LI[12::16, :], T.IDI[12::16, :])], ["IDI"], ["LIc"], 2.0)
-    dma("s", [(T.TR[m::16, :], T.tab0[:]) for m in range(16)], [], ["TR"], 3.0)
-    dma("s", [(T.RQ[:], T.req[:]), (T.CE[:, 0:4096], T.cells[:]), (T.CE[:, 4096:8192], T.cells[:]), (T.CE[:, 8192:VOID], T.cells[:, 0:VOID - 8192])],
-        ["TR"], ["RQ", "CEa"], 12.0)
-    ms(T.CE[:, VOID:], 65536.0, ["CEb"])
+    dma("s", [(T.TR[m::16], T.tab0[:]) for m in range(16)], ["IDI"], ["TR"], 4.0)
 
-    for n, (sh, an) in enumerate([(0, 15), (2, 3), (0, 3), (1, 7), (4, 7), (4, 1), (0, 31)]):
+    for n, (sh, an) in enumerate([(0, 15), (2, 3), (0, 3), (4, 7), (2, 31), (0, 1)]):
         ts(T.PJ[:, n:n + 1], T.PI[:, 0:1], sh, an, AL.logical_shift_right, AL.bitwise_and, ["PI"], ["PJ%d" % n])
-    cp(T.PF[:, 0:7], T.PJ[:, 0:7], ["PJ%d" % n for n in range(7)], ["PF"])
-    p16, kc, lc, q2, gc_, hc, c32 = [T.PF[:, n:n + 1] for n in range(7)]
-    io(T.GI[:], [[1, 8]], 0, 0, ["GI"])
-    ts(T.GM[:], T.GI[:], gc_, None, AL.is_equal, None, ["GI", "PF"], ["GM"])
-    ts(T.HC[:], T.GI[:, 0:2], hc, None, AL.is_equal, None, ["GI", "PF"], ["HC"])
-    io(T.OHI[:], [[0, NVT], [1, 16]], 0, 0, ["OHI"])
-    ms(T.RST[:], 1.0, ["RST"]); ms(T.RST[:, 0::16], 0.0, ["RST"]); ms(T.VAL[:, 0:16 * NV0], 0.0, ["VAL"])
-    ms(T.TWO[:, 0:16], 2.0, ["TWO"]); ms(T.TWO[:, 16:32], 0.5, ["TWO"]); ms(T.POWR[:, 32:48], 0.0, ["ZR"])
-    for b, (a0, a1) in enumerate([(0, 16 * NV0), (16 * NV0, 16 * NVT)]):
-        tk, L = [], [x for y in VEC[b].values() for x in y]
-        for s, n, pat, base in (_cover(L) if b else []):
-            tk.append("VAL%d_%d" % (b, s)); io(T.VAL[:, a0 + s:a0 + s + n], pat, base, 0, [tk[-1]])
-        for s, st, n, x in ([] if b else _prog(L)):
-            o = T.VAL[:, a0 + s:a0 + s + (n - 1) * st + 1:st]
-            tk.append("VAL%d_%d" % (b, s))
-            add({"v": (lambda o=o, x=x: vec.memset(o, x), cv(o, 1)), "a": aac(o, T.TWO[:, 0:n], AF.Identity, x, 0.0)}, ["VAL", "TWO"], [tk[-1]])
-        ts(T.OH[:, a0:a1], T.OHI[:, a0:a1], p16, None, AL.is_equal, None, ["OHI", "PF"], ["OH%d" % b])
-        tt(T.OHI[:, a0:a1], T.OH[:, a0:a1], T.VAL[:, a0:a1], AL.mult, tk + ["OH%d" % b], ["OP%d" % b])
-        scan(T.VC[:, a0:a1], T.RST[:, 0:a1 - a0], T.OHI[:, a0:a1], 0.0, AL.mult, AL.add, ["OP%d" % b, "RST"], ["VC%d" % b])
+    cp(T.PF[:, 0:1], T.PJ[:, 0:1], ["PJ0"], ["PF0"])
+    cp(T.PF[:, 1:6], T.PJ[:, 1:6], ["PJ%d" % n for n in range(1, 6)], ["PF1"])
+    p16, kc, lc, gc_, p4, odd = [T.PF[:, n:n + 1] for n in range(6)]
+    PF = ["PF0", "PF1"]
 
-    def vc(n): return T.VC[:, 16 * VN.index(n) + 15:16 * VN.index(n) + 16]
-    V0, V1 = "VC0", "VC1"
+    def vc(n):
+        if n in CN: return T.CO[:, CN.index(n):CN.index(n) + 1]
+        a = 87 + 8 * list(V8).index(n[1:]) if n[0] == "k" else {"si": 127, "sj": 143, "zrow": 159, "nwc1": 175}.get(n) or 8 * list(V8).index(n) + 7
+        return T.VC[:, a:a + 1]
+
+    def vt(*ns): return ["c" + n if n in CN else {"k": "VCk", "s": "VCs", "z": "VCs", "n": "VCs", "b": "VCb"}.get(n[0], "VC8") for n in ns]
+
+    def co(n, a, s1, s2, o0, o1, R): ts(vc(n), a, s1, s2, o0, o1, R, vt(n))
+    co("f13", p16, 13.0, None, AL.is_ge, None, ["PF0"]); co("f12", p16, 12.0, None, AL.is_ge, None, ["PF0"])
+    for n, (at, x, y) in V2_.items(): faff(vc(n), vc("f%d" % at), float(y - x), float(x), vt("f%d" % at), vt(n))
+    for n, o, x, y in [("le12", AL.is_le, 12.0, 1.0), ("le12n", AL.is_le, 12.0, -1 / DL), ("is13", AL.is_equal, 13.0, 1.0), ("is14", AL.is_equal, 14.0, 0.5),
+                       ("is0", AL.is_equal, 0.0, 524288.0), ("is1", AL.is_equal, 1.0, -1 / 32)]: co(n, p16, x, y, o, AL.mult, ["PF0"])
+    faff(vc("p256"), p16, 16.0, 0.0, ["PF0"], vt("p256")); faff(vc("bX"), odd, 2048.0, -2048.0, PF, vt("bX"))
+    co("lo2", lc, 2.0, None, AL.is_lt, None, PF); co("hi2", lc, 2.0, None, AL.is_ge, None, PF)
+    co("c8", kc, 2.0, -4.0, AL.min, AL.mult, PF); co("c8", vc("c8"), p16, None, AL.add, None, PF + vt("c8"))
+    io(T.GI[:], [[1, 32]], 0, 0, ["GI"])
+    ts(T.GM[:], T.GI[:, 0:8], gc_, None, AL.is_equal, None, ["GI"] + PF, ["GM"])
+    faff(T.GN[:], T.GM[:], -1.0, 0.0, ["GM"], ["GN"])
+    ms(T.RST[:], 1.0, ["RST"]); ms(T.RST[:, 0::16], 0.0, ["RST"]); ms(T.RS8[:], 1.0, ["RS8"]); ms(T.RS8[:, 0::8], 0.0, ["RS8"])
+    ms(T.TWO[:, 0:16], 2.0, ["TWO"]); ms(T.TWO[:, 16:32], 0.5, ["TWO"]); ms(T.POWR[:, 32:48], 0.0, ["ZR"])
+    io(T.PIW[:], [[4, 8], [1, 4], [0, 4]], 0, 0, ["PIW"]); io(T.PIW[:, 2::4], [[4, 8], [0, 4]], 3, 0, ["PIW"])
+    io(T.PJW[:], [[4, 8], [0, 4], [1, 4]], 0, 0, ["PJW"]); io(T.PJW[:, 2::4], [[4, 8], [1, 4]], 0, 0, ["PJW"])
+    for q in (12, 13, 14):
+        io(T.PIW[:, q::16], [[4, 8]], SI[q], 0, ["PIW"]); io(T.PJW[:, q::16], [[4, 8]], SJ[q], 0, ["PJW"])
+    vtk = []
+    for a0, cov in zip((0, 72, 80), VCOVER):
+        vtk.append(["VAL%d" % (a0 + y[0]) for y in cov])
+        for s, n, pat, base in cov: io(T.VAL[:, a0 + s:a0 + s + n], pat, base, 0, ["VAL%d" % (a0 + s)])
+    io(T.OHI[:], [[0, 10], [1, 8]], 0, 0, ["OHI"])
+    for a0, n, ft, x, va, R, tok in ((0, 72, vc("c8"), 1 / 128, T.VAL[:, 0:72], vtk[0], "VC8"), (72, 8, vc("c8"), 1.0, T.VAL[:, 72:80], vtk[1], "VCb"),
+                                     (80, 32, kc, 1 / 128, T.VAL[:, 0:32], vtk[0], "VCk")):
+        ts(T.OH[:, a0:a0 + n], T.OHI[:, 0:n], ft, x, AL.is_equal, AL.mult, ["OHI"] + PF + vt("c8"), ["OH" + tok])
+        tt(T.PR[:, a0:a0 + n], T.OH[:, a0:a0 + n], va, AL.mult, ["OH" + tok] + R, ["PR" + tok])
+        scan(T.VC[:, a0:a0 + n], T.RS8[:, 0:n], T.PR[:, a0:a0 + n], 0.0, AL.mult, AL.add, ["PR" + tok, "RS8"], [tok])
+    for a0 in (112, 128): ts(T.OH[:, a0:a0 + 16], T.GI[:, 0:16], p16, None, AL.is_equal, None, ["GI", "PF0"], ["OH%d" % a0])
+    oh, OHT = T.OH[:, 112:144], ["OH112", "OH128"]
+    tt(T.PR[:, 112:128], T.OH[:, 112:128], T.PIW[:, 0:16], AL.mult, OHT + ["PIW"], ["PRa"])
+    tt(T.PR[:, 128:144], T.OH[:, 112:128], T.PJW[:, 0:16], AL.mult, OHT + ["PJW"], ["PRb"])
+    tt(T.PR[:, 144:176], oh, T.VAL[:, 80:112], AL.mult, OHT + vtk[2], ["PRc"])
+    scan(T.VC[:, 112:176], T.RST[:, 0:64], T.PR[:, 112:176], 0.0, AL.mult, AL.add, ["PRa", "PRb", "PRc", "RST"], ["VCs"])
+    co("t5", vc("c8"), 3.0, kc, AL.is_equal, AL.mult, PF + vt("c8"))
+    for n, x in (("cAf", "cA0"), ("cAt", "cA1")): faff(vc(n), vc("t5"), 5.0, vc(x), vt("t5", x), vt(n))
+    faff(vc("bM"), vc("bU"), 1.0, MG, vt("bU"), vt("bM")); faff(vc("bY"), vc("bU"), -1.0, vc("tY"), vt("bU", "tY"), vt("bY"))
+    for n in ("A1", "A2"): faff(vc("n" + n), vc(n), -1.0, 0.0, vt(n), vt("n" + n))
     scan(T.POWR[:, 0:16], T.TWO[:, 0:16], T.POWR[:, 32:48], 0.5, AL.mult, AL.add, ["TWO", "ZR"], ["PWa"])
     scan(T.POWR[:, 16:32], T.TWO[:, 16:32], T.POWR[:, 32:48], 65536.0, AL.mult, AL.add, ["TWO", "ZR"], ["PWb"])
-    tt(T.POWC[:], T.POWR[:, 0:32], T.OH[:, 0:32], AL.mult, ["PWa", "PWb", "OH0"], ["PWc"])
+    tt(T.POWC[:], T.POWR[:, 0:32], oh, AL.mult, ["PWa", "PWb"] + OHT, ["PWc"])
     scan(T.POWR[:, 0:32], T.RST[:, 0:32], T.POWC[:], 0.0, AL.mult, AL.add, ["PWc", "RST"], ["PWa", "PWb"])
     w2m, w15 = T.POWR[:, 15:16], T.POWR[:, 31:32]
-    ts(T.PW2[:, 0:1], w2m, 16.0, w2m, AL.is_ge, AL.mult, ["PWa"], ["PW2a"])
-    ts(T.PW2[:, 1:2], w2m, 200.0, w2m, AL.is_le, AL.mult, ["PWa"], ["PW2b"])
+    co("w2hi", w2m, 16.0, w2m, AL.is_ge, AL.mult, ["PWa"]); co("w2lo", w2m, 200.0, w2m, AL.is_le, AL.mult, ["PWa"])
 
-    ts(T.PM[:, 0:1], p16, 13.0, 15.0, AL.is_ge, AL.mult, ["PF"], ["PM"])
-    ts(T.PM[:, 1:2], T.PM[:, 0:1], 1.0, None, AL.add, None, ["PM"], ["PM1"])
-    ts(T.PM[:, 2:3], T.PM[:, 0:1], -1 / 16, 1.0, AL.mult, AL.add, ["PM"], ["PM2"])
-    ts(T.PM[:, 3:4], p16, 8.0, vc("bR"), AL.is_lt, AL.mult, ["PF", V0], ["PM3"])
-    for h in range(NCH):
-        x = T.LI[:, h * w:(h + 1) * w]
-        ts(x, x, T.PM[:, 1:2], None, AL.mult, None, ["LIa", "LIb", "LIc", "PM1"], ["LI%d" % h])
+    for h in range(2):
+        x = T.LI[:, h * BORD:(h + 1) * BORD]
+        ts(x, x, vc("mul"), vc("off"), AL.mult, AL.add, ["LIa", "LIb", "LIc"] + vt("mul", "off"), ["LI%d" % h])
         ts(x, x, 4095, None, AL.bitwise_and, None, ["LI%d" % h], ["LI%d" % h])
-        ts(T.Gw0[:, h * w:(h + 1) * w], x, T.PM[:, 2:3], 2048.0, AL.mult, AL.min, ["LI%d" % h, "PM2"], ["Gw0_%d" % h])
+        ts(T.Gw0[:, h * BORD:(h + 1) * BORD], x, vc("sub"), 0.0, AL.subtract, AL.max, ["LI%d" % h] + vt("sub"), tk("Gw0", (2 * h, 2 * h + 1)))
     send_g(0)
-    for c in range(3):
-        x = T.TR[:, c * V:(c + 1) * V]
-        ts(x, x, w15, None, AL.mult, None, ["TR", "PWa"], ["TR%d" % c])
-        ts(x, x, 32768, None, AL.bitwise_and, None, ["TR%d" % c], ["TR%d" % c])
-        ts(T.W0[:, LUTW + WN * c:LUTW + WN * c + V], x, 0.0, None, AL.is_gt, None, ["TR%d" % c], ["W0_%d_%d" % (h, c) for h in range(NCH)])
+    for h in range(2):
+        x, a0 = T.TR[:, :, h * BORD:(h + 1) * BORD], LUTW + h * BORD
+        ts(x, x, w15, None, AL.mult, None, ["TR", "PWa"], ["TR%d" % h])
+        ts(x, x, 32768, None, AL.bitwise_and, None, ["TR%d" % h], ["TR%d" % h])
+        for c in range(3):
+            ts(T.W0[:, a0 + WN * c:a0 + WN * c + BORD], T.TR[:, c, h * BORD:(h + 1) * BORD], 0.0, None, AL.is_gt, None, ["TR%d" % h], tk("W0", (6 * h + c, 6 * h + 3 + c)))
     send_b(0)
     cp(T.fanU[:], T.fanI[:], ["fanI"], ["fanU"])
-    cp(T.IDf[:], T.IDI[:], ["IDI"], ["IDf"])
-    io(T.IW[:], [[1, WN]], 0, 0, ["IW"])
-    fcp(T.Gc[:], T.IW[:].indirect(T.fanU[:]), ["IW", "fanU"], ["Gc"], GC)
-    cp(T.ps7[:], T.RQ[:], ["RQ"], ["ps7"])
+    ts(T.IDf[:], T.IDI[:], -1.0, 2048.0, AL.mult, AL.add, ["IDI"], ["IDf"])
+    dma("s", [(T.RQ[:], T.req[:]), (T.CE[:, 0:CE0], T.cells[:, 4096 - CE0:]), (T.CE[:, CE0:CE0 + 4096], T.cells[:]),
+              (T.CE[:, CE0 + 4096:], T.cells[:, 0:CEW - CE0 - 4096])], ["Gw0r"], ["RQ", "CE"], 10.0)
+    ts(T.IW[:, 0:V], T.IDI[:], -1.0 * V * rank, None, AL.add, None, ["IDI"], ["IW0"])
+    for a0 in (V, 2 * V): faff(T.IW[:, a0:min(WN, a0 + V)], T.IW[:, 0:min(V, WN - a0)], 1.0, float(a0), ["IW0"], ["IW%d" % a0])
+    fcp(T.Gc[:], T.IW[:].indirect(T.fanU[:]), ["IW0", "IW512", "IW1024", "fanU"], ["Gc"], GC)
+    bankof["rq"] = 7
+    fcp(ps("rq", 0, V), T.RQ[:], ["RQ"], ["rq"])
 
     for k, n in enumerate(PN):
-        for s, x, pat, base in _cover(PHI[n]): io(T.PH[:, k, s:s + x], pat, base, 0, ["PH%s_%d" % (n, s)])
+        for s, x, pat, base in COVER[n]: io(T.PH[:, k, s:s + x], pat, base, 0, ["PH%s_%d" % (n, s)])
 
-    def P_(n, a=0, b=16): return T.PH[:, PN.index(n), a:b], ["PH%s_%d" % (n, y[0]) for y in _cover(PHI[n])]
+    def P_(n, a=0, b=16, st=1): return T.PH[:, PN.index(n), a:b:st], ["PH%s_%d" % (n, y[0]) for y in COVER[n]]
 
     def mf(n, a=0, b=16, st=1): return T.MF[:, FN.index(n), a:b:st], "MF" + n
 
@@ -305,46 +326,49 @@ def rank_program(g, core, T, topo):
 
     def tm(a, n): return T.TM[:, a:a + n], "TM%d" % a
 
-    def eqm(dst, phi, feat, x, tok=()): ts(dst[0], phi[0], feat, x, AL.is_equal, AL.mult, phi[1] + ["PF"] + list(tok), [dst[1]])
+    def eqm(dst, phi, feat, x, tok=()): ts(dst[0], phi[0], feat, x, AL.is_equal, AL.mult, phi[1] + PF + list(tok), [dst[1]])
 
-    def col(dst, z, tok, sc=1.0): faff(dst[0], z, sc, 0.0, [tok], [dst[1]])
+    def col(dst, z, tok, sc=1.0): faff(dst[0], z, sc, 0.0, tok, [dst[1]])
+
+    def plus(dst, a, b): tt(dst[0], a[0], b[0], AL.add, [a[1], b[1]], [dst[1]])
 
     def ramp(dst, phi, feat, tmp, top):
-        ts(tmp[0], phi[0], feat, 1.0, AL.subtract, AL.add, phi[1] + ["PF"], [tmp[1]])
+        ts(tmp[0], phi[0], feat, 1.0, AL.subtract, AL.add, phi[1] + PF, [tmp[1]])
         ts(tmp[0], tmp[0], -top / 2, 0.0, AL.mult, AL.min, [tmp[1]], [tmp[1]])
         ts(dst[0], tmp[0], -top, None, AL.max, None, [tmp[1]], [dst[1]])
     add({"v": (lambda: vec.memset(T.MF[:], 0.0), 0.3)}, [], ["MF" + n for n in FN])
     add({"v": (lambda: vec.memset(T.MB[:], 0.0), 0.3)}, [], ["MB" + n for n in BN])
     ms(T.BF[:, :, 128:144], 0.0, ["BFz"], 0.5); ms(T.BB[:, :, 128:144], 0.0, ["BBz"], 0.5)
-    for M, N, ns, ft in ((T.MF, FN, FM[0], p16), (T.MF, FN, FM[1][:3], p16), (T.MF, FN, FM[1][4:6], q2), (T.MF, FN, FM[2][:5], p16), (T.MB, BN, BM[0], p16)):
+    for M, N, ns, x in ((T.MF, FN, FM[0][:3], 1 / DL), (T.MF, FN, FM[0][3:6], -1 / DL), (T.MB, BN, BM[0], 1.0)):
         a0, b0 = N.index(ns[0]), PN.index(ns[0])
-        ts(M[:, a0:a0 + len(ns), :], T.PH[:, b0:b0 + len(ns), :], ft, None, AL.is_equal, None, sum([P_(n)[1] for n in ns], ["PF"]),
+        ts(M[:, a0:a0 + len(ns), :], T.PH[:, b0:b0 + len(ns), :], p16, x, AL.is_equal, AL.mult, sum([P_(n)[1] for n in ns], ["PF0"]),
            [("MF" if N is FN else "MB") + n for n in ns])
-    eqm(mf("XLn"), P_("XL"), p16, -1.0); eqm(mf("HA"), P_("HA"), p16, -1.0)
-    x = mf("XP", 0, 16, 2); ts(x[0], x[0], -1.0, None, AL.mult, None, [x[1]], [x[1]])
-    for n, pn, vn in [("VPa", "CK", "wV"), ("VPb", "CL", "wV"), ("PA3", "CK", "wP"), ("PB3", "CL", "wP")]: eqm(mf(n), P_(pn), kc, vc(vn), [V0])
-    eqm(mf("E12"), P_("COL"), p16, vc("is12"), [V1]); eqm(mf("UH", 8, 11), P_("COL", 0, 3), vc("zrow"), -1.0, [V1])
-    col(mf("UH", 11, 12), vc("u3"), V1); col(mf("UA", 11, 12), vc("ua"), V1)
-    eqm(mb("Zs", 8, 11), P_("COL", 0, 3), kc, -0.5); eqm(mb("Zs", 11, 14), P_("COL", 0, 3), lc, 0.5)
-    ramp(mb("Ze", 8, 11), P_("COL", 0, 3), kc, tm(0, 3), 1.0); ramp(mb("Ze", 11, 14), P_("COL", 0, 3), lc, tm(3, 3), 1.0)
-    eqm(mb("T1s", 0, 13), P_("COL", 0, 13), p16, -0.5); eqm(mb("T1s", 3, 12, 4), P_("COL", 0, 3), kc, 0.5)
-    eqm(mb("T1s", 13, 14), P_("RID", 0, 1), p16, 0.5); col(mb("T2s"), *mb("T1s"), -1.0)
-    ramp(tm(16, 12), P_("CL", 0, 12), lc, tm(16, 12), 1.0); eqm(tm(32, 12), P_("CK", 0, 12), kc, 1.0)
-    tt(mb("Te", 0, 12)[0], tm(16, 12)[0], tm(32, 12)[0], AL.mult, ["TM16", "TM32"], ["MBTe"])
-    eqm(mb("Te", 3, 12, 4), P_("COL", 0, 3), kc, -0.5); eqm(mb("Te", 12, 14), P_("RID", 0, 2), p16, -0.5)
-    eqm(mb("VT1"), P_("VT1"), kc, 1.0); eqm(mb("VT2"), P_("VT2"), kc, 1.0)
-    for n, a0, x in (("Zp1", 15, 1.0), ("Zm1", 15, -1.0), ("ONE", 0, 1.0)): ms(mb(n, a0)[0], x, ["MB" + n])
-    for n, c0, c1, lo, hi in [("A1", 14, 15, "valo", "vahi"), ("B1", 14, 15, "vblo", "vbhi"), ("A4", 2, 6, "valo", "vahi"), ("B4", 2, 6, "vblo", "vbhi")]:
-        col(mb(n, c0, c0 + 1), vc(lo), V0); col(mb(n, c1, c1 + 1), vc(hi), V0)
-    for n, pn, vn in [("T1a", "VT1", "w3"), ("T1b", "VT1", "wb"), ("T2a", "VT2", "wb"), ("T2b", "VT2", "w3")]: eqm(mb(n), P_(pn), kc, vc(vn), [V0])
-    col(mb("Zc1", 15), vc("nwc1"), V1); col(mb("Zc2", 15), T.PW2[:, 0:1], "PW2a", -1 / 16)
-    col(mb("Zlb", 15), T.PW2[:, 1:2], "PW2b"); col(mb("ZT", 15), w2m, "PWa")
-    eqm(mb("IV"), P_("COL"), p16, 16384.0); col(mb("BH"), T.VAL[:, 16 * NVT - 16:], "OP1")
-    eqm(mb("Hs", 0, 6), P_("HA", 0, 6), kc, -2048.0); eqm(mb("Hs", 6, 12), P_("HA", 0, 6), lc, 2048.0)
-    ramp(mb("He", 0, 6), P_("HA", 0, 6), kc, tm(48, 6), 4096.0); ramp(tm(54, 6), P_("HA", 0, 6), lc, tm(54, 6), 4096.0)
-    eqm(tm(60, 6), P_("HA", 0, 6), lc, 16384.0)
-    tt(mb("He", 6, 12)[0], tm(54, 6)[0], tm(60, 6)[0], AL.add, ["TM54", "TM60"], ["MBHe"])
-    eqm(mb("He", 12, 16), P_("COL", 0, 4), lc, 4096.0)
+    for n in (13, 12):
+        eqm(mf("I%d" % n, 0, n), P_("COL", 0, n), p16, 1 / DL); eqm(mf("R%d" % n, 0, n), P_("RID", 0, n), p16, -1 / DL)
+    eqm(mf("J13", 0, 13), P_("COL", 0, 13), p16, 1.0)
+    eqm(mf("XC", 2, 12, 4), P_("RID", 0, 3), p16, 1.0); eqm(mf("XL", 3, 12, 4), P_("COL", 13, 16), p16, 1 / 16)
+    eqm(mf("XP", 2, 12, 4), P_("COL", 3, 12, 4), p16, 2048.0); eqm(mf("XP", 3, 12, 4), P_("COL", 3, 12, 4), p16, -2048.0)
+    si, sj = (T.PIW[:, 0:16], ["PIW"]), (T.PJW[:, 0:16], ["PJW"])
+    eqm(mf("XA"), si, kc, vc("lo2"), vt("lo2")); eqm(mf("XB"), sj, kc, vc("hi2"), vt("hi2")); eqm(mf("I256"), P_("COL"), p16, 256.0)
+    eqm(mf("RMa"), P_("CK"), vc("si"), 16.0, vt("si")); eqm(mf("RMb", 0, 13), P_("CK", 0, 13), vc("sj"), 16.0, vt("sj"))
+    ms(mf("RMb", 14, 15)[0], -1 / 128, ["MFRMb"])
+    eqm(mf("EA"), P_("CK"), lc, 1 / DL); eqm(tm(0, 16), P_("CL"), lc, vc("le12n"), vt("le12n"))
+    faff(mf("EB")[0], tm(0, 16)[0], 1.0, vc("is14"), ["TM0"] + vt("is14"), ["MFEB"])
+    eqm(mf("HA", 0, 6), P_("HK", 0, 6), lc, 1.0)
+    eqm((T.TM[:, 16:22], "TM16"), P_("HK", 0, 6), lc, vc("le12"), vt("le12")); eqm((T.TM[:, 22:26], "TM16"), P_("COL", 0, 4), lc, vc("le12"), vt("le12"))
+    faff(mf("HB")[0], P_("HC")[0], vc("is13"), 0.0, P_("HC")[1] + vt("is13"), ["MFHB"]); plus(mf("HB", 6, 16), mf("HB", 6, 16), tm(16, 10))
+    eqm(mf("Hs", 0, 6), P_("HK", 0, 6), kc, 2048.0); eqm(mf("Hs", 6, 12), P_("HK", 0, 6), lc, -2048.0)
+    ramp(mf("He", 0, 6), P_("HK", 0, 6), kc, tm(48, 6), 4096.0); ramp(tm(54, 6), P_("HK", 0, 6), lc, tm(54, 6), 4096.0)
+    eqm(tm(60, 6), P_("HK", 0, 6), lc, 12288.0); plus(mf("He", 6, 12), tm(54, 6), tm(60, 6))
+    eqm(mf("He", 12, 16), P_("COL", 0, 4), lc, 4096.0)
+    eqm(mf("UH", 8, 11), P_("COL", 0, 3), vc("zrow"), 1.0, vt("zrow")); col(mf("UH", 11, 12), vc("u3"), vt("u3"))
+    ms(mf("UA", 11, 12)[0], 1.0, ["MFUA"]); col(mf("UE", 15), vc("is14"), vt("is14"), -65536.0)
+    eqm(mf("E12", 12, 13), P_("RID", 0, 1), p16, 1.0); col(mf("LP", 15), p16, PF, 1 / 256)
+    col(mb("Zc1", 15), vc("nwc1"), vt("nwc1")); col(mb("Zc2", 15), vc("w2hi"), vt("w2hi"), -1 / 16)
+    col(mb("Zlb", 15), vc("w2lo"), vt("w2lo"), 16.0); col(mb("ZT", 15), w2m, ["PWa"])
+    eqm(mb("IV"), P_("COL"), p16, -524288.0); ms(mb("ONE")[0], 1.0, ["MBONE"])
+    faff(tm(66, 16)[0], si[0], 4.0, 32.0, si[1], ["TM66"]); plus(tm(66, 16), tm(66, 16), (sj[0], "PJW"))
+    faff(mb("KC")[0], tm(66, 16)[0], vc("is1"), vc("is0"), ["TM66"] + vt("is0", "is1"), ["MBKC"])
     TK = {}
     for tag, grp, M, B in (("F", FM, T.MF, T.BF), ("B", BM, T.MB, T.BB)):
         o = 0
@@ -358,205 +382,225 @@ def rank_program(g, core, T, topo):
     def LF(n, s=0): return T.BF[:, FN.index(n), s:s + 128]
 
     def LB(n, s=0): return T.BB[:, BN.index(n), s:s + 128]
-    F0, F1, F2, B0, B1, B2 = [TK[x] for x in ("F0", "F1", "F2", "B0", "B1", "B2")]
-    io(T.D0[:], [[-1, 128]], 0, 1, ["D0"])
-    for u in range(4):
-        ts(T.SW[:, u * 128:(u + 1) * 128], T.D0[:], 16.0 * (u // 2 - u % 2), T.HC[:, u // 2:u // 2 + 1], AL.is_equal, AL.mult, ["D0", "HC"], ["SW%d" % u])
-    io(T.KI[0:2, :], [[0, 8], [-1, 16]], 0, 0, ["KI"])
-    ts(T.KC[0:2, :], T.KI[0:2, :], 1 / 16, None, AL.mult, None, ["KI"], ["KC"]); ms(T.KC[0:1, :], 524288.0, ["KC"])
-    ms(T.ON[:], 1.0, ["ON"], 0.5); ms(T.CB[:], 0.0, ["CB"])
-    io(T.BCI[:], [[1, 16]], 0, 0, ["BCI"], False); cp(T.BC[:], T.BCI[:], ["BCI"], ["BC"])
-    io(T.VNI[:], [[0, 3], [32, w // 32], [0, 2]], 0, 0, ["VNI"])
-    ts(T.VNN[:], T.VNI[:], c32, None, AL.add, None, ["VNI", "PF"], ["VNN"])
-    for h in range(NCH):
-        ms(T["AN%d" % h][:, 16 * w:], 1.0, ["ANp%d" % h])
-        faff(T["AB%d" % h][:, 4 * w:], T.GI[:], 0.0, vc("padAB"), ["GI", V1], ["ABp%d" % h])
+    F0, F1, F2, B0, B1 = [TK[x] for x in ("F0", "F1", "F2", "B0", "B1")]
+    for n, x in enumerate(["kA1", "kA2", "A1", "A2", "kN1", "kN2", "N1", "N2"]):
+        ts(T.W2[:, 8 * n:8 * n + 8], T.GM[:], vc(x), 1.0 - 2 * (n < 2), AL.mult, AL.mult, ["GM"] + vt(x), ["W2_%d" % n])
+    fcp(T.W2[:, 64:72], T.GM[:], ["GM"], ["W2_8"])
+    for n, x in enumerate(["nA1", "nA2", 0.5, "N1", "N2", 0.5, 1.0]):
+        c_ = isinstance(x, str)
+        ts(T.W9[:, 32 * n:32 * n + 32], T.GI[:], p4, vc(x) if c_ else x, AL.is_equal, AL.mult, ["GI"] + PF + (vt(x) if c_ else []), ["W9_%d" % n])
 
-    io(T.BYI[:], [[1, 256]], 0, 0, ["BYI"], False)
-    ts(T.BYI[:], T.BYI[:], w15, None, AL.mult, None, ["BYI", "PWa"], ["BYI"])
+    def wide(n, a0, pn, s, st, x): ts(T[n][:, a0 + s:a0 + 128:st], T[pn][:, s::st], p4, vc(x), AL.is_equal, AL.mult, [pn] + PF + vt(x), [n + str(a0)])
+    for a0, x in ((0, "cA"), (128, "cB")):
+        wide("PA", a0, "PIW", 0, 1, x + "f"); wide("PA", a0, "PIW", 3, 4, x + "t")
+        wide("PB", a0, "PJW", 0, 1, x + "f"); wide("PB", a0, "PJW", 2, 4, x + "t"); wide("PB", a0, "PJW", 14, 16, x + "f")
+    ms(T.PA[:, 256:512], 0.0, ["PA256"], 0.5)
+    for n, pn in (("PAV", "PIW"), ("PBV", "PJW")):
+        wide(n, 0, pn, 0, 1, "cV"); ms(T[n][:, 15::16], 0.0, [n + "0"])
+    WT = tk("W2", range(9)) + tk("W9", range(7)) + ["PA0", "PA128", "PA256", "PB0", "PB128", "PAV0", "PBV0"]
+    ms(T.ON[:], 1.0, ["ON"], 0.5); ms(T.ONH[:], 1.0, ["ONH"], 0.5); ms(T.ONF[:], 1.0, ["ONF"])
+    add({"g": (lambda: g.affine_select(T.IDN[:], T.ONF[:], [[-1, 128]], AL.is_equal, 0.0, 0, 1), 0.4)}, ["ONF"], ["IDN"])
+    io(T.BCI[:], [[16, 16]], 15, 0, ["BCI"], False); cp(T.BC[:], T.BCI[:], ["BCI"], ["BC"])
+    for w in sorted(set(sum(CH, []))): io(T.CV[0:1, 3 * w // 16:6 * w // 16], [[0, 3], [256, w // 16]], 0, 0, ["CV%d" % w])
+
+    ts(T.BYI[:], T.IW[:, 0:256], w15, None, AL.mult, None, ["IW0", "PWa"], ["BYI"])
     ts(T.BYI[:], T.BYI[:], 32768, None, AL.bitwise_and, None, ["BYI"], ["BYI"])
     ts(T.BYB[:], T.BYI[:], 0.0, None, AL.is_gt, None, ["BYI"], ["BYB"])
-    for q in range(4):
-        pb = "ps%d" % (3 + q)
-        for u in range(2): mm(T[pb][:, 256 * u:256 * u + 256], [(LB("LUT%d" % (2 * q + u)), T.BYB[:])], B0 + ["BYB"], [pb])
-        fcp(T.W0[:, 512 * q:512 * q + 512], T[pb][:], [pb], ["LUT%d" % q])
-    io(T.NI[:], [[0, 2], [256, 8], [0, 16]], 0, 0, ["NI"], False)
-    ts(T.TM[:, 80:81], p16, 17.0, None, AL.mult, None, ["PF"], ["TM80"]); ts(T.TM[:, 81:82], lc, 85.0, None, AL.mult, None, ["PF"], ["TM81"])
-    for u in range(2):
-        ts(T.NL[:, 128 * u:128 * u + 128], T.NI[:, 128 * u:128 * u + 128], T.TM[:, 80 + u:81 + u], None, AL.add, None, ["NI", "TM%d" % (80 + u)], ["NL%d" % u])
-        for x in range(2):
-            fcp(T.W0[:, 2048 * (u + 1) + 1024 * x:2048 * (u + 1) + 1024 * (x + 1)], T.W0[:, 0:2048].indirect(T.NL[:, 128 * u + 64 * x:128 * u + 64 * (x + 1)]),
-                ["NL%d" % u] + ["LUT%d" % q for q in range(4)], ["LUT%d" % (4 + 2 * u + x)], GC)
-    LUT0 = ["LUT%d" % q for q in range(8)]
-    dma("s", [(T.W1[:, 0:LUTW], T.W0[:, 0:LUTW])], LUT0, ["LUTc"], 10.0)
+    for q in range(7):
+        pb = tile()
+        for u in range(2): mm([(ps(pb, 256 * u, 256 * u + 256), LB("LUT%d" % (2 * q + u)), T.BYB[:])], B0 + ["BYB"], [pb])
+        fcp(T.W0[:, 512 * q:512 * q + 512], ps(pb, 0, 512), [pb], ["LUT%d" % q])
+    LUT0 = ["LUT%d" % q for q in range(7)]
+    dma("s", [(T.W1[:, 0:LUTW], T.W0[:, 0:LUTW])], LUT0, ["LUTc"], 8.0)
 
-    FULL = [0, 1, 4, 5, 8, 9, 2, 6, 10]
-    rot = {}
-    BAS, BC_, BE = ((1, 2, 3, 4, 5, 6, 0), (1, 2, 0, 5, 6)), (3, 4), (5, 6, 0, 1, 2)
+    def groups(n, w): return [list(range(a, min(n, a + 512 // w))) for a in range(0, n, 512 // w)]
 
-    def bank(lst):
-        rot[lst] = rot.get(lst, -1) + 1
-        return "ps%d" % lst[rot[lst] % len(lst)]
+    def chunk(r, v0, w):
+        bl, nb, ns = list(range(v0 // 128, (v0 + w) // 128)), w // 128, w // 16
 
-    def blk(buf, x, n=1): return buf[:, x * w:(x + n) * w]
+        def t_(n, x=0): return ["%s%d_%d" % (n, x, b) for b in bl]
 
-    def tk(n, xs): return ["%s_%d" % (n, x) for x in xs]
+        def ts_(n, xs): return sum([t_(n, x) for x in xs], [])
 
-    def stage_a(r, h):
-        Gw, v0, SG, NE, RR, BA = T["Gw%d" % r], h * w, T.SG, T.NE, T.RR, BAS[h]
-        Ga, Gn, Gb, Pa, Pb = [blk(T["GG%d" % h], x) for x in range(5)]
-        ga, gn, gb, pa, pb_ = ["G%d_%d" % (x, h) for x in range(5)]
-        gw = ["Gw%d_%d" % (r, x) for x in range(NCH)] + ["Gw%dr" % r, "fanU"]
-        fcp(Ga, Gw[:].indirect(T.fanU[:, v0 // 16:(v0 + w) // 16]), gw, [ga], GC)
-        faff(Gb, Gw[:].indirect(T.fanU[:, (V + v0) // 16:(V + v0 + w) // 16]), -1.0, 0.0, gw, [gb], GC)
-        ts(Pb, Gb, -2048.0, 2048.0, AL.is_le, AL.mult, [gb], [pb_], 0.5)
-        tt(Gn, Gb, Pb, AL.subtract, [gb, pb_], [gn])
-        ts(Pa, Ga, 2048.0, 2048.0, AL.is_ge, AL.mult, [ga], [pa], 0.5)
-        for b0 in range(0, 11, 2):
-            bs, pb = list(range(b0, min(11, b0 + 2))), bank(BA)
-            for u, bl in enumerate(bs):
-                l = ("SA%d" % (FULL[bl] >> 2), "SB%d" % (FULL[bl] & 3)) if bl < 9 else (("COL", "RID") if bl == 9 else ("RID", "COL"))
-                mm(blk(T[pb], u), [(LF(l[0]), Ga), (LF(l[1]), Gn)], F0 + [ga, gn], [pb])
-            fsign(blk(SG, b0, len(bs)), blk(T[pb], 0, len(bs)), [pb], tk("SG", bs))
-            fne(blk(NE, b0, len(bs)), blk(SG, b0, len(bs)), tk("SG", bs), tk("NE", bs))
-        pb = bank(BA)
-        mm(blk(T[pb], 0), [(LF("XC", 2), T.Gc[:, v0:v0 + w]), (LF("XC"), T.Gc[:, V + v0:V + v0 + w]), (LF("XL", 2), Ga), (LF("XLn"), Gn),
-                           (LF("XP", 2), Pa), (LF("XP"), Pb)], F1 + ["Gc", ga, gn, pa, pb_], [pb])
-        frelu(T.XX[:], blk(T[pb], 0), vc("bX"), [pb, V0], ["XX"])
-        src = [[0, 1], [2, 3], [4, 5], [6, 7], [8], [9], [10]]
-        for grp, bi in [([0, 1], vc("bR")), ([2, 3], vc("bR")), ([4], T.PM[:, 3:4]), ([5, 6], 3.0)]:
-            pb = bank(BA)
-            for u, t in enumerate(grp):
-                pr = []
-                for n, x in enumerate(src[t]):
-                    l = (LB("Zs", 8 - 8 * n), LB("Ze", 8 - 8 * n)) if x < 9 else (LB("T%ds" % (x - 8)), LB("Te"))
-                    pr += [(l[0], blk(SG, x)), (l[1], blk(NE, x))]
-                mm(blk(T[pb], u), pr, B1 + tk("SG", src[t]) + tk("NE", src[t]), [pb])
-            frelu(blk(RR, grp[0], len(grp)), blk(T[pb], 0, len(grp)), bi, [pb, V0, "PM3"], tk("RR", grp))
-        for u, (x, P) in enumerate((("a", Pa), ("b", Pb))):
-            m1, pb = x.upper() + "1", bank(BA)
-            l = [LB(m1, 14), LB(m1, 10), LB(m1, 6), LB(x.upper() + "4"), LB(m1, 4), LB("T1" + x), LB("T2" + x)]
-            mms(blk(T[pb], 0), [([(LF("X" + x.upper()), T.XX[:]), (LF("P%s3" % x.upper()), P)] * (k == 0) + [(l[t], blk(RR, t)) for t in grp],
-                                 B1 + F1 + tk("RR", grp) + ["XX", pa, pb_]) for k, grp in enumerate((range(4), range(4, 7)))], [pb])
-            ts(blk(T["IX%d" % h], u), blk(T[pb], 0), vc("bI" + x), float(WW - 1), AL.add, AL.min, [pb, V0], ["IX%d_%d" % (h, u)])
-        pb = bank(BA)
-        mm(blk(T[pb], 0), [(LF("VPa"), Pa), (LF("VPb"), Pb)] + [(LB("Zp1", 15 - FULL[x]), blk(NE, x)) for x in range(9)] +
-           [(LB("VT1"), blk(NE, 9)), (LB("VT2"), blk(NE, 10))], B1 + F1 + tk("NE", range(11)) + [pa, pb_], [pb])
-        frelu(T["VD%d" % h][:], blk(T[pb], 0), vc("bVoid"), [pb, V0], ["VD%d" % h])
-        AB = T["AB%d" % h]
-        for i0 in (0, 2):
-            pb = bank(BA)
-            for u in range(2): mm(blk(T[pb], u), [(LF("SEL%d" % (i0 + u), 4), Ga), (LF("SEL%d" % (i0 + u)), Gn)], F2 + [ga, gn], [pb])
-            fcp(blk(AB, i0, 2 - i0 // 2), blk(T[pb], 0, 2 - i0 // 2), [pb], ["AB%d_%d" % (h, i0)])
-        faff(blk(AB, 3), blk(T[pb], 1), 1.0, vc("bAB3"), [pb, V1], ["AB%d_3" % h])
+        def blk(buf, k, x, n=1): return buf[:, k * v0 + x * w:k * v0 + (x + n) * w]
 
-    def stage_b(r, h):
-        Wt, IX, AN = T["W%d" % r], T["IX%d" % h], T["AN%d" % h]
-        wt = ["W%d_%d_%d" % (r, x, c) for x in range(NCH) for c in range(3)] + ["W%dr" % r] + (LUT0 if r == 0 else ["LUTc"])
-        for u in range(w // GW):
-            s = slice(16 * GW * u, 16 * GW * (u + 1))
-            ac(T.AG[:, s], Wt[:].indirect(IX[:, GW * u:GW * (u + 1)]), wt + ["IX%d_0" % h], ["AG_%d" % u])
-            tt(AN[:, s], Wt[:].indirect(IX[:, w + GW * u:w + GW * (u + 1)]), T.AG[:, s], AL.mult, wt + ["IX%d_1" % h, "AG_%d" % u], ["AN%d_%d" % (h, u)], GC)
-        for c0 in range(0, w, WB):
-            for u, (zm, bi) in enumerate((("Zc2", 4095.0), ("Zc1", sum(WC1) + 4096.0))):
-                pb = bank(BC_)
-                mm(T[pb][:, 0:WB], [(LB("IV"), T["VD%d" % h][:, c0:c0 + WB])] + [(LB(zm, 15 - q), AN[:, 16 * c0 + q:16 * (c0 + WB):16]) for q in range(16)],
-                   B2 + tk("AN%d" % h, range(c0 // GW, (c0 + WB) // GW)) + ["VD%d" % h], [pb])
-                ts(IX[:, (2 + u) * w + c0:(2 + u) * w + c0 + WB], T[pb][:, 0:WB], bi, float(VOID), AL.add, AL.min, [pb], ["CX%d_%d_%d" % (h, u, c0 // WB)])
+        def sub(buf, k, x, b): return buf[:, k * v0 + x * w + 128 * b:k * v0 + x * w + 128 * (b + 1)]
+        Gw, Wt, Wn = T["Gw%d" % r], T["W%d" % r], T["W%d" % (1 - r)]
+        Ga, Gb, Pa, Pb = blk(T.GG, 2, 0), blk(T.GG, 2, 1), blk(T.PP, 2, 0), blk(T.PP, 2, 1)
+        ga, gb, pp = t_("GG", 0), t_("GG", 1), t_("PP")
+        gws = range(w // GW)
 
-    def stage_c(r, h):
-        IX, v0, XM, xm = T["IX%d" % h], h * w, T.XM, tk("XM", range(16))
-        for u in range(w // GW):
-            s = slice(16 * GW * u, 16 * GW * (u + 1))
-            ac(T.CG[:, s], T.CE[:].indirect(IX[:, 2 * w + GW * u:2 * w + GW * (u + 1)]), ["CEa", "CEb", "CX%d_0_%d" % (h, u * GW // WB)], ["CG_%d" % u])
-            tt(XM[:, s], T.CE[:].indirect(IX[:, 3 * w + GW * u:3 * w + GW * (u + 1)]), T.CG[:, s], AL.min,
-               ["CEa", "CEb", "CX%d_1_%d" % (h, u * GW // WB), "CG_%d" % u] + xm, ["XG_%d" % u], GC)
-        for q in range(16): tt(XM[:, q::16], XM[:, q::16], T.ps7[:, v0:v0 + w], AL.max, ["ps7"] + tk("XG", range(w // GW)), [xm[q]], 1.0)
-        pb = bank(BC_)
-        mms(blk(T[pb], 0), [([(T.KC[0:2, :], T.ON[0:2, 0:w]), (LB("ONE"), T.RQ[:, v0:v0 + w])] * (q0 == 0) +
-            [(LB("Zm1", 15 - q), XM[:, q::16]) for q in range(q0, q0 + QS)],
-            B2 + ["KC", "ON", "RQ"] + xm[q0:q0 + QS] + tk("XG", range(w // GW))) for q0 in range(0, 16, QS)], [pb])
-        tr(blk(T.NK, 0), blk(T[pb], 0), [pb], ["NK_0"])
+        def stage_a():
+            gw = tk("Gw%d" % r, range(4)) + ["Gw%dr" % r, "fanU"]
+            ts(Ga, Gw[:].indirect(T.fanU[:, v0 // 16:(v0 + w) // 16]), MG * r, vc("dcol"), AL.subtract, AL.max, gw + vt("dcol"), ga, GC)
+            faff(Gb, Gw[:].indirect(T.fanU[:, (V + v0) // 16:(V + v0 + w) // 16]), 1.0, -MG * r, gw, gb, GC)
+            ts(blk(T.PP, 2, 0, 2), blk(T.GG, 2, 0, 2), 0.5, None, AL.is_ge, None, ga + gb, pp, 0.5)
+            for bs in groups(11, w):
+                pb = tile()
+                for u, x in enumerate(bs):
+                    l = ("SA%d" % SI[FULL[x]], "SB%d" % SJ[FULL[x]]) if x < 9 else (("I13", "R13") if x == 9 else ("R12", "I12"))
+                    o = ps(pb, u * w, u * w + w)
+                    mm([(o, LF(l[0]), Ga), (o, LF(l[1]), Gb)], F0 + ga + gb, [pb])
+                sign(blk(T.SG, 11, bs[0], len(bs)), ps(pb, 0, len(bs) * w), [pb], ts_("SG", bs))
+                fne(blk(T.NE, 11, bs[0], len(bs)), blk(T.SG, 11, bs[0], len(bs)), ts_("SG", bs), ts_("NE", bs))
+            pb = tile()
+            o = ps(pb, 0, w)
+            mm([(o, LF("XC", 2), T.Gc[:, v0:v0 + w]), (o, LF("XC"), T.Gc[:, V + v0:V + v0 + w]), (o, LF("XL", 2), Ga), (o, LF("XL"), Gb),
+                (o, LF("XP", 2), Pa), (o, LF("XP"), Pb)], F1 + ["Gc"] + ga + gb + pp, [pb])
+            frelu(blk(T.XX, 1, 0), o, vc("bX"), [pb] + vt("bX"), t_("XX"))
+            W2, W9, pv = T.W2, T.W9, tile() + "v"
+            for b in range(nb):
+                pb = tile()
 
-    def stage_d(r, h):
-        NK, SC, TT, KP, LV, LU, QI, n3 = T.NK, T.SC, T.TT, T.KP[:], T.LV, T.LU, T.QI[:], 3 * NS
-        nk, sc, tn = [tk(n, range(3)) for n in ("NK", "SC", "TT")]
-        for c in range(3):
-            scan(blk(SC, c), T.RST[:, 0:w], blk(NK, c), 0.0, AL.mult, AL.max, ["RST", nk[c]], [sc[c]])
-            ts(TT[:, c * NS:(c + 1) * NS], SC[:, c * w + 15:(c + 1) * w:16], -0.53125, None, AL.add, None, [sc[c]], [tn[c]])
-            if c < 2:
-                tt(KP, TT[:, c * NS:(c + 1) * NS].indirect(T.BC[:, 0:NS]), blk(NK, c), AL.is_ge, [tn[c], "BC", nk[c]], ["KP"], GC)
-                tt(blk(NK, c + 1), KP, blk(NK, c), AL.mult, ["KP", nk[c]], [nk[c + 1]])
-        M, Q, q, lv = SC[:, 15::16], [T.Q[:, n * n3:(n + 1) * n3] for n in range(7)], tk("Q", range(8)), tk("LV", range(3))
-        tt(Q[0], TT[:], M, AL.subtract, sc + tn, [q[0]])
-        ts(Q[1], M, 0.0, 8192.0, AL.is_le, AL.mult, sc, [q[1]])
-        ts(QI, Q[0], 4.0, 3.625, AL.mult, AL.add, [q[0]], [q[7]])
-        tt(Q[2], Q[1], T.VNN[:], AL.add, [q[1], "VNN"], [q[2]])
-        ts(Q[3], Q[0], 16.0 * w, 16.0 * w, AL.mult, AL.add, [q[0]], [q[3]])
-        tt(Q[4], Q[0], Q[2], AL.add, [q[0], q[2]], [q[4]])
-        ts(Q[5], QI, float(w), None, AL.mult, None, [q[7]], [q[5]])
-        ts(Q[6], QI, -4.0 * w, None, AL.mult, None, [q[7]], [q[6]])
-        tt(Q[3], Q[3], Q[2], AL.add, [q[3], q[2]], [q[3]])
-        ts(LV[:, 2 * n3:], Q[4], 16.0, 16.0, AL.mult, AL.add, [q[4]], [lv[2]])
-        tt(LV[:, 0:n3], Q[5], Q[2], AL.add, [q[5], q[2]], [lv[0]])
-        tt(LV[:, n3:2 * n3], Q[6], Q[3], AL.add, [q[6], q[3]], [lv[1]])
-        pb = bank(BE)
-        for h1 in range(2):
-            mm(T[pb][:, h1:3 * n3:2], [(T.SW[:, (2 * h1 + x) * 128:(2 * h1 + x + 1) * 128], LV[:, x::2]) for x in range(2)],
-               lv + ["SW%d" % x for x in range(4)], [pb], 4)
-        ts(LU[:, 0:2 * n3], T[pb][:, 0:2 * n3], 4.0 * w, None, AL.min, None, [pb], ["LU"])
-        ts(LU[:, 2 * n3:], T[pb][:, 2 * n3:3 * n3], 16.0 * w, None, AL.min, None, [pb], ["LW"])
-        if r == 1:
-            ts(Q[5], TT[:], -1.0, 524287.0, AL.mult, AL.add, tn, [q[5]])
-            ts(Q[6], M, 0.0, -524289.0, AL.is_le, AL.mult, sc, [q[6]])
+                def sg(x): return sub(T.SG, 11, x, b)
+
+                def ne(x): return sub(T.NE, 11, x, b)
+                parts = [([(ps(pb, 0, 512), sub(T.PP, 2, 0, b), T.PA[:]), (ps(pb, 256, 512), sub(T.PP, 2, 1, b), T.PB[:])], [])]
+                for xs in ((0, 1, 2, 3), (4, 5, 6, 7), (8,)):
+                    parts.append((sum([[(ps(pb, FULL[x], 512, 16), sg(x), W2[:, 0:32]), (ps(pb, FULL[x], 512, 16), ne(x), W2[:, 32:64])] for x in xs], []), xs))
+                for x, own, oth in ((9, ps(pb, 3, 256, 4), ps(pb, 259, 384, 4)), (10, ps(pb, 258, 512, 4), ps(pb, 2, 128, 4))):
+                    parts[-1] = (parts[-1][0] + [(own, sg(x), W9[:, 0:64]), (oth, sg(x), W9[:, 64:96]), (own, ne(x), W9[:, 96:160]),
+                                                 (oth, ne(x), W9[:, 160:192])], parts[-1][1] + (x,))
+                parts = [(parts[0][0] + parts[1][0], parts[1][1])] + parts[2:]
+                for n, (tr, xs) in enumerate(parts): mm(tr, WT + pp + ts_("SG", xs) + ts_("NE", xs), [pb], n == 0, n == len(parts) - 1)
+                frelu(T.XT[:, 512 * bl[b]:512 * bl[b] + 512], ps(pb, 0, 512), 0.0, [pb], ["XT_%d" % bl[b]])
+                a0 = 128 * b
+                mm([(ps(pv, a0, a0 + 128), sub(T.PP, 2, 0, b), T.PAV[:]), (ps(pv, a0, a0 + 128), sub(T.PP, 2, 1, b), T.PBV[:])] +
+                   [(ps(pv, a0 + FULL[x], a0 + 128, 16), ne(x), W2[:, 64:72]) for x in range(9)] +
+                   [(ps(pv, a0 + 12 - x, a0 + 128, 4), ne(x), W9[:, 192:224]) for x in (9, 10)], WT + pp + ts_("NE", range(11)), [pv])
+            frelu(blk(T.VT, 1, 0), ps(pv, 0, w), -4.0, [pv], t_("VT"))
+            pb = tile()
+            for u, x in enumerate("AB"):
+                mm([(ps(pb, u * w, u * w + w), LF("X" + x), blk(T.XX, 1, 0))] +
+                   [(ps(pb, u * w + 128 * b, u * w + 128 * b + 128), T.XT[:, 512 * bl[b] + 128 * y:512 * bl[b] + 128 * y + 128], LF("I256"))
+                    for b in range(nb) for y in (2 * u, 2 * u + 1)], F1 + t_("XX") + tk("XT", bl), [pb])
+            ts(blk(T.IX, 2, 0, 2), ps(pb, 0, 2 * w), float(WW - 1), None, AL.min, None, [pb], t_("IX"))
+
+        def big(u): return slice(16 * (v0 + GW * u), 16 * (v0 + GW * (u + 1)))
+
+        def gt(n, us): return ["%s_%d" % (n, v0 // GW + u) for u in us]
+
+        def stage_b():
+            wt = tk("W%d" % r, range(12)) + ["W%dr" % r] + (LUT0 if r == 0 else ["LUTc"])
+            for u in gws:
+                a0 = 2 * v0 + GW * u
+                ac(T.AG[:, big(u)], Wt[:].indirect(T.IX[:, a0:a0 + GW]), wt + t_("IX"), gt("AG", [u]) + ts_("XM", P16), cy=GC)
+                tt(T.AN[:, big(u)], Wt[:].indirect(T.IX[:, a0 + w:a0 + w + GW]), T.AG[:, big(u)], AL.mult, wt + t_("IX") + gt("AG", [u]), gt("AN", [u]), GC)
+            for b in range(nb):
+                a0, us = 16 * (v0 + 128 * b), range(128 * b // GW, 128 * (b + 1) // GW)
+                for u, (zm, bi) in enumerate((("Zc2", 4095.0 + CE0), ("Zc1", sum(WC1) + float(CE0)))):
+                    pb = tile()
+                    mm([(ps(pb, 0, 128), LB(zm, 15 - q), T.AN[:, a0 + q:a0 + 2048:16]) for q in P16], B1 + gt("AN", us), [pb])
+                    ts(sub(T.CX, 2, u, b), ps(pb, 0, 128), bi, None, AL.add, None, [pb], ["CX%d_%d" % (u, bl[b])])
+        key = []
+
+        def stage_c():
+            for u in gws:
+                a0, b = 2 * v0 + GW * u, (v0 + GW * u) // 128
+                ac(T.AG[:, big(u)], T.CE[:].indirect(T.CX[:, a0:a0 + GW]), ["CE", "CX0_%d" % b], gt("AG", [u]), cy=GC)
+                tt(T.XG[:, big(u)], T.CE[:].indirect(T.CX[:, a0 + w:a0 + w + GW]), T.AG[:, big(u)], AL.min,
+                   ["CE", "CX1_%d" % b] + gt("AG", [u]), gt("XG", [u]), GC)
+            for q in P16:
+                tt(blk(T.AG, 16, q), T.XG[:, 16 * v0 + q:16 * (v0 + w):16], ps("rq", v0, v0 + w), AL.max, ["rq"] + gt("XG", gws), t_("XM", q), 1.0)
+            pb = tile()
+            key.append(pb)
+            for b in range(nb):
+                a0 = 128 * b
+                o = ps(pb, a0, a0 + 128)
+                for q0 in range(0, 16, QS):
+                    mm([(o, T.RQ[:, v0 + a0:v0 + a0 + 128], LB("ONE")), (o, LB("IV"), sub(T.VT, 1, 0, b))] * (q0 == 0) +
+                       [(ps(pb, a0 + q, a0 + 128, 16), sub(T.AG, 16, q, b), T.GN[:]) for q in range(q0, q0 + QS)] +
+                       [(o, T.ON[:], LB("KC"))] * (q0 + QS == 16),
+                       B1 + ["GN", "ON", "RQ"] + t_("VT") + ts_("XM", range(q0, q0 + QS)), [pb], q0 == 0, q0 + QS == 16)
+
+        def stage_d():
+            pb = key[0]
+            K, K0, K1, bc = ps(pb, 0, w), blk(T.NK0, 1, 0), blk(T.NK1, 1, 0), T.BC[:, 0:ns]
+            ac(K0, K, [pb], t_("NK0"))
+            ac(K1, K0, t_("NK0"), t_("NK1"), AF.Identity, 0.5)
             for c in range(3):
-                a0 = c * NS
-                tt(T.CB[:, c::16], T.Q[:, 5 * n3 + a0:5 * n3 + a0 + NS], T.Q[:, 6 * n3 + a0:6 * n3 + a0 + NS], AL.add, [q[5], q[6]], ["CB"])
-            tr(blk(T.YC, h), T.CB[:], ["CB"], ["YC%d" % h])
+                sc = blk(T.SC, 3, c)
+                scan(sc, T.RST[:, 0:w], blk(T.NKN, 2, c - 1) if c else K, 0.0, AL.mult, AL.max, ["RST"] + (t_("NKN", c - 1) if c else [pb]), t_("SC", c))
+                if c < 2:
+                    tt(blk(T.KP, 2, c), sc.indirect(bc), K1, AL.is_gt, t_("SC", c) + t_("NK1") + ["BC"], t_("KP", c), GC)
+                    tt(blk(T.NKN, 2, c), blk(T.KP, 2, c), K, AL.mult, t_("KP", c) + [pb], t_("NKN", c), 1.0)
+                tt(blk(T.MT, 3, c), sc.indirect(bc), K0, AL.is_equal, t_("SC", c) + t_("NK0") + ["BC"], t_("MT", c), GC)
+            for cs in groups(3, w):
+                pb = tile()
+                for u, c in enumerate(cs):
+                    for b in range(nb): mm([(ps(pb, u * w + 128 * b, u * w + 128 * b + 128), sub(T.MT, 3, c, b), LF("I256"))], F1 + t_("MT", c), [pb])
+                fcp(blk(T.MK, 3, cs[0], len(cs)), ps(pb, 0, len(cs) * w), [pb], ts_("MK", cs))
+            pb = tile()
+            o = ps(pb, 0, 3 * ns)
+            mm([(o, T.ONH[0:1, :], T.CV[0:1, 3 * ns:6 * ns])] + [(o, LF("LP", 15 - x), T.MK[:, 3 * v0 + x:3 * (v0 + w):16]) for x in P16],
+               F2 + ["ONH", "CV%d" % w] + ts_("MK", range(3)), [pb])
+            ts(T.LU[:, 3 * v0 // 16:3 * (v0 + w) // 16], o, vc("p256"), None, AL.add, None, [pb] + vt("p256"), t_("LU"))
+            if r == 1:
+                M, s, n = T.SC[:, 3 * v0 + 15:3 * (v0 + w):16], slice(3 * v0 // 16, 3 * (v0 + w) // 16), 3 * ns
+                ts(T.TT[:, s], M, 0.25, None, AL.add, None, ts_("SC", range(3)), t_("TT"))
+                ts(T.Q6[:, s], M, 0.0, -524288.0, AL.is_le, AL.mult, ts_("SC", range(3)), t_("Q6"))
+                ts(T.Q5[:, s], T.TT[:, s], -1.0, 524287.0, AL.mult, AL.add, t_("TT"), t_("Q5"))
+                tt(T.Q5[:, s], T.Q5[:, s], T.Q6[:, s], AL.add, t_("Q5") + t_("Q6"), t_("Q5"))
+                pb = tile()
+                mm([(ps(pb, 0, 128, 1, n), T.Q5[:, s], T.IDN[:])], t_("Q5") + ["IDN"], [pb], k=4)
+                fcp(T.YC[0:n, v0:v0 + 128], ps(pb, 0, 128, 1, n), [pb], t_("YC"))
+                dma("s", [(T.yc[:, c * V + 128 * bl[b]:c * V + 128 * bl[b] + 128], T.YC[8 * (c * nb + b):8 * (c * nb + b) + 8, v0:v0 + 128])
+                          for c in range(3) for b in range(nb)], t_("YC"), [])
 
-    def stage_e(r, h):
-        v0, AB, Wn, LU, CA, CN, S2, E2, HH = h * w, T["AB%d" % h], (T.WF if r else T.W1), T.LU, T.CA, T.CN, T.S2, T.E2, T.HH
-        n3, (w0, w1) = 3 * NS, ((0, V) if r else (LUTW, WN))
-        ab = tk("AB%d" % h, (0, 2, 3)) + ["ABp%d" % h, "LU"]
-        fcp(CA[:], AB[:].indirect(LU[:, 0:n3]), ab, ["CA"], GC)
-        fcp(CN[:], AB[:].indirect(LU[:, n3:2 * n3]), ab, ["CN"], GC)
-        wn = ["W%d_%d_%d" % (1 + r, h, c) for c in range(3)]
-        for c in range(3):
-            o = w0 + w1 * c + v0
-            faff(Wn[:, o:o + w], T["AN%d" % h][:].indirect(LU[:, 2 * n3 + c * NS:2 * n3 + (c + 1) * NS]), -1.0, 1.0,
-                 tk("AN%d" % h, range(w // GW)) + ["ANp%d" % h, "LW"], [wn[c]], GC)
-        if r == 0 and h == 0: send_b(1)
-        for a0, n in ((0, 512), (512, 256)):
-            s, y, pb = slice(a0, a0 + n), str(a0), bank(BE)
-            mm(T[pb][:, 0:n], [(LF("SA0"), CA[:, s]), (LF("SB1"), CN[:, s])], F0 + ["CA", "CN"], [pb])
-            fsign(S2[:, s], T[pb][:, 0:n], [pb], ["S2" + y]); fne(E2[:, s], S2[:, s], ["S2" + y], ["E2" + y])
-            pb = bank(BE)
-            mms(T[pb][:, 0:n], [([(LB("BH"), T.ON[:, 0:n]), (LF("HA"), CA[:, s]), (LF("HB"), CN[:, s])], F2 + B2 + ["ON", "CA", "CN"]),
-                                ([(LB("Hs"), S2[:, s])], ["S2" + y]), ([(LB("He"), E2[:, s])], ["E2" + y])], [pb])
-            ts(HH[:, s], T[pb][:, 0:n], 0.0, 4096.0, AL.max, AL.min, [pb], ["HH" + y])
-        pb, pr = bank(BE), [(LF("E12"), T.IDf[:, v0:v0 + w])]
-        for c in range(3):
-            o = w0 + w1 * c + v0
-            pr += [(LB("ZT" if r else "Zlb", 2 - c), Wn[:, o:o + w]), (LF("UA", 8 - 4 * c), blk(CA, c))]
-        mms(blk(T[pb], 0), [(pr, F2 + B2 + ["IDf", "CA"] + wn), ([(LF("UH", 8 - 4 * c), blk(HH, c)) for c in range(3)], ["HH0", "HH512"])], [pb])
-        if r == 0:
-            faff(blk(T.Gw1, h), blk(T[pb], 0), 1.0, vc("bU"), [pb, V1], ["Gw1_%d" % h])
-            if h == 0: send_g(1)
-        else:
-            Y = blk(T.Y, h)
-            faff(Y, blk(T[pb], 0), 1.0, vc("bU"), [pb, V1], ["Y%d" % h])
-            ts(T.YP[:], Y, vc("thr"), -2049.0, AL.is_ge, AL.mult, ["Y%d" % h, V1], ["YP"])
-            tt(Y, Y, T.YP[:], AL.add, ["Y%d" % h, "YP"], ["Y%d" % h])
+        def stage_e():
+            wn = [tk("W%d" % (1 - r), [3 * b + c for b in bl]) for c in range(3)]
+            bits = [Wn[:, LUTW + WN * c + v0:LUTW + WN * c + v0 + w] for c in range(3)]
+            for c in range(3):
+                a0 = 3 * v0 // 16 + c * ns
+                faff(bits[c], T.AN[:, 16 * v0:16 * (v0 + w)].indirect(T.LU[:, a0:a0 + ns]), -1.0, 1.0, gt("AN", gws) + t_("LU"), wn[c], GC)
+            if r == 0 and v0 + w == BORD: send_b(1)
+            for cs in groups(3, w):
+                c0, n = cs[0], len(cs)
+                for R, G, gk, x in ((T.RA, Ga, ga, "a"), (T.RB, Gb, gb, "b")):
+                    pb = tile()
+                    for u, c in enumerate(cs):
+                        o = ps(pb, u * w, u * w + w)
+                        mm([(o, LF("J13"), G), (o, LF("RM" + x), blk(T.MK, 3, c))], F2 + gk + t_("MK", c), [pb])
+                    frelu(blk(R, 3, c0, n), ps(pb, 0, n * w), vc("bR" + x), [pb] + vt("bR" + x), ts_("R" + x, cs))
+                ra, rb, s2, e2, rk = blk(T.RA, 3, c0, n), blk(T.RB, 3, c0, n), blk(T.S2, 3, c0, n), blk(T.E2, 3, c0, n), F2 + ts_("Ra", cs) + ts_("Rb", cs)
+                pb = tile()
+                o = ps(pb, 0, n * w)
+                mm([(o, LF("EA"), ra), (o, LF("EB"), rb)], rk, [pb])
+                sign(s2, o, [pb], ts_("S2", cs)); fne(e2, s2, ts_("S2", cs), ts_("E2", cs))
+                pb = tile()
+                o = ps(pb, 0, n * w)
+                mm([(o, LF("HA"), ra), (o, LF("HB"), rb), (o, LF("Hs"), s2)], rk + ts_("S2", cs), [pb], True, False)
+                mm([(o, LF("He"), e2)], ts_("E2", cs), [pb], False, True)
+                ts(blk(T.HH, 3, c0, n), o, 0.0, 4096.0, AL.max, AL.min, [pb], ts_("HH", cs))
+            pb = tile()
+            o = ps(pb, 0, w)
+            pr = [] if r else [(o, LF("E12"), blk(T.IDf, 1, 0))]
+            for c in range(3):
+                pr += [(o, LB("ZT" if r else "Zlb", 2 - c), bits[c]), (o, LF("UA", 8 - 4 * c), blk(T.RA, 3, c))] + [(o, LF("UE", 2 - c), blk(T.RB, 3, c))] * r
+            mm(pr + [(o, LF("UH", 8 - 4 * c), blk(T.HH, 3, c)) for c in range(3)],
+               F2 + B1 + ["IDf"] + ts_("Ra", range(3)) + ts_("Rb", range(3)) + sum(wn, []) + ts_("HH", range(3)), [pb])
+            ops[-1]["b"] = AHEAD * (V - v0 - w)
+            if r == 0:
+                faff(blk(T.Gw1, 1, 0), o, 1.0, vc("bM"), [pb] + vt("bM"), tk("Gw1", bl))
+                if v0 + w == BORD: send_g(1)
+            else:
+                Y, YP, y = blk(T.Y, 1, 0), blk(T.YP, 1, 0), t_("Y")
+                add({"a": aac(Y, o, AF.Relu, vc("bY"), vc("sY"))}, [pb] + vt("bY", "sY"), y)
+                ts(YP, Y, vc("thr"), -2049.0, AL.is_ge, AL.mult, y + vt("thr"), t_("YP"))
+                ts(Y, Y, MG, MG, AL.add, AL.subtract, y, y)
+                tt(Y, Y, YP, AL.add, y + t_("YP"), y)
+                if v0 + w in (V - CH[1][-1], V):
+                    a0 = 0 if v0 + w < V else v0
+                    ys, a1 = ["Y0_%d" % b for b in range(a0 // 128, (v0 + w) // 128)], v0 + w
+                    prs = [(T.yl[:, f * V + a0:f * V + a1], T.Y[f::16, a0:a1]) for f in range(12)] + \
+                          [(T.yt[:, c * V + a0:c * V + a1], T.Y[13 + c::16, a0:a1]) for c in range(3)]
+                    if a1 < V: dma("s", prs, ys, [])
+                    else: dma("s", prs[:8], ys, []); dma("a", prs[8:], ys, [])
+        return [stage_a, stage_b, stage_c, stage_d, stage_e]
     for r in range(2):
-        for s in range(NCH + 3):
-            for k, sts in ((3, (stage_d, stage_e)), (2, (stage_c,)), (1, (stage_b,)), (0, (stage_a,))):
-                if 0 <= s - k < NCH:
-                    for st in sts: st(r, s - k)
-    ys = ["Y%d" % h for h in range(NCH)]
-    dma("s", [(T.yc[:, c * V:(c + 1) * V], T.YC[c::16, :]) for c in range(3)], ["YC%d" % h for h in range(NCH)], [])
-    dma("s", [(T.yl[:, f * V:(f + 1) * V], T.Y[f::16, :]) for f in range(8)], ys, [])
-    dma("a", [(T.yl[:, f * V:(f + 1) * V], T.Y[f::16, :]) for f in range(8, 12)] +
-        [(T.yt[:, c * V:(c + 1) * V], T.Y[13 + c::16, :]) for c in range(3)], ys, [])
+        cs = [chunk(r, sum(CH[r][:h]), CH[r][h]) for h in range(len(CH[r]))]
+        for k in range(5):
+            for st in cs: st[k]()
 
     n = len(ops)
     succ, pl, rdy = [[] for _ in range(n)], [0.0] * n, [0.0] * n
@@ -564,28 +608,41 @@ def rank_program(g, core, T, topo):
         o["dd"] = set(o["d"]) | ({o["o"]} if "o" in o else set())
         for d in o["dd"]: succ[d].append(i)
     for i in range(n - 1, -1, -1):
-        pl[i] = max(c for f, c in ops[i]["a"].values()) + ops[i]["l"] + 0.06 + max([pl[j] for j in succ[i]], default=0.0)
-    for i in range(n): pl[i] += 20.0 * (ops[i]["k"] in ("VAL", "TWO"))
+        pl[i] = min(c for f, c in ops[i]["a"].values()) + ops[i]["l"] + HOP + max([pl[j] for j in succ[i]], default=0.0) + ops[i].get("b", 0.0)
     left, free, order = [len(o["dd"]) for o in ops], {e: 0.0 for e in "atgsxv"}, []
     pool = {i for i in range(n) if left[i] == 0}
+    banks, open_ = {b: (0.0, set()) for b in range(7)}, {t: len(u) for t, u in users.items()}
+    fin = {}
+    if EST:
+        pool, order = None, EST[2]
+        bankof.update(EST[3])
+        for o, p in zip(ops, EST[1]): o.update({"e": p["e"], "d": p["d"]})
     while pool:
-        best = None
-        for i in pool:
-            al = ops[i]["a"]
-            e = min(al, key=lambda e: max(free[e], rdy[i]) + al[e][1] + (MARG if e == "v" else 0.0))
-            key = (round(max(free[e], rdy[i]), 6), -pl[i], i, e)
-            if best is None or key < best: best = key
-        t0, i, e = best[0], best[2], best[3]
-        soon = [j for j in pool if ops[j]["e"] == e and rdy[j] < t0 + 0.5 * ops[i]["a"][e][1] and pl[j] > pl[i] + 1.0]
+        bt = min([x[0] for x in banks.values()], default=None)
+        cand = [i for i in pool if ops[i]["new"] is None or bt is not None]
+        at = {i: max(rdy[i], bt) if ops[i]["new"] else rdy[i] for i in cand}
+        t0, e = min((max(free[e], at[i]), e) for i in cand for e in ops[i]["a"])
+        mine_ = [i for i in cand if e in ops[i]["a"]]
+
+        def rank_(i): return (pl[i] - (MARG if e == "v" and len(ops[i]["a"]) > 1 else 0.0), -i)
+        i = max((i for i in mine_ if at[i] <= t0 + 1e-9), key=rank_)
+        soon = [j for j in mine_ if at[j] < t0 + min(SOON, 0.5 * ops[i]["a"][e][1]) and rank_(j)[0] > rank_(i)[0] + 1.0]
         if soon:
-            i = max(soon, key=lambda j: (pl[j], j)); t0 = max(free[e], rdy[i])
+            i = max(soon, key=rank_); t0 = max(free[e], at[i])
         pool.remove(i); order.append(i)
-        ops[i].update({"e": e, "t": t0, "c": ops[i]["a"][e][1]})
-        free[e] = t0 + ops[i]["c"]
+        o = ops[i]
+        if o["new"]:
+            b = min(banks, key=lambda b: (banks[b][0], b))
+            bankof[o["new"]] = b; o["d"] = o["d"] | banks.pop(b)[1]
+        o.update({"e": e, "t": t0, "c": o["a"][e][1]})
+        free[e] = t0 + o["c"]; fin[i] = free[e] + o["l"] + HOP
+        for t in o["ps"]:
+            open_[t] -= 1
+            if open_[t] == 0: banks[bankof[t]] = (max(fin[j] for j in users[t]), users[t])
         for j in succ[i]:
-            rdy[j] = max(rdy[j], free[e] + ops[i]["l"] + 0.06); left[j] -= 1
+            rdy[j] = max(rdy[j], fin[i]); left[j] -= 1
             if left[j] == 0: pool.add(j)
-    EST[:] = [free, ops, order]
+    if not EST: EST[:] = [free, ops, order, bankof]
     qs = {"v": vec, "a": act, "t": ten, "g": g, "s": g.sync}
     cnt, seen, final = {"v": 0, "a": 0, "t": 0, "g": 0}, {}, {}
     for i in order:

@@ -4,6 +4,10 @@ from concourse.mybir import AluOpType as AL, ActivationFunctionType as AF
 
 V, NR, BORD, WN = 512, 4, 256, 1280
 CH = [[128] * 4, [128] * 4]
+NFS = [[0, 8, 8, 8], [0, 8, 8, 8]]
+NFV = [0, 8]
+RLAT, FLAT, FINE = 8.0, 9.0, True
+NHELP, HENG, LAND = 2, 8, ("AN", "XG")
 GW, QS = 64, 4
 LUTW = 14 * 256
 WW = LUTW + 3 * WN
@@ -17,7 +21,9 @@ SI = [0, 0, 3, 0, 1, 1, 3, 1, 2, 2, 3, 2, 0, 1, 2, 3]
 SJ = [0, 1, 0, 3, 0, 1, 1, 3, 0, 1, 2, 3, 2, 2, 2, 3]
 FULL = [q for q in P16 if SI[q] < 3 and SJ[q] < 3]
 PLACINGS = [7, 11, 13, 3, 14, 5, 6, 9, 10, 12, 1, 2, 4, 8]
-MARG, OVH, PEC, GC, HOP, AHEAD, SOON = 20.0, 0.06, 0.43e-3, 1.4, 0.08, 0.02, 0.3
+EARLY, LEAD = 7, 0.0
+NBANK, PASSES, MARG2, HALF, HALFA = 7, 6, 10.0, 0.0, 0.2
+MARG, OVH, PEC, GC, HOP, AHEAD, SOON = 20.0, 0.06, 0.43e-3, 1.5, 0.08, 0.01, 0.3
 
 
 def _old(s):
@@ -39,7 +45,7 @@ V8 = {"A1": A1 * 2, "A2": A2 * 2, "N1": N1 * 2, "N2": N2 * 2,
       "cBt": [9, -26, 16, 0, TRIV, 0, 0, 0], "cV": [-7, 1, 1, 1, 5, 0, 0, 0], "bU": [0, -4096, -8192, 12288, 0, 0, 0, 0]}
 V16 = {"zrow": HZ * 2 + [9] * 4, "nwc1": [-x for x in WC1]}
 V2_ = {"mul": (13, -1, 16), "off": (13, -1, 0), "sub": (13, 2047, 0), "dcol": (12, DL, 0), "bRa": (13, -4096, DL - 4096),
-       "bRb": (13, -4096, 2), "u3": (12, -1, 1), "sY": (13, -1, 1), "thr": (13, 2047.5, 70000), "tY": (13, 2048, 0)}
+       "bRb": (13, -4096, 2), "u3": (12, -1, 1), "sY": (13, -1, 1), "thr": (13, 2049, 0), "tY": (13, 2048 + MG, MG)}
 CN = list(V2_) + ["f12", "f13", "c8", "t5", "cAf", "cAt", "bX", "lo2", "hi2", "bY", "le12", "le12n", "is13", "is14", "is0", "is1", "bM",
                   "p256", "w2hi", "w2lo", "nA1", "nA2"]
 _hc = [2048 * (HZ[c] - HK[c]) + 8192 * HK[c] for c in range(6)]
@@ -53,10 +59,10 @@ PHI.update({"CK": KK, "CL": LL, "HK": HK + [N_] * 10, "HC": _hc + [x - 24576 for
 PN = list(PHI)
 FM = [["SA0", "SA1", "SA2", "SB0", "SB1", "SB2", "I13", "R13", "I12", "R12"], ["XC", "XL", "XP", "XA", "XB", "I256"],
       ["J13", "RMa", "RMb", "EA", "EB", "HA", "HB", "Hs", "He", "UH", "UA", "UE", "E12", "LP"]]
-BM = [["LUT%d" % i for i in range(14)], ["Zc1", "Zc2", "IV", "ONE", "KC", "Zlb", "ZT"]]
+BM = [["LUT%d" % i for i in range(14)], ["Zc1", "Zc2", "IV", "ID", "IDn", "KC", "Zlb", "ZT"] + ["ONE%d" % n for n in NFV]]
 FN, BN = sum(FM, []), sum(BM, [])
 f32, f16, b16, i32, u16 = "float32", "float16", "bfloat16", "int32", "uint16"
-_S = [("fanI", 64, i32), ("fanU", 64, u16), ("LI", V, i32), ("IDI", V, i32), ("TR", 3 * V, i32), ("CE", CEW, b16), ("RQ", V, b16),
+_S = [("fanI", 64, i32), ("fanU", 64, u16), ("LI", V, i32), ("IDI", V, i32), ("GNF", 8, f32), ("XF", 128 * 16, f32), ("RP", 16 * 384 if min(sum(NFS, [])) < 0 else 16, b16), ("CE", CEW, b16), ("RQ", V, b16),
       ("Gw0", WN, f32), ("Gw1", WN, f32), ("W0", WW, b16), ("W1", WW, b16), ("IW", WN, f32), ("Gc", 2 * V, f16),
       ("IDf", V, f16), ("PI", 8, i32), ("PJ", 8, i32), ("PF", 8, f32), ("GI", 32, f32), ("GM", 8, f32), ("GN", 8, b16), ("CO", len(CN), f32),
       ("VAL", 112, f32), ("OHI", 80, f32), ("OH", 176, f32), ("PR", 176, f32), ("VC", 176, f32), ("RST", 256, f32), ("RS8", 112, f32),
@@ -69,12 +75,14 @@ _S = [("fanI", 64, i32), ("fanU", 64, u16), ("LI", V, i32), ("IDI", V, i32), ("T
       ("NK0", V, f32), ("NK1", V, f32), ("NKN", 2 * V, f32), ("KP", 2 * V, f32), ("SC", 3 * V, f32), ("MT", 3 * V, f16), ("MK", 3 * V, f16),
       ("LU", 3 * V // 16, u16), ("RA", 3 * V, f16), ("RB", 3 * V, f16), ("S2", 3 * V, f16), ("E2", 3 * V, f16), ("HH", 3 * V, f16),
       ("Y", V, f32), ("YP", V, f32), ("TT", 96, i32), ("Q5", 96, f32), ("Q6", 96, f32), ("YC", V, f32)]
-SCRATCH = {n: ("sbuf", [128, k], d) for n, k, d in _S}
+RING = ("NK0", "NK1", "NKN", "KP", "MT", "RA", "RB", "S2", "E2", "HH", "YP")
+SCRATCH = {n: ("sbuf", [128, k // 2 if n in RING else k], d) for n, k, d in _S}
 SCRATCH.update({"TR": ("sbuf", [128, 3, V], i32), "PH": ("sbuf", [128, len(PN), 16], f32), "MF": ("sbuf", [128, len(FN), 16], f16), "MB": ("sbuf", [128, len(BN), 16], b16),
                 "BF": ("sbuf", [128, len(FN), 144], f16), "BB": ("sbuf", [128, len(BN), 144], b16)})
 for _b in range(8):
     SCRATCH["ps%d" % _b] = ("psum", [128, 512], f32)
-SEMAPHORES = ["sv", "sa", "st", "sg", "loc"] + ["d%d" % i for i in range(32)] + ["ar%d" % i for i in range(4)]
+SEMAPHORES = ["sv", "sa", "st", "sg", "loc", "go"] + ["d%d" % i for i in range(32)] + ["ar%d" % i for i in range(4)] + \
+    ["h%s%d_%d" % (x, r, u) for x in "fb" for r in range(2) for u in range(V // GW)]
 EST = []
 
 
@@ -107,10 +115,101 @@ COVER = {n: _cover(x) for n, x in PHI.items()}
 VCOVER = [_cover([int(x * 128) for y in list(V8.values())[:9] for x in y]), _cover(V8["bU"]), _cover(sum(V16.values(), []))]
 
 
+def _plan(ops, users):
+    n = len(ops)
+    pred = [set(o["d"]) | ({o["o"]} if "o" in o else set()) for o in ops]
+    succ, pl = [[] for _ in range(n)], [0.0] * n
+    for i in range(n):
+        for d in pred[i]: succ[d].append(i)
+    for i in range(n - 1, -1, -1):
+        pl[i] = min(c for f, c in ops[i]["a"].values()) + ops[i]["l"] + HOP + max([pl[j] for j in succ[i]], default=0.0) + ops[i].get("b", 0.0)
+
+    shy = [({"v": 1.0} if o["a"]["a"][1] < 1.4 * o["a"]["v"][1] else {"v": HALF, "a": HALFA}) if len(o["a"]) > 1 else {} for o in ops]
+
+    def forward(pr, marg):
+        left, free, order, rdy, fin = [len(x) for x in pred], {e: 0.0 for e in "atgsxv"}, [], [0.0] * n, [0.0] * n
+        eng, bank, more, early, INF = [None] * n, {}, [set() for _ in range(n)], {}, 1e9
+        pool = {i for i in range(n) if left[i] == 0}
+        banks, open_ = {b: (0.0, set()) for b in range(NBANK)}, {t: len(u) for t, u in users.items()}
+        while pool:
+            bt = min([x[0] for x in banks.values()], default=None)
+            at = {i: max(rdy[i], bt) if ops[i]["new"] else rdy[i] for i in pool if ops[i]["new"] is None or bt is not None}
+            held = sorted(early.values())
+            if len(held) >= EARLY:
+                for i in [i for i in at if ops[i]["new"] and ops[i]["new"][-1] == "a"]:
+                    if held[-EARLY] is INF: del at[i]
+                    else: at[i] = max(at[i], held[-EARLY])
+            t0, e = min((max(free[e], at[i]), e) for i in at for e in ops[i]["a"])
+            mine = {i: (pr[i] - marg * shy[i].get(e, 0.0), -i) for i in at if e in ops[i]["a"]}
+            i = max((i for i in mine if at[i] <= t0 + 1e-9), key=mine.get)
+            soon = [j for j in mine if at[j] < t0 + min(SOON, 0.5 * ops[i]["a"][e][1]) and mine[j][0] > mine[i][0] + 1.0]
+            if soon:
+                i = max(soon, key=mine.get); t0 = max(free[e], at[i])
+            pool.remove(i); order.append(i)
+            o = ops[i]
+            if o["new"]:
+                b = min(banks, key=lambda b: (banks[b][0], b))
+                bank[o["new"]] = b; more[i] = banks.pop(b)[1]
+                if o["new"][-1] == "a": early[o["new"]] = INF
+            eng[i] = e; free[e] = t0 + o["a"][e][1]; fin[i] = free[e] + o["l"] + HOP
+            for t in o["ps"]:
+                open_[t] -= 1
+                if open_[t] == 0:
+                    banks[bank[t]] = (max(fin[j] for j in users[t]), users[t])
+                    if t in early: early[t] = banks[bank[t]][0]
+            for j in succ[i]:
+                rdy[j] = max(rdy[j], fin[i]); left[j] -= 1
+                if left[j] == 0: pool.add(j)
+        return [max(fin), order, eng, bank, more, fin]
+
+    def backward(eng, fin):
+        left, free, rdy, end = [len(x) for x in succ], {e: 0.0 for e in "atgsxv"}, [o["l"] for o in ops], [0.0] * n
+        pool = {i for i in range(n) if left[i] == 0}
+        while pool:
+            t0, e = min((max(free[eng[i]], rdy[i]), eng[i]) for i in pool)
+            i = max((i for i in pool if eng[i] == e and rdy[i] <= t0 + 1e-9), key=lambda i: (fin[i], i))
+            pool.remove(i)
+            free[e] = end[i] = t0 + ops[i]["a"][e][1]
+            for j in pred[i]:
+                rdy[j] = max(rdy[j], end[i] + ops[j]["l"] + HOP); left[j] -= 1
+                if left[j] == 0: pool.add(j)
+        return end
+    best = cur = forward(pl, MARG)
+    for k in range(PASSES):
+        cur = forward(backward(cur[2], cur[5]), MARG2)
+        if cur[0] < best[0]: best = cur
+    return best
+
+
+def helpers(T, topo, core):
+    return [c for c in topo.cores_of(core) if topo.die(c) == topo.die(core) and c not in T.cores][:NHELP]
+
+
+def back(topo, c, core): return topo.engines(c, core)[:HENG]
+
+
+def folds():
+    return [(r, u) for r in range(2) for h, w in enumerate(CH[r]) if NFS[r][h] < 0 for u in range(sum(CH[r][:h]) // GW, sum(CH[r][:h + 1]) // GW)]
+
+
+def helper_program(g, core, T, topo):
+    for c in T.cores:
+        if core in helpers(T, topo, c):
+            k, es, n = helpers(T, topo, c).index(core), back(topo, core, c), 0
+            rid, pid = topo.addr(c, core)
+            for r, u in folds():
+                if u % NHELP == k:
+                    s = slice(16 * GW * u, 16 * GW * (u + 1))
+                    g.wait_ge(T.sem["hf%d_%d" % (r, u)], len(topo.engines(c, core)) // NHELP)
+                    g.remote_dma(T.AG[:, s], T[LAND[r]][:, s], T.sem["hb%d_%d" % (r, u)], T.sem.loc, pid, rid, sum(1 << e for e in es))
+                    n += len(es)
+            if n: g.wait_ge(T.sem.loc, n)
+
+
 def rank_program(g, core, T, topo):
     rank = T.rank_of(core)
     if rank is None:
-        return
+        return helper_program(g, core, T, topo)
     ops, lastw, readers, users, bankof = [], {}, {}, {}, {}
     vec, act, ten = g.vector, g.scalar, g.tensor
     CY = 0.83e-3
@@ -176,7 +275,7 @@ def rank_program(g, core, T, topo):
         def f():
             for n, (o, l, r) in enumerate(trips): x = ten.matmul(rs(o), l, r, st and n == 0, sp and n == len(trips) - 1)
             return x
-        add({"t": (f, 0.03 + sum(0.012 + max(64, nel(o)) * k * PEC for o, l, r in trips))}, R, Wr, 0.05)
+        add({"t": (f, 0.03 + sum(0.012 + max(64, nel(o)) * (4 if "float32" in str(l.dtype) else 1) * PEC for o, l, r in trips))}, R, Wr, 0.05)
 
     def io(out, pat, base, cm, Wr, fl=True):
         if fl: f = lambda: g.iota(out, pat, base, cm, allow_small_or_imprecise_dtypes=True)
@@ -217,22 +316,34 @@ def rank_program(g, core, T, topo):
                                                  src=buf[:, o:o + BORD], dst=buf[:, o + V + (d - 1) * BORD:o + V + d * BORD]))
                 g.remote_dma_fused(trs, local_sem=T.sem.loc)
         locn[0] += len(offs) * sum(len(x) for x in mine.values())
-        i = add({"g": (f, 0.4 * len(offs))}, R, [], 0.0, "loc", 0)
+        i = add({"g": (f, 0.4 * len(offs))}, R, ["sent"], 0.0, "loc", 0)
         ops[add({"x": (None, 0.0)}, [], Wr, lat, sem, inc_in * len(offs))]["o"] = i
+
+    def fold(r, u, R, Wr):
+        c, s = helpers(T, topo, core)[u % NHELP], slice(16 * GW * u, 16 * GW * (u + 1))
+        es = topo.engines(core, c)
+        es = es[u % NHELP * len(es) // NHELP:(u % NHELP + 1) * len(es) // NHELP]
+        rid, pid = topo.addr(c, core)
+        tr = RemoteDMATransfer(dst_ids=[DstId(rid=rid, pnc=pid)], dma_engine_mask=sum(1 << e for e in es), remote_sem=T.sem["hf%d_%d" % (r, u)],
+                               srcs=[T.XG[:, s], T.RP[:, s]], dsts=[T[LAND[r]][:, s]], alu_op=2)
+        locn[0] += len(es)
+        i = add({"g": (lambda: g.remote_dma_fused([tr], local_sem=T.sem.loc), 0.4)}, R, [], 0.0, "loc", 0)
+        ops[add({"x": (None, 0.0)}, [], Wr, FLAT, "hb%d_%d" % (r, u), len(back(topo, c, core)))]["o"] = i
 
     def tk(n, xs): return ["%s_%d" % (n, x) for x in xs]
 
-    def send_g(r): send(T["Gw%d" % r], [0], "ar%d" % (2 * r), tk("Gw%d" % r, (0, 1)), ["Gw%dr" % r], 5.0)
+    def send_g(r): send(T["Gw%d" % r], [0], "ar%d" % (2 * r), tk("Gw%d" % r, (0, 1)), ["Gw%dr" % r], RLAT - 2 + 2 * r)
 
-    def send_b(r): send(T["W%d" % r], [LUTW + WN * c for c in range(3)], "ar%d" % (2 * r + 1), tk("W%d" % r, range(6)), ["W%dr" % r], 5.0)
+    def send_b(r): send(T["W%d" % r], [LUTW + WN * c for c in range(3)], "ar%d" % (2 * r + 1), tk("W%d" % r, range(6)), ["W%dr" % r], RLAT)
 
     dma("s", [(T.LI[f::16, :], T.leaf0[:, f * V:(f + 1) * V]) for f in range(8)], [], ["LIa"])
     dma("a", [(T.LI[f::16, :], T.leaf0[:, f * V:(f + 1) * V]) for f in range(8, 12)] +
         [(T.LI[13 + c::16, :], T.tab0[:, c * V:(c + 1) * V]) for c in range(3)] + [(T.fanI[:], T.fan[:])], [], ["LIb", "fanI"])
     io(T.PI[:, 0:1], [[0, 1]], 0, 1, ["PI"], False)
     io(T.IDI[:], [[1, V]], V * rank, 0, ["IDI"], False)
-    dma("s", [(T.LI[12::16, :], T.IDI[12::16, :])], ["IDI"], ["LIc"], 2.0)
-    dma("s", [(T.TR[m::16], T.tab0[:]) for m in range(16)], ["IDI"], ["TR"], 4.0)
+    dma("s", [(T.LI[12::16, :], T.IDI[12::16, :])], ["IDI"], ["LIc"], 3.0)
+    ops[-1]["b"] = 9.0
+    dma("s", [(T.TR[m::16], T.tab0[:]) for m in range(16)] + [(T.RQ[:], T.req[:])], ["IDI"], ["TR", "RQ"], 6.0)
 
     for n, (sh, an) in enumerate([(0, 15), (2, 3), (0, 3), (4, 7), (2, 31), (0, 1)]):
         ts(T.PJ[:, n:n + 1], T.PI[:, 0:1], sh, an, AL.logical_shift_right, AL.bitwise_and, ["PI"], ["PJ%d" % n])
@@ -258,7 +369,7 @@ def rank_program(g, core, T, topo):
     co("c8", kc, 2.0, -4.0, AL.min, AL.mult, PF); co("c8", vc("c8"), p16, None, AL.add, None, PF + vt("c8"))
     io(T.GI[:], [[1, 32]], 0, 0, ["GI"])
     ts(T.GM[:], T.GI[:, 0:8], gc_, None, AL.is_equal, None, ["GI"] + PF, ["GM"])
-    faff(T.GN[:], T.GM[:], -1.0, 0.0, ["GM"], ["GN"])
+    faff(T.GN[:], T.GM[:], -1.0, 0.0, ["GM"], ["GN"]); faff(T.GNF[:], T.GM[:], -1.0, 0.0, ["GM"], ["GNF"])
     ms(T.RST[:], 1.0, ["RST"]); ms(T.RST[:, 0::16], 0.0, ["RST"]); ms(T.RS8[:], 1.0, ["RS8"]); ms(T.RS8[:, 0::8], 0.0, ["RS8"])
     ms(T.TWO[:, 0:16], 2.0, ["TWO"]); ms(T.TWO[:, 16:32], 0.5, ["TWO"]); ms(T.POWR[:, 32:48], 0.0, ["ZR"])
     io(T.PIW[:], [[4, 8], [1, 4], [0, 4]], 0, 0, ["PIW"]); io(T.PIW[:, 2::4], [[4, 8], [0, 4]], 3, 0, ["PIW"])
@@ -303,13 +414,18 @@ def rank_program(g, core, T, topo):
         ts(x, x, w15, None, AL.mult, None, ["TR", "PWa"], ["TR%d" % h])
         ts(x, x, 32768, None, AL.bitwise_and, None, ["TR%d" % h], ["TR%d" % h])
         for c in range(3):
-            ts(T.W0[:, a0 + WN * c:a0 + WN * c + BORD], T.TR[:, c, h * BORD:(h + 1) * BORD], 0.0, None, AL.is_gt, None, ["TR%d" % h], tk("W0", (6 * h + c, 6 * h + 3 + c)))
+            faff(T.W0[:, a0 + WN * c:a0 + WN * c + BORD], T.TR[:, c, h * BORD:(h + 1) * BORD], 1 / 32768, 0.0, ["TR%d" % h], tk("W0", (6 * h + c, 6 * h + 3 + c)))
     send_b(0)
     cp(T.fanU[:], T.fanI[:], ["fanI"], ["fanU"])
-    ts(T.IDf[:], T.IDI[:], -1.0, 2048.0, AL.mult, AL.add, ["IDI"], ["IDf"])
-    dma("s", [(T.RQ[:], T.req[:]), (T.CE[:, 0:CE0], T.cells[:, 4096 - CE0:]), (T.CE[:, CE0:CE0 + 4096], T.cells[:]),
-              (T.CE[:, CE0 + 4096:], T.cells[:, 0:CEW - CE0 - 4096])], ["Gw0r"], ["RQ", "CE"], 10.0)
-    ts(T.IW[:, 0:V], T.IDI[:], -1.0 * V * rank, None, AL.add, None, ["IDI"], ["IW0"])
+    faff(T.IDf[:], T.IDI[:], -1.0, 2048.0, ["IDI"], ["IDf"])
+    add({"g": (lambda: g.sem_inc(T.sem.go, 1), 0.05)}, ["sent"], ["go"], 0.0, "go", 1)
+    dma("s", [(T.CE[:, 0:CE0], T.cells[:, 4096 - CE0:]), (T.CE[:, CE0:CE0 + 4096], T.cells[:]),
+              (T.CE[:, CE0 + 4096:], T.cells[:, 0:CEW - CE0 - 4096])], ["go"], ["CE"], 14.0)
+    for b in sorted({u * GW // 128 for r, u in folds()}):
+        for q in P16:
+            o, x = T.RP[:, 2048 * b + q:2048 * (b + 1):16], T.RQ[:, 128 * b:128 * b + 128]
+            add({"g": (lambda o=o, x=x: g.affine_select(o, x, [[0, 128]], AL.is_ge, 0.0, 0, 0), 0.39)}, ["RQ"], ["RP%d_%d" % (q, b)])
+    faff(T.IW[:, 0:V], T.IDI[:], 1.0, -1.0 * V * rank, ["IDI"], ["IW0"])
     for a0 in (V, 2 * V): faff(T.IW[:, a0:min(WN, a0 + V)], T.IW[:, 0:min(V, WN - a0)], 1.0, float(a0), ["IW0"], ["IW%d" % a0])
     fcp(T.Gc[:], T.IW[:].indirect(T.fanU[:]), ["IW0", "IW512", "IW1024", "fanU"], ["Gc"], GC)
     bankof["rq"] = 7
@@ -366,7 +482,8 @@ def rank_program(g, core, T, topo):
     eqm(mf("E12", 12, 13), P_("RID", 0, 1), p16, 1.0); col(mf("LP", 15), p16, PF, 1 / 256)
     col(mb("Zc1", 15), vc("nwc1"), vt("nwc1")); col(mb("Zc2", 15), vc("w2hi"), vt("w2hi"), -1 / 16)
     col(mb("Zlb", 15), vc("w2lo"), vt("w2lo"), 16.0); col(mb("ZT", 15), w2m, ["PWa"])
-    eqm(mb("IV"), P_("COL"), p16, -524288.0); ms(mb("ONE")[0], 1.0, ["MBONE"])
+    eqm(mb("IV"), P_("COL"), p16, -524288.0); eqm(mb("ID"), P_("COL"), p16, 1.0); eqm(mb("IDn"), P_("COL"), p16, -1.0)
+    for n in NFV: ms(mb("ONE%d" % n, 0, 16 - n)[0], 1.0, ["MBONE%d" % n])
     faff(tm(66, 16)[0], si[0], 4.0, 32.0, si[1], ["TM66"]); plus(tm(66, 16), tm(66, 16), (sj[0], "PJW"))
     faff(mb("KC")[0], tm(66, 16)[0], vc("is1"), vc("is0"), ["TM66"] + vt("is0", "is1"), ["MBKC"])
     TK = {}
@@ -405,7 +522,7 @@ def rank_program(g, core, T, topo):
 
     ts(T.BYI[:], T.IW[:, 0:256], w15, None, AL.mult, None, ["IW0", "PWa"], ["BYI"])
     ts(T.BYI[:], T.BYI[:], 32768, None, AL.bitwise_and, None, ["BYI"], ["BYI"])
-    ts(T.BYB[:], T.BYI[:], 0.0, None, AL.is_gt, None, ["BYI"], ["BYB"])
+    faff(T.BYB[:], T.BYI[:], 1 / 32768, 0.0, ["BYI"], ["BYB"])
     for q in range(7):
         pb = tile()
         for u in range(2): mm([(ps(pb, 256 * u, 256 * u + 256), LB("LUT%d" % (2 * q + u)), T.BYB[:])], B0 + ["BYB"], [pb])
@@ -418,17 +535,20 @@ def rank_program(g, core, T, topo):
     def chunk(r, v0, w):
         bl, nb, ns = list(range(v0 // 128, (v0 + w) // 128)), w // 128, w // 16
 
-        def t_(n, x=0): return ["%s%d_%d" % (n, x, b) for b in bl]
+        def t_(n, x=0): return ["%s%d_%d" % (n, x, b % 2 if n.upper() in RING else b) for b in bl]
 
         def ts_(n, xs): return sum([t_(n, x) for x in xs], [])
 
-        def blk(buf, k, x, n=1): return buf[:, k * v0 + x * w:k * v0 + (x + n) * w]
+        def at(buf, k): return k * (v0 % 256 if buf.name in RING else v0)
 
-        def sub(buf, k, x, b): return buf[:, k * v0 + x * w + 128 * b:k * v0 + x * w + 128 * (b + 1)]
+        def blk(buf, k, x, n=1): return buf[:, at(buf, k) + x * w:at(buf, k) + (x + n) * w]
+
+        def sub(buf, k, x, b): return buf[:, at(buf, k) + x * w + 128 * b:at(buf, k) + x * w + 128 * (b + 1)]
         Gw, Wt, Wn = T["Gw%d" % r], T["W%d" % r], T["W%d" % (1 - r)]
         Ga, Gb, Pa, Pb = blk(T.GG, 2, 0), blk(T.GG, 2, 1), blk(T.PP, 2, 0), blk(T.PP, 2, 1)
         ga, gb, pp = t_("GG", 0), t_("GG", 1), t_("PP")
-        gws = range(w // GW)
+        gws, last = range(w // GW), v0 + w == V and FINE
+        cgs = [[0, 1], [2]] if last else groups(3, w)
 
         def stage_a():
             gw = tk("Gw%d" % r, range(4)) + ["Gw%dr" % r, "fanU"]
@@ -436,7 +556,7 @@ def rank_program(g, core, T, topo):
             faff(Gb, Gw[:].indirect(T.fanU[:, (V + v0) // 16:(V + v0 + w) // 16]), 1.0, -MG * r, gw, gb, GC)
             ts(blk(T.PP, 2, 0, 2), blk(T.GG, 2, 0, 2), 0.5, None, AL.is_ge, None, ga + gb, pp, 0.5)
             for bs in groups(11, w):
-                pb = tile()
+                pb = tile() + "a"
                 for u, x in enumerate(bs):
                     l = ("SA%d" % SI[FULL[x]], "SB%d" % SJ[FULL[x]]) if x < 9 else (("I13", "R13") if x == 9 else ("R12", "I12"))
                     o = ps(pb, u * w, u * w + w)
@@ -475,6 +595,7 @@ def rank_program(g, core, T, topo):
                    [(ps(pb, u * w + 128 * b, u * w + 128 * b + 128), T.XT[:, 512 * bl[b] + 128 * y:512 * bl[b] + 128 * y + 128], LF("I256"))
                     for b in range(nb) for y in (2 * u, 2 * u + 1)], F1 + t_("XX") + tk("XT", bl), [pb])
             ts(blk(T.IX, 2, 0, 2), ps(pb, 0, 2 * w), float(WW - 1), None, AL.min, None, [pb], t_("IX"))
+            ops[-1]["b"] = LEAD
 
         def big(u): return slice(16 * (v0 + GW * u), 16 * (v0 + GW * (u + 1)))
 
@@ -491,7 +612,7 @@ def rank_program(g, core, T, topo):
                 for u, (zm, bi) in enumerate((("Zc2", 4095.0 + CE0), ("Zc1", sum(WC1) + float(CE0)))):
                     pb = tile()
                     mm([(ps(pb, 0, 128), LB(zm, 15 - q), T.AN[:, a0 + q:a0 + 2048:16]) for q in P16], B1 + gt("AN", us), [pb])
-                    ts(sub(T.CX, 2, u, b), ps(pb, 0, 128), bi, None, AL.add, None, [pb], ["CX%d_%d" % (u, bl[b])])
+                    faff(sub(T.CX, 2, u, b), ps(pb, 0, 128), 1.0, bi, [pb], ["CX%d_%d" % (u, bl[b])])
         key = []
 
         def stage_c():
@@ -500,18 +621,42 @@ def rank_program(g, core, T, topo):
                 ac(T.AG[:, big(u)], T.CE[:].indirect(T.CX[:, a0:a0 + GW]), ["CE", "CX0_%d" % b], gt("AG", [u]), cy=GC)
                 tt(T.XG[:, big(u)], T.CE[:].indirect(T.CX[:, a0 + w:a0 + w + GW]), T.AG[:, big(u)], AL.min,
                    ["CE", "CX1_%d" % b] + gt("AG", [u]), gt("XG", [u]), GC)
-            for q in P16:
-                tt(blk(T.AG, 16, q), T.XG[:, 16 * v0 + q:16 * (v0 + w):16], ps("rq", v0, v0 + w), AL.max, ["rq"] + gt("XG", gws), t_("XM", q), 1.0)
+            NF = NFS[r][sum(1 for x in range(len(CH[r])) if sum(CH[r][:x]) < v0)]
+            if NF < 0:
+                for u in gws: fold(r, v0 // GW + u, gt("XG", [u]) + ["RP%d_%d" % (q, (v0 + GW * u) // 128) for q in P16], gt("AG", [u]))
+                pb = tile()
+                key.append(pb)
+                for b in range(nb):
+                    a0, c0 = 128 * b, 16 * (v0 + 128 * b)
+                    o = ps(pb, a0, a0 + 128)
+                    mm([(o, LB("IV"), sub(T.VT, 1, 0, b)), (o, T.RQ[:, v0 + a0:v0 + a0 + 128], LB("ONE0"))] +
+                       [(ps(pb, a0 + q, a0 + 128, 16), T.AG[:, c0 + q:c0 + 2048:16], T.GN[:]) for q in P16] + [(o, T.ON[:], LB("KC"))],
+                       B1 + ["GN", "ON", "RQ"] + t_("VT") + gt("AG", range(128 * b // GW, 128 * (b + 1) // GW)), [pb])
+                return
+
+            def xg(q): return T.XG[:, 16 * v0 + q:16 * (v0 + w):16]
+
+            def xf(q, a, n): return T.XF[:, (q - 16 + NF) * w + a:(q - 16 + NF) * w + a + n]
+
+            def xt(qs): return [("XM%d_%d" % (q, b) if q < 16 - NF else "XF%d" % ((q - 16 + NF) * w // 512)) for q in qs for b in bl]
+            for q in range(16 - NF):
+                tt(blk(T.AG, 16, q), xg(q), ps("rq", v0, v0 + w), AL.max, ["rq"] + gt("XG", gws), xt([q]), 1.0)
+            for qs in groups(NF, w):
+                qs, pb = [16 - NF + q for q in qs], tile()
+                for u, q in enumerate(qs):
+                    o = ps(pb, u * w, u * w + w)
+                    mm([(o, LB("IDn"), T.RQ[:, v0:v0 + w]), (o, LB("ID"), xg(q))], B1 + ["RQ"] + gt("XG", gws), [pb])
+                frelu(xf(qs[0], 0, len(qs) * w), ps(pb, 0, len(qs) * w), 0.0, [pb], xt(qs))
             pb = tile()
             key.append(pb)
             for b in range(nb):
                 a0 = 128 * b
                 o = ps(pb, a0, a0 + 128)
                 for q0 in range(0, 16, QS):
-                    mm([(o, T.RQ[:, v0 + a0:v0 + a0 + 128], LB("ONE")), (o, LB("IV"), sub(T.VT, 1, 0, b))] * (q0 == 0) +
-                       [(ps(pb, a0 + q, a0 + 128, 16), sub(T.AG, 16, q, b), T.GN[:]) for q in range(q0, q0 + QS)] +
-                       [(o, T.ON[:], LB("KC"))] * (q0 + QS == 16),
-                       B1 + ["GN", "ON", "RQ"] + t_("VT") + ts_("XM", range(q0, q0 + QS)), [pb], q0 == 0, q0 + QS == 16)
+                    mm([(o, LB("IV"), sub(T.VT, 1, 0, b))] * (q0 == 0) + [(o, T.RQ[:, v0 + a0:v0 + a0 + 128], LB("ONE%d" % (NF % 16)))] * (q0 == 0 and NF < 16) +
+                       [(ps(pb, a0 + q, a0 + 128, 16), sub(T.AG, 16, q, b), T.GN[:]) if q < 16 - NF else (ps(pb, a0 + q, a0 + 128, 16), xf(q, a0, 128), T.GNF[:])
+                        for q in range(q0, q0 + QS)] + [(o, T.ON[:], LB("KC"))] * (q0 + QS == 16),
+                       B1 + ["GN", "GNF", "ON", "RQ"] + t_("VT") + xt(range(q0, q0 + QS)), [pb], q0 == 0, q0 + QS == 16)
 
         def stage_d():
             pb = key[0]
@@ -525,25 +670,26 @@ def rank_program(g, core, T, topo):
                     tt(blk(T.KP, 2, c), sc.indirect(bc), K1, AL.is_gt, t_("SC", c) + t_("NK1") + ["BC"], t_("KP", c), GC)
                     tt(blk(T.NKN, 2, c), blk(T.KP, 2, c), K, AL.mult, t_("KP", c) + [pb], t_("NKN", c), 1.0)
                 tt(blk(T.MT, 3, c), sc.indirect(bc), K0, AL.is_equal, t_("SC", c) + t_("NK0") + ["BC"], t_("MT", c), GC)
-            for cs in groups(3, w):
+            for cs in cgs:
                 pb = tile()
                 for u, c in enumerate(cs):
                     for b in range(nb): mm([(ps(pb, u * w + 128 * b, u * w + 128 * b + 128), sub(T.MT, 3, c, b), LF("I256"))], F1 + t_("MT", c), [pb])
                 fcp(blk(T.MK, 3, cs[0], len(cs)), ps(pb, 0, len(cs) * w), [pb], ts_("MK", cs))
-            pb = tile()
-            o = ps(pb, 0, 3 * ns)
-            mm([(o, T.ONH[0:1, :], T.CV[0:1, 3 * ns:6 * ns])] + [(o, LF("LP", 15 - x), T.MK[:, 3 * v0 + x:3 * (v0 + w):16]) for x in P16],
-               F2 + ["ONH", "CV%d" % w] + ts_("MK", range(3)), [pb])
-            ts(T.LU[:, 3 * v0 // 16:3 * (v0 + w) // 16], o, vc("p256"), None, AL.add, None, [pb] + vt("p256"), t_("LU"))
+            for cs in (cgs if last else [[0, 1, 2]]):
+                pb, n, a0 = tile(), len(cs) * ns, at(T.MK, 3) + cs[0] * w
+                o = ps(pb, 0, n)
+                mm([(o, T.ONH[0:1, :], T.CV[0:1, 3 * ns:3 * ns + n])] + [(o, LF("LP", 15 - x), T.MK[:, a0 + x:a0 + len(cs) * w:16]) for x in P16],
+                   F2 + ["ONH", "CV%d" % w] + ts_("MK", cs), [pb])
+                a0 = 3 * v0 // 16 + cs[0] * ns
+                faff(T.LU[:, a0:a0 + n], o, 1.0, vc("p256"), [pb] + vt("p256"), ts_("LU", cs))
             if r == 1:
-                M, s, n = T.SC[:, 3 * v0 + 15:3 * (v0 + w):16], slice(3 * v0 // 16, 3 * (v0 + w) // 16), 3 * ns
-                ts(T.TT[:, s], M, 0.25, None, AL.add, None, ts_("SC", range(3)), t_("TT"))
-                ts(T.Q6[:, s], M, 0.0, -524288.0, AL.is_le, AL.mult, ts_("SC", range(3)), t_("Q6"))
-                ts(T.Q5[:, s], T.TT[:, s], -1.0, 524287.0, AL.mult, AL.add, t_("TT"), t_("Q5"))
-                tt(T.Q5[:, s], T.Q5[:, s], T.Q6[:, s], AL.add, t_("Q5") + t_("Q6"), t_("Q5"))
+                M, s, n = T.SC[:, at(T.SC, 3) + 15:at(T.SC, 3) + 3 * w:16], slice(3 * v0 // 16, 3 * (v0 + w) // 16), 3 * ns
+                faff(T.Q5[:, s], M, 1.0, -524287.0 - MG, ts_("SC", range(3)), t_("Q5"))
+                add({"v": vts(T.Q6[:, s], M, 0.0, 524288.0, AL.is_le, AL.mult), "a": aac(T.Q6[:, s], M, AF.Relu, 524288.0, -524288.0)}, ts_("SC", range(3)), t_("Q6"))
                 pb = tile()
-                mm([(ps(pb, 0, 128, 1, n), T.Q5[:, s], T.IDN[:])], t_("Q5") + ["IDN"], [pb], k=4)
-                fcp(T.YC[0:n, v0:v0 + 128], ps(pb, 0, 128, 1, n), [pb], t_("YC"))
+                o = ps(pb, 0, 128, 1, n)
+                mm([(o, T.Q5[:, s], T.IDN[:]), (o, T.Q6[:, s], T.IDN[:])], t_("Q5") + t_("Q6") + ["IDN"], [pb])
+                faff(T.YC[0:n, v0:v0 + 128], o, -1.0, -MG, [pb], t_("YC"))
                 dma("s", [(T.yc[:, c * V + 128 * bl[b]:c * V + 128 * bl[b] + 128], T.YC[8 * (c * nb + b):8 * (c * nb + b) + 8, v0:v0 + 128])
                           for c in range(3) for b in range(nb)], t_("YC"), [])
 
@@ -552,9 +698,8 @@ def rank_program(g, core, T, topo):
             bits = [Wn[:, LUTW + WN * c + v0:LUTW + WN * c + v0 + w] for c in range(3)]
             for c in range(3):
                 a0 = 3 * v0 // 16 + c * ns
-                faff(bits[c], T.AN[:, 16 * v0:16 * (v0 + w)].indirect(T.LU[:, a0:a0 + ns]), -1.0, 1.0, gt("AN", gws) + t_("LU"), wn[c], GC)
-            if r == 0 and v0 + w == BORD: send_b(1)
-            for cs in groups(3, w):
+                faff(bits[c], T.AN[:, 16 * v0:16 * (v0 + w)].indirect(T.LU[:, a0:a0 + ns]), -1.0, 1.0, gt("AN", gws) + t_("LU", c), wn[c], GC)
+            for cs in cgs:
                 c0, n = cs[0], len(cs)
                 for R, G, gk, x in ((T.RA, Ga, ga, "a"), (T.RB, Gb, gb, "b")):
                     pb = tile()
@@ -574,21 +719,24 @@ def rank_program(g, core, T, topo):
                 ts(blk(T.HH, 3, c0, n), o, 0.0, 4096.0, AL.max, AL.min, [pb], ts_("HH", cs))
             pb = tile()
             o = ps(pb, 0, w)
-            pr = [] if r else [(o, LF("E12"), blk(T.IDf, 1, 0))]
-            for c in range(3):
-                pr += [(o, LB("ZT" if r else "Zlb", 2 - c), bits[c]), (o, LF("UA", 8 - 4 * c), blk(T.RA, 3, c))] + [(o, LF("UE", 2 - c), blk(T.RB, 3, c))] * r
-            mm(pr + [(o, LF("UH", 8 - 4 * c), blk(T.HH, 3, c)) for c in range(3)],
-               F2 + B1 + ["IDf"] + ts_("Ra", range(3)) + ts_("Rb", range(3)) + sum(wn, []) + ts_("HH", range(3)), [pb])
+            parts = []
+            for cs in (cgs if last else [[0, 1, 2]]):
+                pr = [(o, LF("E12"), blk(T.IDf, 1, 0))] * (r == 0 and cs[0] == 0)
+                for c in cs:
+                    pr += [(o, LB("ZT" if r else "Zlb", 2 - c), bits[c]), (o, LF("UA", 8 - 4 * c), blk(T.RA, 3, c))] + [(o, LF("UE", 2 - c), blk(T.RB, 3, c))] * r
+                hh, R = [(o, LF("UH", 8 - 4 * c), blk(T.HH, 3, c)) for c in cs], F2 + B1 + ["IDf"] + ts_("Ra", cs) + ts_("Rb", cs) + sum([wn[c] for c in cs], [])
+                parts += [(pr, R), (hh, ts_("HH", cs))] if last and cs[-1] == 2 else [(pr + hh, R + ts_("HH", cs))]
+            for n, (pr, R) in enumerate(parts): mm(pr, R, [pb], n == 0, n == len(parts) - 1)
             ops[-1]["b"] = AHEAD * (V - v0 - w)
             if r == 0:
                 faff(blk(T.Gw1, 1, 0), o, 1.0, vc("bM"), [pb] + vt("bM"), tk("Gw1", bl))
-                if v0 + w == BORD: send_g(1)
+                if v0 + w == BORD: send_g(1); send_b(1)
             else:
                 Y, YP, y = blk(T.Y, 1, 0), blk(T.YP, 1, 0), t_("Y")
-                add({"a": aac(Y, o, AF.Relu, vc("bY"), vc("sY"))}, [pb] + vt("bY", "sY"), y)
-                ts(YP, Y, vc("thr"), -2049.0, AL.is_ge, AL.mult, y + vt("thr"), t_("YP"))
-                ts(Y, Y, MG, MG, AL.add, AL.subtract, y, y)
-                tt(Y, Y, YP, AL.add, y + t_("YP"), y)
+                faff(Y, o, vc("sY"), vc("bY"), [pb] + vt("bY", "sY"), y)
+                frelu(Y, Y, -MG, y, y)
+                add({"v": vts(YP, Y, 2047.5, vc("thr"), AL.is_ge, AL.mult), "a": aac(YP, Y, AF.Relu, -2049.0 * 2047, vc("thr"))}, y + vt("thr"), t_("YP"))
+                tt(Y, Y, YP, AL.subtract, y + t_("YP"), y)
                 if v0 + w in (V - CH[1][-1], V):
                     a0 = 0 if v0 + w < V else v0
                     ys, a1 = ["Y0_%d" % b for b in range(a0 // 128, (v0 + w) // 128)], v0 + w
@@ -599,50 +747,14 @@ def rank_program(g, core, T, topo):
         return [stage_a, stage_b, stage_c, stage_d, stage_e]
     for r in range(2):
         cs = [chunk(r, sum(CH[r][:h]), CH[r][h]) for h in range(len(CH[r]))]
-        for k in range(5):
-            for st in cs: st[k]()
+        for ks in ((0,), (1,), (2, 3, 4)):
+            for st in cs:
+                for k in ks: st[k]()
 
-    n = len(ops)
-    succ, pl, rdy = [[] for _ in range(n)], [0.0] * n, [0.0] * n
-    for i, o in enumerate(ops):
-        o["dd"] = set(o["d"]) | ({o["o"]} if "o" in o else set())
-        for d in o["dd"]: succ[d].append(i)
-    for i in range(n - 1, -1, -1):
-        pl[i] = min(c for f, c in ops[i]["a"].values()) + ops[i]["l"] + HOP + max([pl[j] for j in succ[i]], default=0.0) + ops[i].get("b", 0.0)
-    left, free, order = [len(o["dd"]) for o in ops], {e: 0.0 for e in "atgsxv"}, []
-    pool = {i for i in range(n) if left[i] == 0}
-    banks, open_ = {b: (0.0, set()) for b in range(7)}, {t: len(u) for t, u in users.items()}
-    fin = {}
-    if EST:
-        pool, order = None, EST[2]
-        bankof.update(EST[3])
-        for o, p in zip(ops, EST[1]): o.update({"e": p["e"], "d": p["d"]})
-    while pool:
-        bt = min([x[0] for x in banks.values()], default=None)
-        cand = [i for i in pool if ops[i]["new"] is None or bt is not None]
-        at = {i: max(rdy[i], bt) if ops[i]["new"] else rdy[i] for i in cand}
-        t0, e = min((max(free[e], at[i]), e) for i in cand for e in ops[i]["a"])
-        mine_ = [i for i in cand if e in ops[i]["a"]]
-
-        def rank_(i): return (pl[i] - (MARG if e == "v" and len(ops[i]["a"]) > 1 else 0.0), -i)
-        i = max((i for i in mine_ if at[i] <= t0 + 1e-9), key=rank_)
-        soon = [j for j in mine_ if at[j] < t0 + min(SOON, 0.5 * ops[i]["a"][e][1]) and rank_(j)[0] > rank_(i)[0] + 1.0]
-        if soon:
-            i = max(soon, key=rank_); t0 = max(free[e], at[i])
-        pool.remove(i); order.append(i)
-        o = ops[i]
-        if o["new"]:
-            b = min(banks, key=lambda b: (banks[b][0], b))
-            bankof[o["new"]] = b; o["d"] = o["d"] | banks.pop(b)[1]
-        o.update({"e": e, "t": t0, "c": o["a"][e][1]})
-        free[e] = t0 + o["c"]; fin[i] = free[e] + o["l"] + HOP
-        for t in o["ps"]:
-            open_[t] -= 1
-            if open_[t] == 0: banks[bankof[t]] = (max(fin[j] for j in users[t]), users[t])
-        for j in succ[i]:
-            rdy[j] = max(rdy[j], fin[i]); left[j] -= 1
-            if left[j] == 0: pool.add(j)
-    if not EST: EST[:] = [free, ops, order, bankof]
+    if not EST: EST[:] = _plan(ops, users)
+    order = EST[1]
+    bankof.update(EST[3])
+    for o, e, d in zip(ops, EST[2], EST[4]): o.update({"e": e, "d": o["d"] | d})
     qs = {"v": vec, "a": act, "t": ten, "g": g, "s": g.sync}
     cnt, seen, final = {"v": 0, "a": 0, "t": 0, "g": 0}, {}, {}
     for i in order:

@@ -4,9 +4,11 @@ from concourse.mybir import AluOpType as AL, ActivationFunctionType as AF
 
 V, NR, BORD, WN = 512, 4, 256, 1280
 CH = [[128] * 4, [128] * 4]
-NFS = [[0, 8, 8, 8], [0, 8, 8, 8]]
-NFV = [0, 8]
-RLAT, FLAT, FINE = 8.0, 9.0, True
+NFS = [[4, 4, 4, 4], [4, 4, 4, 4]]
+NFV = sorted({max(x, 0) for x in sum(NFS, [])} - {16})
+LATE = ("F2", "B1")
+BT = [[1, 1, 1, 1], [1, 1, 1, 1]]
+RLAT, FLAT, FINE = 7.0, 9.0, True
 NHELP, HENG, LAND = 2, 8, ("AN", "XG")
 GW, QS = 64, 4
 LUTW = 14 * 256
@@ -21,9 +23,9 @@ SI = [0, 0, 3, 0, 1, 1, 3, 1, 2, 2, 3, 2, 0, 1, 2, 3]
 SJ = [0, 1, 0, 3, 0, 1, 1, 3, 0, 1, 2, 3, 2, 2, 2, 3]
 FULL = [q for q in P16 if SI[q] < 3 and SJ[q] < 3]
 PLACINGS = [7, 11, 13, 3, 14, 5, 6, 9, 10, 12, 1, 2, 4, 8]
-EARLY, LEAD = 7, 0.0
-NBANK, PASSES, MARG2, HALF, HALFA = 7, 6, 10.0, 0.0, 0.2
-MARG, OVH, PEC, GC, HOP, AHEAD, SOON = 20.0, 0.06, 0.43e-3, 1.5, 0.08, 0.01, 0.3
+EARLY = 7
+NBANK, PASSES, MARG2, HALF, HALFA = 7, 3, (5.0, 12.0), 0.0, 0.2
+MARG, OVH, PEC, GC, HOP, AHEAD, SOON = 20.0, 0.035, 0.46e-3, 1.56, 0.07, (0.006, 0.01, 0.014, 0.02, 0.03), 0.3
 
 
 def _old(s):
@@ -44,10 +46,10 @@ V8 = {"A1": A1 * 2, "A2": A2 * 2, "N1": N1 * 2, "N2": N2 * 2,
       "cA0": [-24, 19, -3, 14, TRIV, 0, 0, 0], "cA1": [-18, 19, -3, 14, -16, 0, 0, 0], "cBf": [6, -26, 16, 0, 0, 0, 0, 0],
       "cBt": [9, -26, 16, 0, TRIV, 0, 0, 0], "cV": [-7, 1, 1, 1, 5, 0, 0, 0], "bU": [0, -4096, -8192, 12288, 0, 0, 0, 0]}
 V16 = {"zrow": HZ * 2 + [9] * 4, "nwc1": [-x for x in WC1]}
-V2_ = {"mul": (13, -1, 16), "off": (13, -1, 0), "sub": (13, 2047, 0), "dcol": (12, DL, 0), "bRa": (13, -4096, DL - 4096),
+V2_ = {"mul": (13, -1, 16), "off": (13, -1, 0), "sub": (13, -2047, 0), "dcol": (12, DL, 0), "bRa": (13, -4096, DL - 4096),
        "bRb": (13, -4096, 2), "u3": (12, -1, 1), "sY": (13, -1, 1), "thr": (13, 2049, 0), "tY": (13, 2048 + MG, MG)}
 CN = list(V2_) + ["f12", "f13", "c8", "t5", "cAf", "cAt", "bX", "lo2", "hi2", "bY", "le12", "le12n", "is13", "is14", "is0", "is1", "bM",
-                  "p256", "w2hi", "w2lo", "nA1", "nA2"]
+                  "p256", "w2hi", "w2lo", "nA1", "nA2", "wlo", "whi"]
 _hc = [2048 * (HZ[c] - HK[c]) + 8192 * HK[c] for c in range(6)]
 PHI = {}
 for _i in range(6):
@@ -59,7 +61,7 @@ PHI.update({"CK": KK, "CL": LL, "HK": HK + [N_] * 10, "HC": _hc + [x - 24576 for
 PN = list(PHI)
 FM = [["SA0", "SA1", "SA2", "SB0", "SB1", "SB2", "I13", "R13", "I12", "R12"], ["XC", "XL", "XP", "XA", "XB", "I256"],
       ["J13", "RMa", "RMb", "EA", "EB", "HA", "HB", "Hs", "He", "UH", "UA", "UE", "E12", "LP"]]
-BM = [["LUT%d" % i for i in range(14)], ["Zc1", "Zc2", "IV", "ID", "IDn", "KC", "Zlb", "ZT"] + ["ONE%d" % n for n in NFV]]
+BM = [["LUT%d" % i for i in range(14)], ["Zc1", "Zc2"] * (set(sum(BT, [])) != {1}) + ["IV", "ID", "IDn", "KC", "Zlb", "ZT"] + ["ONE%d" % n for n in NFV]]
 FN, BN = sum(FM, []), sum(BM, [])
 f32, f16, b16, i32, u16 = "float32", "float16", "bfloat16", "int32", "uint16"
 _S = [("fanI", 64, i32), ("fanU", 64, u16), ("LI", V, i32), ("IDI", V, i32), ("GNF", 8, f32), ("XF", 128 * 16, f32), ("RP", 16 * 384 if min(sum(NFS, [])) < 0 else 16, b16), ("CE", CEW, b16), ("RQ", V, b16),
@@ -69,7 +71,7 @@ _S = [("fanI", 64, i32), ("fanU", 64, u16), ("LI", V, i32), ("IDI", V, i32), ("G
       ("POWR", 48, f32), ("POWC", 32, f32), ("TWO", 32, f32), ("TM", 128, f32), ("ONF", 128, f32), ("IDN", 128, f32),
       ("ON", 128, b16), ("ONH", 128, f16), ("BYI", 256, i32), ("BYB", 256, b16), ("BCI", 16, i32), ("BC", 16, u16), ("CV", 96, f16),
       ("PIW", 128, f32), ("PJW", 128, f32), ("PA", 512, f16), ("PB", 256, f16), ("PAV", 128, f16), ("PBV", 128, f16),
-      ("W2", 72, f16), ("W9", 224, f16),
+      ("W2", 72, f16), ("W3", 24, b16), ("CT", 768, f16), ("W9", 224, f16),
       ("GG", 2 * V, f16), ("PP", 2 * V, f16), ("SG", 11 * V, f16), ("NE", 11 * V, f16), ("XX", V, f16), ("XT", 4 * V, f16), ("VT", V, b16),
       ("IX", 2 * V, u16), ("CX", 2 * V, u16), ("AG", 16 * V, b16), ("AN", 16 * V, b16), ("XG", 16 * V, b16),
       ("NK0", V, f32), ("NK1", V, f32), ("NKN", 2 * V, f32), ("KP", 2 * V, f32), ("SC", 3 * V, f32), ("MT", 3 * V, f16), ("MK", 3 * V, f16),
@@ -121,8 +123,6 @@ def _plan(ops, users):
     succ, pl = [[] for _ in range(n)], [0.0] * n
     for i in range(n):
         for d in pred[i]: succ[d].append(i)
-    for i in range(n - 1, -1, -1):
-        pl[i] = min(c for f, c in ops[i]["a"].values()) + ops[i]["l"] + HOP + max([pl[j] for j in succ[i]], default=0.0) + ops[i].get("b", 0.0)
 
     shy = [({"v": 1.0} if o["a"]["a"][1] < 1.4 * o["a"]["v"][1] else {"v": HALF, "a": HALFA}) if len(o["a"]) > 1 else {} for o in ops]
 
@@ -174,10 +174,16 @@ def _plan(ops, users):
                 rdy[j] = max(rdy[j], end[i] + ops[j]["l"] + HOP); left[j] -= 1
                 if left[j] == 0: pool.add(j)
         return end
-    best = cur = forward(pl, MARG)
-    for k in range(PASSES):
-        cur = forward(backward(cur[2], cur[5]), MARG2)
-        if cur[0] < best[0]: best = cur
+    best = None
+    for ahead in AHEAD:
+        for i in range(n - 1, -1, -1):
+            pl[i] = min(c for f, c in ops[i]["a"].values()) + ops[i]["l"] + HOP + max([pl[j] for j in succ[i]], default=0.0) + ahead * ops[i].get("b", 0.0)
+        first = forward(pl, MARG)
+        for marg in MARG2:
+            cur = first
+            for k in range(PASSES):
+                cur = forward(backward(cur[2], cur[5]), marg)
+                if best is None or cur[0] < best[0]: best = cur
     return best
 
 
@@ -226,7 +232,7 @@ def rank_program(g, core, T, topo):
         for t in R: readers.setdefault(t, []).append(i)
         for t in Wr: lastw[t] = i; readers[t] = []
         deps.discard(i)
-        ops.append({"e": eng, "a": alts, "d": deps, "l": lat, "s": sem, "n": cnt, "new": new, "ps": [t for t in set(R) | set(Wr) if t[0] == "#"]})
+        ops.append({"e": eng, "a": alts, "d": deps, "l": lat, "s": sem, "n": cnt, "new": new, "k": (list(Wr) + ["-"])[0], "ps": [t for t in set(R) | set(Wr) if t[0] == "#"]})
         return i
 
     def tile():
@@ -275,7 +281,7 @@ def rank_program(g, core, T, topo):
         def f():
             for n, (o, l, r) in enumerate(trips): x = ten.matmul(rs(o), l, r, st and n == 0, sp and n == len(trips) - 1)
             return x
-        add({"t": (f, 0.03 + sum(0.012 + max(64, nel(o)) * (4 if "float32" in str(l.dtype) else 1) * PEC for o, l, r in trips))}, R, Wr, 0.05)
+        add({"t": (f, sum(0.016 + max(64, nel(o)) * (4 if "float32" in str(l.dtype) else 1) * PEC for o, l, r in trips))}, R, Wr, 0.05)
 
     def io(out, pat, base, cm, Wr, fl=True):
         if fl: f = lambda: g.iota(out, pat, base, cm, allow_small_or_imprecise_dtypes=True)
@@ -342,7 +348,7 @@ def rank_program(g, core, T, topo):
     io(T.PI[:, 0:1], [[0, 1]], 0, 1, ["PI"], False)
     io(T.IDI[:], [[1, V]], V * rank, 0, ["IDI"], False)
     dma("s", [(T.LI[12::16, :], T.IDI[12::16, :])], ["IDI"], ["LIc"], 3.0)
-    ops[-1]["b"] = 9.0
+    ops[-1]["b"] = 900.0
     dma("s", [(T.TR[m::16], T.tab0[:]) for m in range(16)] + [(T.RQ[:], T.req[:])], ["IDI"], ["TR", "RQ"], 6.0)
 
     for n, (sh, an) in enumerate([(0, 15), (2, 3), (0, 3), (4, 7), (2, 31), (0, 1)]):
@@ -405,18 +411,18 @@ def rank_program(g, core, T, topo):
 
     for h in range(2):
         x = T.LI[:, h * BORD:(h + 1) * BORD]
-        ts(x, x, vc("mul"), vc("off"), AL.mult, AL.add, ["LIa", "LIb", "LIc"] + vt("mul", "off"), ["LI%d" % h])
+        faff(x, x, vc("mul"), vc("off"), ["LIa", "LIb", "LIc"] + vt("mul", "off"), ["LI%d" % h])
         ts(x, x, 4095, None, AL.bitwise_and, None, ["LI%d" % h], ["LI%d" % h])
-        ts(T.Gw0[:, h * BORD:(h + 1) * BORD], x, vc("sub"), 0.0, AL.subtract, AL.max, ["LI%d" % h] + vt("sub"), tk("Gw0", (2 * h, 2 * h + 1)))
+        frelu(T.Gw0[:, h * BORD:(h + 1) * BORD], x, vc("sub"), ["LI%d" % h] + vt("sub"), tk("Gw0", (2 * h, 2 * h + 1)))
     send_g(0)
     for h in range(2):
         x, a0 = T.TR[:, :, h * BORD:(h + 1) * BORD], LUTW + h * BORD
-        ts(x, x, w15, None, AL.mult, None, ["TR", "PWa"], ["TR%d" % h])
+        faff(x, x, w15, 0.0, ["TR", "PWa"], ["TR%d" % h])
         ts(x, x, 32768, None, AL.bitwise_and, None, ["TR%d" % h], ["TR%d" % h])
         for c in range(3):
             faff(T.W0[:, a0 + WN * c:a0 + WN * c + BORD], T.TR[:, c, h * BORD:(h + 1) * BORD], 1 / 32768, 0.0, ["TR%d" % h], tk("W0", (6 * h + c, 6 * h + 3 + c)))
     send_b(0)
-    cp(T.fanU[:], T.fanI[:], ["fanI"], ["fanU"])
+    fcp(T.fanU[:], T.fanI[:], ["fanI"], ["fanU"])
     faff(T.IDf[:], T.IDI[:], -1.0, 2048.0, ["IDI"], ["IDf"])
     add({"g": (lambda: g.sem_inc(T.sem.go, 1), 0.05)}, ["sent"], ["go"], 0.0, "go", 1)
     dma("s", [(T.CE[:, 0:CE0], T.cells[:, 4096 - CE0:]), (T.CE[:, CE0:CE0 + 4096], T.cells[:]),
@@ -480,7 +486,7 @@ def rank_program(g, core, T, topo):
     eqm(mf("UH", 8, 11), P_("COL", 0, 3), vc("zrow"), 1.0, vt("zrow")); col(mf("UH", 11, 12), vc("u3"), vt("u3"))
     ms(mf("UA", 11, 12)[0], 1.0, ["MFUA"]); col(mf("UE", 15), vc("is14"), vt("is14"), -65536.0)
     eqm(mf("E12", 12, 13), P_("RID", 0, 1), p16, 1.0); col(mf("LP", 15), p16, PF, 1 / 256)
-    col(mb("Zc1", 15), vc("nwc1"), vt("nwc1")); col(mb("Zc2", 15), vc("w2hi"), vt("w2hi"), -1 / 16)
+    if "Zc1" in BN: col(mb("Zc1", 15), vc("nwc1"), vt("nwc1")); col(mb("Zc2", 15), vc("w2hi"), vt("w2hi"), -1 / 16)
     col(mb("Zlb", 15), vc("w2lo"), vt("w2lo"), 16.0); col(mb("ZT", 15), w2m, ["PWa"])
     eqm(mb("IV"), P_("COL"), p16, -524288.0); eqm(mb("ID"), P_("COL"), p16, 1.0); eqm(mb("IDn"), P_("COL"), p16, -1.0)
     for n in NFV: ms(mb("ONE%d" % n, 0, 16 - n)[0], 1.0, ["MBONE%d" % n])
@@ -491,8 +497,14 @@ def rank_program(g, core, T, topo):
         o = 0
         for gi, ns in enumerate(grp):
             for q in range(8):
-                faff(B[:, o:o + len(ns), 16 * q:16 * q + 16], M[:, o:o + len(ns), :], T.GM[:, q:q + 1], 0.0, ["GM"] + ["M" + tag + n for n in ns],
-                     ["B%s%d_%d" % (tag, gi, q)], 1.0, 0.5)
+                dst, src, R, Wr = B[:, o:o + len(ns), 16 * q:16 * q + 16], M[:, o:o + len(ns), :], ["M" + tag + n for n in ns], ["B%s%d_%d" % (tag, gi, q)]
+                if tag + str(gi) not in LATE:
+                    faff(dst, src, T.GM[:, q:q + 1], 0.0, ["GM"] + R, Wr, 1.0, 0.5)
+                    continue
+                for base, cm in [(-16 * q, 1)] * (q > 0) + [(16 * q + 15, -1)] * (q < 7):
+                    add({"g": (lambda dst=dst, src=src, base=base, cm=cm: g.affine_select(dst, src, [[0, nel(dst)]], AL.is_ge, 0.0, base, cm),
+                               0.17 + 2 * nel(dst) * CY)}, R, Wr)
+                    src, R = dst, Wr
             TK[tag + str(gi)] = ["B%s%d_%d" % (tag, gi, q) for q in range(8)] + ["B%sz" % tag]
             o += len(ns)
 
@@ -503,6 +515,10 @@ def rank_program(g, core, T, topo):
     for n, x in enumerate(["kA1", "kA2", "A1", "A2", "kN1", "kN2", "N1", "N2"]):
         ts(T.W2[:, 8 * n:8 * n + 8], T.GM[:], vc(x), 1.0 - 2 * (n < 2), AL.mult, AL.mult, ["GM"] + vt(x), ["W2_%d" % n])
     fcp(T.W2[:, 64:72], T.GM[:], ["GM"], ["W2_8"])
+    if max(sum(BT, [])):
+        co("wlo", p16, 10.0, vc("nwc1"), AL.is_le, AL.mult, PF + vt("nwc1")); co("whi", p16, 10.0, vc("nwc1"), AL.is_gt, AL.mult, PF + vt("nwc1"))
+        for n, (x, y) in enumerate((("w2hi", -1 / 16), ("wlo", 1.0), ("whi", 1.0))):
+            ts(T.W3[:, 8 * n:8 * n + 8], T.GM[:], vc(x), y, AL.mult, AL.mult, ["GM"] + vt(x), ["W3"])
     for n, x in enumerate(["nA1", "nA2", 0.5, "N1", "N2", 0.5, 1.0]):
         c_ = isinstance(x, str)
         ts(T.W9[:, 32 * n:32 * n + 32], T.GI[:], p4, vc(x) if c_ else x, AL.is_equal, AL.mult, ["GI"] + PF + (vt(x) if c_ else []), ["W9_%d" % n])
@@ -511,16 +527,15 @@ def rank_program(g, core, T, topo):
     for a0, x in ((0, "cA"), (128, "cB")):
         wide("PA", a0, "PIW", 0, 1, x + "f"); wide("PA", a0, "PIW", 3, 4, x + "t")
         wide("PB", a0, "PJW", 0, 1, x + "f"); wide("PB", a0, "PJW", 2, 4, x + "t"); wide("PB", a0, "PJW", 14, 16, x + "f")
-    ms(T.PA[:, 256:512], 0.0, ["PA256"], 0.5)
     for n, pn in (("PAV", "PIW"), ("PBV", "PJW")):
         wide(n, 0, pn, 0, 1, "cV"); ms(T[n][:, 15::16], 0.0, [n + "0"])
-    WT = tk("W2", range(9)) + tk("W9", range(7)) + ["PA0", "PA128", "PA256", "PB0", "PB128", "PAV0", "PBV0"]
+    WT = tk("W2", range(9)) + tk("W9", range(7)) + ["PA0", "PA128", "PB0", "PB128", "PAV0", "PBV0"]
     ms(T.ON[:], 1.0, ["ON"], 0.5); ms(T.ONH[:], 1.0, ["ONH"], 0.5); ms(T.ONF[:], 1.0, ["ONF"])
     add({"g": (lambda: g.affine_select(T.IDN[:], T.ONF[:], [[-1, 128]], AL.is_equal, 0.0, 0, 1), 0.4)}, ["ONF"], ["IDN"])
     io(T.BCI[:], [[16, 16]], 15, 0, ["BCI"], False); cp(T.BC[:], T.BCI[:], ["BCI"], ["BC"])
     for w in sorted(set(sum(CH, []))): io(T.CV[0:1, 3 * w // 16:6 * w // 16], [[0, 3], [256, w // 16]], 0, 0, ["CV%d" % w])
 
-    ts(T.BYI[:], T.IW[:, 0:256], w15, None, AL.mult, None, ["IW0", "PWa"], ["BYI"])
+    faff(T.BYI[:], T.IW[:, 0:256], w15, 0.0, ["IW0", "PWa"], ["BYI"])
     ts(T.BYI[:], T.BYI[:], 32768, None, AL.bitwise_and, None, ["BYI"], ["BYI"])
     faff(T.BYB[:], T.BYI[:], 1 / 32768, 0.0, ["BYI"], ["BYB"])
     for q in range(7):
@@ -575,7 +590,7 @@ def rank_program(g, core, T, topo):
                 def sg(x): return sub(T.SG, 11, x, b)
 
                 def ne(x): return sub(T.NE, 11, x, b)
-                parts = [([(ps(pb, 0, 512), sub(T.PP, 2, 0, b), T.PA[:]), (ps(pb, 256, 512), sub(T.PP, 2, 1, b), T.PB[:])], [])]
+                parts = [([(ps(pb, 0, 256), sub(T.PP, 2, 0, b), T.PA[:, 0:256]), (ps(pb, 256, 512), sub(T.PP, 2, 1, b), T.PB[:])], [])]
                 for xs in ((0, 1, 2, 3), (4, 5, 6, 7), (8,)):
                     parts.append((sum([[(ps(pb, FULL[x], 512, 16), sg(x), W2[:, 0:32]), (ps(pb, FULL[x], 512, 16), ne(x), W2[:, 32:64])] for x in xs], []), xs))
                 for x, own, oth in ((9, ps(pb, 3, 256, 4), ps(pb, 259, 384, 4)), (10, ps(pb, 258, 512, 4), ps(pb, 2, 128, 4))):
@@ -590,12 +605,10 @@ def rank_program(g, core, T, topo):
                    [(ps(pv, a0 + 12 - x, a0 + 128, 4), ne(x), W9[:, 192:224]) for x in (9, 10)], WT + pp + ts_("NE", range(11)), [pv])
             frelu(blk(T.VT, 1, 0), ps(pv, 0, w), -4.0, [pv], t_("VT"))
             pb = tile()
-            for u, x in enumerate("AB"):
-                mm([(ps(pb, u * w, u * w + w), LF("X" + x), blk(T.XX, 1, 0))] +
-                   [(ps(pb, u * w + 128 * b, u * w + 128 * b + 128), T.XT[:, 512 * bl[b] + 128 * y:512 * bl[b] + 128 * y + 128], LF("I256"))
-                    for b in range(nb) for y in (2 * u, 2 * u + 1)], F1 + t_("XX") + tk("XT", bl), [pb])
+            mm([(ps(pb, u * w, u * w + w), LF("X" + x), blk(T.XX, 1, 0)) for u, x in enumerate("AB")], F1 + t_("XX"), [pb], True, False)
+            mm([(ps(pb, y // 2 * w + 128 * b, y // 2 * w + 128 * b + 128), T.XT[:, 512 * bl[b] + 128 * y:512 * bl[b] + 128 * y + 128], LF("I256"))
+                for b in range(nb) for y in range(4)], F1 + tk("XT", bl), [pb], False, True)
             ts(blk(T.IX, 2, 0, 2), ps(pb, 0, 2 * w), float(WW - 1), None, AL.min, None, [pb], t_("IX"))
-            ops[-1]["b"] = LEAD
 
         def big(u): return slice(16 * (v0 + GW * u), 16 * (v0 + GW * (u + 1)))
 
@@ -605,22 +618,41 @@ def rank_program(g, core, T, topo):
             wt = tk("W%d" % r, range(12)) + ["W%dr" % r] + (LUT0 if r == 0 else ["LUTc"])
             for u in gws:
                 a0 = 2 * v0 + GW * u
-                ac(T.AG[:, big(u)], Wt[:].indirect(T.IX[:, a0:a0 + GW]), wt + t_("IX"), gt("AG", [u]) + ts_("XM", P16), cy=GC)
+                fcp(T.AG[:, big(u)], Wt[:].indirect(T.IX[:, a0:a0 + GW]), wt + t_("IX"), gt("AG", [u]) + ts_("XM", P16), GC)
                 tt(T.AN[:, big(u)], Wt[:].indirect(T.IX[:, a0 + w:a0 + w + GW]), T.AG[:, big(u)], AL.mult, wt + t_("IX") + gt("AG", [u]), gt("AN", [u]), GC)
             for b in range(nb):
                 a0, us = 16 * (v0 + 128 * b), range(128 * b // GW, 128 * (b + 1) // GW)
+                if BT[r][bl[b]] == 2:
+                    for y in us:
+                        for u, (zm, bi) in enumerate((("Zc2", 4095.0 + CE0), ("Zc1", sum(WC1) + float(CE0)))):
+                            pb, c0 = tile(), 16 * (v0 + GW * y)
+                            mm([(ps(pb, 0, GW), LB(zm, 15 - q), T.AN[:, c0 + q:c0 + 16 * GW:16]) for q in P16], B1 + gt("AN", [y]), [pb])
+                            c0 = 2 * v0 + u * w + GW * y
+                            faff(T.CX[:, c0:c0 + GW], ps(pb, 0, GW), 1.0, bi, [pb], gt("CX%d" % u, [y]))
+                    continue
+                if BT[r][bl[b]]:
+                    pb, ct, c0 = tile(), "CT%d" % (bl[b] % 2), 384 * (bl[b] % 2)
+                    for q0 in (0, 8):
+                        add({"t": (lambda pb=pb, q0=q0, a0=a0: [ten.matmul(rs(ps(pb, q, 384, 16)), T.AN[:, a0 + q:a0 + 2048:16], T.W3[:], True, True)
+                                                                for q in range(q0, q0 + 8)][-1], 8 * (0.016 + 64 * PEC))}, ["W3"] + gt("AN", us), [pb], 0.05)
+                    faff(T.CT[:, c0:c0 + 384], ps(pb, 0, 384), 1.0, 2048.0, [pb], [ct])
+                    for u, (ys, bi) in enumerate((((0,), 4095.0 + CE0 - 2048), ((1, 2), sum(WC1) + CE0 - 4096.0))):
+                        pb = tile()
+                        mm([(ps(pb, 0, 128), T.CT[:, c0 + 128 * y:c0 + 128 * y + 128], LF("I256")) for y in ys], F1 + [ct], [pb])
+                        faff(sub(T.CX, 2, u, b), ps(pb, 0, 128), 1 / 256, bi, [pb], gt("CX%d" % u, us))
+                    continue
                 for u, (zm, bi) in enumerate((("Zc2", 4095.0 + CE0), ("Zc1", sum(WC1) + float(CE0)))):
                     pb = tile()
                     mm([(ps(pb, 0, 128), LB(zm, 15 - q), T.AN[:, a0 + q:a0 + 2048:16]) for q in P16], B1 + gt("AN", us), [pb])
-                    faff(sub(T.CX, 2, u, b), ps(pb, 0, 128), 1.0, bi, [pb], ["CX%d_%d" % (u, bl[b])])
+                    faff(sub(T.CX, 2, u, b), ps(pb, 0, 128), 1.0, bi, [pb], gt("CX%d" % u, us))
         key = []
 
         def stage_c():
             for u in gws:
                 a0, b = 2 * v0 + GW * u, (v0 + GW * u) // 128
-                ac(T.AG[:, big(u)], T.CE[:].indirect(T.CX[:, a0:a0 + GW]), ["CE", "CX0_%d" % b], gt("AG", [u]), cy=GC)
+                fcp(T.AG[:, big(u)], T.CE[:].indirect(T.CX[:, a0:a0 + GW]), ["CE"] + gt("CX0", [u]), gt("AG", [u]), GC)
                 tt(T.XG[:, big(u)], T.CE[:].indirect(T.CX[:, a0 + w:a0 + w + GW]), T.AG[:, big(u)], AL.min,
-                   ["CE", "CX1_%d" % b] + gt("AG", [u]), gt("XG", [u]), GC)
+                   ["CE"] + gt("CX1", [u]) + gt("AG", [u]), gt("XG", [u]), GC)
             NF = NFS[r][sum(1 for x in range(len(CH[r])) if sum(CH[r][:x]) < v0)]
             if NF < 0:
                 for u in gws: fold(r, v0 // GW + u, gt("XG", [u]) + ["RP%d_%d" % (q, (v0 + GW * u) // 128) for q in P16], gt("AG", [u]))
@@ -653,7 +685,7 @@ def rank_program(g, core, T, topo):
                 a0 = 128 * b
                 o = ps(pb, a0, a0 + 128)
                 for q0 in range(0, 16, QS):
-                    mm([(o, LB("IV"), sub(T.VT, 1, 0, b))] * (q0 == 0) + [(o, T.RQ[:, v0 + a0:v0 + a0 + 128], LB("ONE%d" % (NF % 16)))] * (q0 == 0 and NF < 16) +
+                    mm([(o, LB("IV"), sub(T.VT, 1, 0, b))] * (q0 == 0) + [(o, T.RQ[:, v0 + a0:v0 + a0 + 128], LB("ONE%d" % min(NF, NFV[-1])))] * (q0 == 0 and NF < 16) +
                        [(ps(pb, a0 + q, a0 + 128, 16), sub(T.AG, 16, q, b), T.GN[:]) if q < 16 - NF else (ps(pb, a0 + q, a0 + 128, 16), xf(q, a0, 128), T.GNF[:])
                         for q in range(q0, q0 + QS)] + [(o, T.ON[:], LB("KC"))] * (q0 + QS == 16),
                        B1 + ["GN", "GNF", "ON", "RQ"] + t_("VT") + xt(range(q0, q0 + QS)), [pb], q0 == 0, q0 + QS == 16)
@@ -675,11 +707,12 @@ def rank_program(g, core, T, topo):
                 for u, c in enumerate(cs):
                     for b in range(nb): mm([(ps(pb, u * w + 128 * b, u * w + 128 * b + 128), sub(T.MT, 3, c, b), LF("I256"))], F1 + t_("MT", c), [pb])
                 fcp(blk(T.MK, 3, cs[0], len(cs)), ps(pb, 0, len(cs) * w), [pb], ts_("MK", cs))
-            for cs in (cgs if last else [[0, 1, 2]]):
+            for cs in (cgs if last and FINE > 1 else [[0, 1, 2]]):
                 pb, n, a0 = tile(), len(cs) * ns, at(T.MK, 3) + cs[0] * w
                 o = ps(pb, 0, n)
-                mm([(o, T.ONH[0:1, :], T.CV[0:1, 3 * ns:3 * ns + n])] + [(o, LF("LP", 15 - x), T.MK[:, a0 + x:a0 + len(cs) * w:16]) for x in P16],
-                   F2 + ["ONH", "CV%d" % w] + ts_("MK", cs), [pb])
+                for x0 in range(0, 16, 4):
+                    mm([(o, T.ONH[0:1, :], T.CV[0:1, 3 * ns:3 * ns + n])] * (x0 == 0) + [(o, LF("LP", 15 - x), T.MK[:, a0 + x:a0 + len(cs) * w:16]) for x in range(x0, x0 + 4)],
+                       F2 + ["ONH", "CV%d" % w] + ts_("MK", cs), [pb], x0 == 0, x0 == 12)
                 a0 = 3 * v0 // 16 + cs[0] * ns
                 faff(T.LU[:, a0:a0 + n], o, 1.0, vc("p256"), [pb] + vt("p256"), ts_("LU", cs))
             if r == 1:
@@ -703,9 +736,8 @@ def rank_program(g, core, T, topo):
                 c0, n = cs[0], len(cs)
                 for R, G, gk, x in ((T.RA, Ga, ga, "a"), (T.RB, Gb, gb, "b")):
                     pb = tile()
-                    for u, c in enumerate(cs):
-                        o = ps(pb, u * w, u * w + w)
-                        mm([(o, LF("J13"), G), (o, LF("RM" + x), blk(T.MK, 3, c))], F2 + gk + t_("MK", c), [pb])
+                    mm([(ps(pb, 0, n * w), LF("RM" + x), blk(T.MK, 3, c0, n))] + [(ps(pb, u * w, u * w + w), LF("J13"), G) for u in range(n)],
+                       F2 + gk + ts_("MK", cs), [pb])
                     frelu(blk(R, 3, c0, n), ps(pb, 0, n * w), vc("bR" + x), [pb] + vt("bR" + x), ts_("R" + x, cs))
                 ra, rb, s2, e2, rk = blk(T.RA, 3, c0, n), blk(T.RB, 3, c0, n), blk(T.S2, 3, c0, n), blk(T.E2, 3, c0, n), F2 + ts_("Ra", cs) + ts_("Rb", cs)
                 pb = tile()
@@ -722,12 +754,13 @@ def rank_program(g, core, T, topo):
             parts = []
             for cs in (cgs if last else [[0, 1, 2]]):
                 pr = [(o, LF("E12"), blk(T.IDf, 1, 0))] * (r == 0 and cs[0] == 0)
-                for c in cs:
-                    pr += [(o, LB("ZT" if r else "Zlb", 2 - c), bits[c]), (o, LF("UA", 8 - 4 * c), blk(T.RA, 3, c))] + [(o, LF("UE", 2 - c), blk(T.RB, 3, c))] * r
-                hh, R = [(o, LF("UH", 8 - 4 * c), blk(T.HH, 3, c)) for c in cs], F2 + B1 + ["IDf"] + ts_("Ra", cs) + ts_("Rb", cs) + sum([wn[c] for c in cs], [])
-                parts += [(pr, R), (hh, ts_("HH", cs))] if last and cs[-1] == 2 else [(pr + hh, R + ts_("HH", cs))]
+                for c in cs: pr += [(o, LF("UA", 8 - 4 * c), blk(T.RA, 3, c))] + [(o, LF("UE", 2 - c), blk(T.RB, 3, c))] * r
+                hh, R = [(o, LF("UH", 8 - 4 * c), blk(T.HH, 3, c)) for c in cs], F2 + B1 + ["IDf"] + ts_("Ra", cs) + ts_("Rb", cs)
+                zz = ([(o, LB("ZT" if r else "Zlb", 2 - c), bits[c]) for c in range(3)], sum(wn, []))
+                if not last: parts = [(pr + zz[0] + hh, R + zz[1] + ts_("HH", cs))]
+                else: parts += [(pr, R), zz, (hh, ts_("HH", cs))] if cs[-1] == 2 else [(pr + hh, R + ts_("HH", cs))]
             for n, (pr, R) in enumerate(parts): mm(pr, R, [pb], n == 0, n == len(parts) - 1)
-            ops[-1]["b"] = AHEAD * (V - v0 - w)
+            ops[-1]["b"] = V - v0 - w
             if r == 0:
                 faff(blk(T.Gw1, 1, 0), o, 1.0, vc("bM"), [pb] + vt("bM"), tk("Gw1", bl))
                 if v0 + w == BORD: send_g(1); send_b(1)

@@ -4,11 +4,12 @@ from concourse.mybir import AluOpType as AL, ActivationFunctionType as AF
 
 V, NR, BORD, WN = 512, 4, 256, 1280
 CH = [[128] * 4, [128] * 4]
-NFS = [[4, 4, 4, 4], [4, 4, 4, 4]]
+SCAN, RD = False, 2
+NFS = [[8, 8, 4, 4], [8, 8, 4, 4]]
 NFV = sorted({max(x, 0) for x in sum(NFS, [])} - {16})
 LATE = ("F2", "B1")
 BT = [[1, 1, 1, 1], [1, 1, 1, 1]]
-RLAT, FLAT, FINE = 7.0, 9.0, True
+RLAT, RLAT1, FLAT, FINE, LLAT = 5.0, 7.0, 7.0, True, 2.5
 NHELP, HENG, LAND = 2, 8, ("AN", "XG")
 GW, QS = 64, 4
 LUTW = 14 * 256
@@ -21,11 +22,14 @@ KK = [p >> 2 for p in P16]
 LL = [p & 3 for p in P16]
 SI = [0, 0, 3, 0, 1, 1, 3, 1, 2, 2, 3, 2, 0, 1, 2, 3]
 SJ = [0, 1, 0, 3, 0, 1, 1, 3, 0, 1, 2, 3, 2, 2, 2, 3]
-FULL = [q for q in P16 if SI[q] < 3 and SJ[q] < 3]
+FULL = sorted((q for q in P16 if SI[q] < 3 and SJ[q] < 3), key=lambda q: (SJ[q], SI[q]))
+CHAIN, NEA = (0, 0, 0, 0), (1, 1, 1, 1, 1)
 PLACINGS = [7, 11, 13, 3, 14, 5, 6, 9, 10, 12, 1, 2, 4, 8]
-EARLY = 7
-NBANK, PASSES, MARG2, HALF, HALFA = 7, 3, (5.0, 12.0), 0.0, 0.2
-MARG, OVH, PEC, GC, HOP, AHEAD, SOON = 20.0, 0.035, 0.46e-3, 1.56, 0.07, (0.006, 0.01, 0.014, 0.02, 0.03), 0.3
+POV, PMIN, VF, VO = 0.012, 64, 1.0, 0.0
+RUSH, RW, RK = 0.0, (1, 1, 0, 0), 3
+EARLY, BV, WAIT, GAP = 8, (384, 256, 128, 0), (0.5, 1.0), 1.0
+NBANK, PASSES, MARG2, HALF, HALFA = 7 + SCAN, 4, ((3.0, 0.0), (6.0, 0.005), (10.0, 0.0), (16.0, 0.01)), 0.0, 0.2
+MARG, OVH, PEC, GC, HOP, AHEAD, SOON = 20.0, 0.02, 0.43e-3, 1.56, 0.3, (0.004, 0.008, 0.012, 0.016, 0.02, 0.03), 0.6
 
 
 def _old(s):
@@ -49,7 +53,7 @@ V16 = {"zrow": HZ * 2 + [9] * 4, "nwc1": [-x for x in WC1]}
 V2_ = {"mul": (13, -1, 16), "off": (13, -1, 0), "sub": (13, -2047, 0), "dcol": (12, DL, 0), "bRa": (13, -4096, DL - 4096),
        "bRb": (13, -4096, 2), "u3": (12, -1, 1), "sY": (13, -1, 1), "thr": (13, 2049, 0), "tY": (13, 2048 + MG, MG)}
 CN = list(V2_) + ["f12", "f13", "c8", "t5", "cAf", "cAt", "bX", "lo2", "hi2", "bY", "le12", "le12n", "is13", "is14", "is0", "is1", "bM",
-                  "p256", "w2hi", "w2lo", "nA1", "nA2", "wlo", "whi"]
+                  "p256", "w2hi", "w2lo", "nA1", "nA2", "wlo", "whi", "p16s"]
 _hc = [2048 * (HZ[c] - HK[c]) + 8192 * HK[c] for c in range(6)]
 PHI = {}
 for _i in range(6):
@@ -57,28 +61,31 @@ for _i in range(6):
 PHI.update({"COL": P16, "RID": [12] * 16})
 for _i, _m in enumerate(PLACINGS):
     PHI["LUT%d" % _i] = _old(_m)
-PHI.update({"CK": KK, "CL": LL, "HK": HK + [N_] * 10, "HC": _hc + [x - 24576 for x in _hc] + [-8192] * 4})
+PHI.update({"HK": HK + [N_] * 10, "HC": _hc + [x - 24576 for x in _hc] + [-8192] * 4})
 PN = list(PHI)
 FM = [["SA0", "SA1", "SA2", "SB0", "SB1", "SB2", "I13", "R13", "I12", "R12"], ["XC", "XL", "XP", "XA", "XB", "I256"],
       ["J13", "RMa", "RMb", "EA", "EB", "HA", "HB", "Hs", "He", "UH", "UA", "UE", "E12", "LP"]]
-BM = [["LUT%d" % i for i in range(14)], ["Zc1", "Zc2"] * (set(sum(BT, [])) != {1}) + ["IV", "ID", "IDn", "KC", "Zlb", "ZT"] + ["ONE%d" % n for n in NFV]]
+BM = [["LUT%d" % i for i in range(14)], ["Zc1", "Zc2"] * (set(sum(BT, [])) != {1}) + ["ID", "IDn"] * (not SCAN) + ["IV", "KC", "Zlb", "ZT"] + ["ONE%d" % n for n in NFV]]
 FN, BN = sum(FM, []), sum(BM, [])
 f32, f16, b16, i32, u16 = "float32", "float16", "bfloat16", "int32", "uint16"
-_S = [("fanI", 64, i32), ("fanU", 64, u16), ("LI", V, i32), ("IDI", V, i32), ("GNF", 8, f32), ("XF", 128 * 16, f32), ("RP", 16 * 384 if min(sum(NFS, [])) < 0 else 16, b16), ("CE", CEW, b16), ("RQ", V, b16),
+_S = [("fanI", 64, i32), ("fanU", 64, u16), ("LI", V, i32), ("LJ", V, i32), ("TF", V, f32), ("PW", 384, f32), ("BT3", 384, f32), ("IDI", V, i32), ("GNF", 8, f32), ("XF", 128 * 16, f32), ("RP", 16 * 384 if min(sum(NFS, [])) < 0 else 16, b16), ("CE", CEW, b16), ("RQ", V, b16),
       ("Gw0", WN, f32), ("Gw1", WN, f32), ("W0", WW, b16), ("W1", WW, b16), ("IW", WN, f32), ("Gc", 2 * V, f16),
       ("IDf", V, f16), ("PI", 8, i32), ("PJ", 8, i32), ("PF", 8, f32), ("GI", 32, f32), ("GM", 8, f32), ("GN", 8, b16), ("CO", len(CN), f32),
-      ("VAL", 112, f32), ("OHI", 80, f32), ("OH", 176, f32), ("PR", 176, f32), ("VC", 176, f32), ("RST", 256, f32), ("RS8", 112, f32),
+      ("VAL", 112, f32), ("OHI", 80, f32), ("OH", 176, f32), ("PR", 176, f32), ("VC", 176, f32), ("RST", 384, f32),
       ("POWR", 48, f32), ("POWC", 32, f32), ("TWO", 32, f32), ("TM", 128, f32), ("ONF", 128, f32), ("IDN", 128, f32),
-      ("ON", 128, b16), ("ONH", 128, f16), ("BYI", 256, i32), ("BYB", 256, b16), ("BCI", 16, i32), ("BC", 16, u16), ("CV", 96, f16),
+      ("ON", 128, b16), ("ONH", 128, f16), ("BYI", 256, i32), ("BYB", 256, b16), ("BCI", 16, i32), ("BC", 16, u16), ("CV", 192, f16), ("IND", 128, f16), ("LS", V, f32),
       ("PIW", 128, f32), ("PJW", 128, f32), ("PA", 512, f16), ("PB", 256, f16), ("PAV", 128, f16), ("PBV", 128, f16),
-      ("W2", 72, f16), ("W3", 24, b16), ("CT", 768, f16), ("W9", 224, f16),
+      ("W2", 72, f16), ("W3", 24, b16), ("CT", 768, f16), ("W9", 352, f16),
       ("GG", 2 * V, f16), ("PP", 2 * V, f16), ("SG", 11 * V, f16), ("NE", 11 * V, f16), ("XX", V, f16), ("XT", 4 * V, f16), ("VT", V, b16),
       ("IX", 2 * V, u16), ("CX", 2 * V, u16), ("AG", 16 * V, b16), ("AN", 16 * V, b16), ("XG", 16 * V, b16),
       ("NK0", V, f32), ("NK1", V, f32), ("NKN", 2 * V, f32), ("KP", 2 * V, f32), ("SC", 3 * V, f32), ("MT", 3 * V, f16), ("MK", 3 * V, f16),
       ("LU", 3 * V // 16, u16), ("RA", 3 * V, f16), ("RB", 3 * V, f16), ("S2", 3 * V, f16), ("E2", 3 * V, f16), ("HH", 3 * V, f16),
       ("Y", V, f32), ("YP", V, f32), ("TT", 96, i32), ("Q5", 96, f32), ("Q6", 96, f32), ("YC", V, f32)]
-RING = ("NK0", "NK1", "NKN", "KP", "MT", "RA", "RB", "S2", "E2", "HH", "YP")
+RING = ("NK0", "NK1", "NKN", "KP", "MT", "RA", "RB", "S2", "E2", "HH", "YP", "SG", "NE")
 SCRATCH = {n: ("sbuf", [128, k // 2 if n in RING else k], d) for n, k, d in _S}
+if SCAN:
+    SCRATCH.update({"D0": ("sbuf", [128, 8192], b16), "D1": ("sbuf", [128, 4096 * RD], b16), "DO": ("sbuf", [128, 8192], b16), "AG": ("sbuf", [128, 4096], b16),
+                    "XG": ("sbuf", [128, 16], b16), "XF": ("sbuf", [128, 16], f32)})
 SCRATCH.update({"TR": ("sbuf", [128, 3, V], i32), "PH": ("sbuf", [128, len(PN), 16], f32), "MF": ("sbuf", [128, len(FN), 16], f16), "MB": ("sbuf", [128, len(BN), 16], b16),
                 "BF": ("sbuf", [128, len(FN), 144], f16), "BB": ("sbuf", [128, len(BN), 144], b16)})
 for _b in range(8):
@@ -114,6 +121,25 @@ def _cover(L):
 
 
 COVER = {n: _cover(x) for n, x in PHI.items()}
+
+
+def _runs(L):
+    out = []
+    for x in sorted(set(L) - {0}):
+        rest = {i for i, y in enumerate(L) if y == x}
+        while rest:
+            best = None
+            for a in sorted(rest):
+                for st in [1] + [b - a for b in sorted(rest) if b > a]:
+                    n = 1
+                    while a + n * st in rest and n < 16: n += 1
+                    if best is None or n > best[2]: best = (a, st, n)
+            out.append(best + (float(x),)); rest -= {best[0] + k * best[1] for k in range(best[2])}
+    return out
+
+
+VRUNS = _runs([x * 128 for y in list(V8.values())[:9] for x in y])
+VS, GOV, TLAT, TRA = 1, 0.1, 6.0, 1
 VCOVER = [_cover([int(x * 128) for y in list(V8.values())[:9] for x in y]), _cover(V8["bU"]), _cover(sum(V16.values(), []))]
 
 
@@ -142,7 +168,7 @@ def _plan(ops, users):
             t0, e = min((max(free[e], at[i]), e) for i in at for e in ops[i]["a"])
             mine = {i: (pr[i] - marg * shy[i].get(e, 0.0), -i) for i in at if e in ops[i]["a"]}
             i = max((i for i in mine if at[i] <= t0 + 1e-9), key=mine.get)
-            soon = [j for j in mine if at[j] < t0 + min(SOON, 0.5 * ops[i]["a"][e][1]) and mine[j][0] > mine[i][0] + 1.0]
+            soon = [j for j in mine if at[j] < t0 + min(SOON, WAIT[e == "t"] * ops[i]["a"][e][1]) and mine[j][0] > mine[i][0] + GAP]
             if soon:
                 i = max(soon, key=mine.get); t0 = max(free[e], at[i])
             pool.remove(i); order.append(i)
@@ -162,7 +188,7 @@ def _plan(ops, users):
                 if left[j] == 0: pool.add(j)
         return [max(fin), order, eng, bank, more, fin]
 
-    def backward(eng, fin):
+    def backward(eng, fin, back):
         left, free, rdy, end = [len(x) for x in succ], {e: 0.0 for e in "atgsxv"}, [o["l"] for o in ops], [0.0] * n
         pool = {i for i in range(n) if left[i] == 0}
         while pool:
@@ -171,7 +197,7 @@ def _plan(ops, users):
             pool.remove(i)
             free[e] = end[i] = t0 + ops[i]["a"][e][1]
             for j in pred[i]:
-                rdy[j] = max(rdy[j], end[i] + ops[j]["l"] + HOP); left[j] -= 1
+                rdy[j] = max(rdy[j], end[i] + ops[j]["l"] + HOP + back * ops[j].get("b", 0.0)); left[j] -= 1
                 if left[j] == 0: pool.add(j)
         return end
     best = None
@@ -179,10 +205,10 @@ def _plan(ops, users):
         for i in range(n - 1, -1, -1):
             pl[i] = min(c for f, c in ops[i]["a"].values()) + ops[i]["l"] + HOP + max([pl[j] for j in succ[i]], default=0.0) + ahead * ops[i].get("b", 0.0)
         first = forward(pl, MARG)
-        for marg in MARG2:
+        for marg, back in MARG2:
             cur = first
             for k in range(PASSES):
-                cur = forward(backward(cur[2], cur[5]), marg)
+                cur = forward([x + RUSH * o.get("r", 0) for x, o in zip(backward(cur[2], cur[5], back), ops)], marg)
                 if best is None or cur[0] < best[0]: best = cur
     return best
 
@@ -222,6 +248,7 @@ def rank_program(g, core, T, topo):
 
     def add(alts, R, Wr, lat=0.0, sem=None, cnt=1):
         i, deps, eng, new = len(ops), set(), "".join(alts), None
+        if "v" in alts: alts["v"] = (alts["v"][0], alts["v"][1] * VF + VO)
         for t in list(R) + list(Wr):
             if t in lastw: deps.add(lastw[t])
             if t[0] == "#":
@@ -269,7 +296,7 @@ def rank_program(g, core, T, topo):
 
     def sign(out, a, R, Wr): add({"v": vts(out, a, -1.0, 1.0, AL.max, AL.min), "a": aac(out, a, AF.Sign)}, R, Wr)
 
-    def fne(out, a, R, Wr): add({"v": vts(out, a, 0.0, None, AL.not_equal, None, 0.5), "a": aac(out, a, AF.Abs)}, R, Wr)
+    def fne(out, a, R, Wr, both=True): add({"v": vts(out, a, 0.0, None, AL.not_equal, None, 0.5), **({"a": aac(out, a, AF.Abs)} if both else {})}, R, Wr)
 
     def ms(out, c, Wr, cy=1.0): add({"v": (lambda: vec.memset(out, c), cv(out, cy))}, [], Wr)
 
@@ -281,12 +308,12 @@ def rank_program(g, core, T, topo):
         def f():
             for n, (o, l, r) in enumerate(trips): x = ten.matmul(rs(o), l, r, st and n == 0, sp and n == len(trips) - 1)
             return x
-        add({"t": (f, sum(0.016 + max(64, nel(o)) * (4 if "float32" in str(l.dtype) else 1) * PEC for o, l, r in trips))}, R, Wr, 0.05)
+        add({"t": (f, sum(POV + max(PMIN, nel(o)) * (4 if "float32" in str(l.dtype) else 1) * PEC for o, l, r in trips))}, R, Wr, 0.05)
 
     def io(out, pat, base, cm, Wr, fl=True):
         if fl: f = lambda: g.iota(out, pat, base, cm, allow_small_or_imprecise_dtypes=True)
         else: f = lambda: g.iota(out, pat, base, cm)
-        add({"g": (f, 0.13 + 2 * nel(out) * CY)}, [], Wr)
+        add({"g": (f, 0.13 + GOV + 2 * nel(out) * CY)}, [], Wr)
     nd = [0]
 
     def dma(q, prs, R, Wr, lat=2.5):
@@ -338,18 +365,17 @@ def rank_program(g, core, T, topo):
 
     def tk(n, xs): return ["%s_%d" % (n, x) for x in xs]
 
-    def send_g(r): send(T["Gw%d" % r], [0], "ar%d" % (2 * r), tk("Gw%d" % r, (0, 1)), ["Gw%dr" % r], RLAT - 2 + 2 * r)
+    def send_g(r): send(T["Gw%d" % r], [0], "ar%d" % (2 * r), tk("Gw%d" % r, (0, 1)), ["Gw%dr" % r], RLAT1 if r else RLAT)
 
-    def send_b(r): send(T["W%d" % r], [LUTW + WN * c for c in range(3)], "ar%d" % (2 * r + 1), tk("W%d" % r, range(6)), ["W%dr" % r], RLAT)
+    def send_b(r): send(T["W%d" % r], [LUTW + WN * c for c in range(3)], "ar%d" % (2 * r + 1), tk("W%d" % r, range(6)), ["W%dr" % r], (RLAT1 if r else RLAT) + 2)
 
-    dma("s", [(T.LI[f::16, :], T.leaf0[:, f * V:(f + 1) * V]) for f in range(8)], [], ["LIa"])
+    dma("s", [(T.LI[f::16, :], T.leaf0[:, f * V:(f + 1) * V]) for f in range(8)], [], ["LIa"], LLAT)
     dma("a", [(T.LI[f::16, :], T.leaf0[:, f * V:(f + 1) * V]) for f in range(8, 12)] +
-        [(T.LI[13 + c::16, :], T.tab0[:, c * V:(c + 1) * V]) for c in range(3)] + [(T.fanI[:], T.fan[:])], [], ["LIb", "fanI"])
+        [(T.LI[13 + c::16, :], T.tab0[:, c * V:(c + 1) * V]) for c in range(3)] + [(T.fanI[:], T.fan[:])], [], ["LIb", "fanI"], LLAT)
     io(T.PI[:, 0:1], [[0, 1]], 0, 1, ["PI"], False)
-    io(T.IDI[:], [[1, V]], V * rank, 0, ["IDI"], False)
-    dma("s", [(T.LI[12::16, :], T.IDI[12::16, :])], ["IDI"], ["LIc"], 3.0)
-    ops[-1]["b"] = 900.0
-    dma("s", [(T.TR[m::16], T.tab0[:]) for m in range(16)] + [(T.RQ[:], T.req[:])], ["IDI"], ["TR", "RQ"], 6.0)
+    for h in range(2):
+        io(T.IDI[:, h * BORD:(h + 1) * BORD], [[1, BORD]], V * rank + h * BORD, 0, ["IDI" + "0" * (1 - h)], False)
+        dma("s", [(T.LI[12::16, h * BORD:(h + 1) * BORD], T.IDI[12::16, h * BORD:(h + 1) * BORD])], ["IDI" + "0" * (1 - h)], ["LIc%d" % h], LLAT)
 
     for n, (sh, an) in enumerate([(0, 15), (2, 3), (0, 3), (4, 7), (2, 31), (0, 1)]):
         ts(T.PJ[:, n:n + 1], T.PI[:, 0:1], sh, an, AL.logical_shift_right, AL.bitwise_and, ["PI"], ["PJ%d" % n])
@@ -370,20 +396,28 @@ def rank_program(g, core, T, topo):
     for n, (at, x, y) in V2_.items(): faff(vc(n), vc("f%d" % at), float(y - x), float(x), vt("f%d" % at), vt(n))
     for n, o, x, y in [("le12", AL.is_le, 12.0, 1.0), ("le12n", AL.is_le, 12.0, -1 / DL), ("is13", AL.is_equal, 13.0, 1.0), ("is14", AL.is_equal, 14.0, 0.5),
                        ("is0", AL.is_equal, 0.0, 524288.0), ("is1", AL.is_equal, 1.0, -1 / 32)]: co(n, p16, x, y, o, AL.mult, ["PF0"])
-    faff(vc("p256"), p16, 16.0, 0.0, ["PF0"], vt("p256")); faff(vc("bX"), odd, 2048.0, -2048.0, PF, vt("bX"))
+    faff(vc("p16s"), p16, 1 / 256, 0.0, ["PF0"], vt("p16s"))
+    faff(vc("p256"), p16, 16.0, -4096.0, ["PF0"], vt("p256")); faff(vc("bX"), odd, 2048.0, -2048.0, PF, vt("bX"))
     co("lo2", lc, 2.0, None, AL.is_lt, None, PF); co("hi2", lc, 2.0, None, AL.is_ge, None, PF)
     co("c8", kc, 2.0, -4.0, AL.min, AL.mult, PF); co("c8", vc("c8"), p16, None, AL.add, None, PF + vt("c8"))
     io(T.GI[:], [[1, 32]], 0, 0, ["GI"])
     ts(T.GM[:], T.GI[:, 0:8], gc_, None, AL.is_equal, None, ["GI"] + PF, ["GM"])
-    faff(T.GN[:], T.GM[:], -1.0, 0.0, ["GM"], ["GN"]); faff(T.GNF[:], T.GM[:], -1.0, 0.0, ["GM"], ["GNF"])
-    ms(T.RST[:], 1.0, ["RST"]); ms(T.RST[:, 0::16], 0.0, ["RST"]); ms(T.RS8[:], 1.0, ["RS8"]); ms(T.RS8[:, 0::8], 0.0, ["RS8"])
+    faff(T.GN[:], T.GM[:], -1.0, 0.0, ["GM"], ["GN"])
+    if not SCAN: faff(T.GNF[:], T.GM[:], -1.0, 0.0, ["GM"], ["GNF"])
+    ms(T.RST[:], 1.0, ["RST"]); ms(T.RST[:, 0::16], 0.0, ["RST"])
     ms(T.TWO[:, 0:16], 2.0, ["TWO"]); ms(T.TWO[:, 16:32], 0.5, ["TWO"]); ms(T.POWR[:, 32:48], 0.0, ["ZR"])
-    io(T.PIW[:], [[4, 8], [1, 4], [0, 4]], 0, 0, ["PIW"]); io(T.PIW[:, 2::4], [[4, 8], [0, 4]], 3, 0, ["PIW"])
-    io(T.PJW[:], [[4, 8], [0, 4], [1, 4]], 0, 0, ["PJW"]); io(T.PJW[:, 2::4], [[4, 8], [1, 4]], 0, 0, ["PJW"])
+    io(T.PIW[:], [[4, 8], [1, 4], [0, 4]], 0, 0, ["PIW"]); io(T.PJW[:], [[4, 8], [0, 4], [1, 4]], 0, 0, ["PJW"])
+    fcp(T.PJW[:, 2::4], T.PIW[:, 2::4], ["PIW"], ["PJW"]); fcp(T.PIW[:, 2::4], T.PJW[:, 3::4], ["PJW"], ["PIW"])
     for q in (12, 13, 14):
-        io(T.PIW[:, q::16], [[4, 8]], SI[q], 0, ["PIW"]); io(T.PJW[:, q::16], [[4, 8]], SJ[q], 0, ["PJW"])
+        faff(T.PIW[:, q::16], T.PIW[:, 0::16], 1.0, float(SI[q]), ["PIW"], ["PIW"]); faff(T.PJW[:, q::16], T.PJW[:, 0::16], 1.0, float(SJ[q]), ["PJW"], ["PJW"])
     vtk = []
-    for a0, cov in zip((0, 72, 80), VCOVER):
+    if VS:
+        vtk.append(["VAL%d" % y[0] for y in VRUNS])
+        ms(T.VAL[:, 0:72], 0.0, ["VAL"])
+        for s, st, n, x in VRUNS:
+            o = T.VAL[:, s:s + (n - 1) * st + 1:st]
+            add({"v": (lambda o=o, x=x: vec.memset(o, x), cv(o, 1)), "a": aac(o, T.TWO[:, 0:n], AF.Identity, x, 0.0)}, ["VAL", "TWO"], ["VAL%d" % s])
+    for a0, cov in list(zip((0, 72, 80), VCOVER))[VS:]:
         vtk.append(["VAL%d" % (a0 + y[0]) for y in cov])
         for s, n, pat, base in cov: io(T.VAL[:, a0 + s:a0 + s + n], pat, base, 0, ["VAL%d" % (a0 + s)])
     io(T.OHI[:], [[0, 10], [1, 8]], 0, 0, ["OHI"])
@@ -391,7 +425,7 @@ def rank_program(g, core, T, topo):
                                      (80, 32, kc, 1 / 128, T.VAL[:, 0:32], vtk[0], "VCk")):
         ts(T.OH[:, a0:a0 + n], T.OHI[:, 0:n], ft, x, AL.is_equal, AL.mult, ["OHI"] + PF + vt("c8"), ["OH" + tok])
         tt(T.PR[:, a0:a0 + n], T.OH[:, a0:a0 + n], va, AL.mult, ["OH" + tok] + R, ["PR" + tok])
-        scan(T.VC[:, a0:a0 + n], T.RS8[:, 0:n], T.PR[:, a0:a0 + n], 0.0, AL.mult, AL.add, ["PR" + tok, "RS8"], [tok])
+        scan(T.VC[:, a0:a0 + n], T.RST[:, 0:2 * n:2], T.PR[:, a0:a0 + n], 0.0, AL.mult, AL.add, ["PR" + tok, "RST"], [tok])
     for a0 in (112, 128): ts(T.OH[:, a0:a0 + 16], T.GI[:, 0:16], p16, None, AL.is_equal, None, ["GI", "PF0"], ["OH%d" % a0])
     oh, OHT = T.OH[:, 112:144], ["OH112", "OH128"]
     tt(T.PR[:, 112:128], T.OH[:, 112:128], T.PIW[:, 0:16], AL.mult, OHT + ["PIW"], ["PRa"])
@@ -410,34 +444,46 @@ def rank_program(g, core, T, topo):
     co("w2hi", w2m, 16.0, w2m, AL.is_ge, AL.mult, ["PWa"]); co("w2lo", w2m, 200.0, w2m, AL.is_le, AL.mult, ["PWa"])
 
     for h in range(2):
-        x = T.LI[:, h * BORD:(h + 1) * BORD]
-        faff(x, x, vc("mul"), vc("off"), ["LIa", "LIb", "LIc"] + vt("mul", "off"), ["LI%d" % h])
+        x, y = T.LJ[:, h * BORD:(h + 1) * BORD], T.LI[:, h * BORD:(h + 1) * BORD]
+        fcp(T.TF[:, h * BORD:(h + 1) * BORD], y, ["LIa", "LIb", "LIc%d" % h], ["TF%d" % h])
+        faff(x, y, vc("mul"), vc("off"), ["LIa", "LIb", "LIc%d" % h] + vt("mul", "off"), ["LI%d" % h])
         ts(x, x, 4095, None, AL.bitwise_and, None, ["LI%d" % h], ["LI%d" % h])
         frelu(T.Gw0[:, h * BORD:(h + 1) * BORD], x, vc("sub"), ["LI%d" % h] + vt("sub"), tk("Gw0", (2 * h, 2 * h + 1)))
     send_g(0)
+    faff(T.PW[:, 0:128], T.RST[:, 0:128], 0.5, 0.0, ["RST"], ["PW0"]); faff(T.PW[:, 128:256], T.RST[:, 0:128], -32768.0, 32768.0, ["RST"], ["PW1"])
+    scan(T.PW[:, 256:384], T.PW[:, 0:128], T.PW[:, 128:256], 0.0, AL.mult, AL.add, ["PW0", "PW1"], ["PW2"])
+    for c in range(3):
+        add({"g": (lambda c=c: g.affine_select(T.BT3[:, 128 * c:128 * c + 128], T.PW[:, 256:384], [[16, 8], [0, 16]], AL.is_equal, 0.0, 13 + c, -1), 0.39 + GOV)},
+            ["PW2"], ["BT3_%d" % c])
     for h in range(2):
         x, a0 = T.TR[:, :, h * BORD:(h + 1) * BORD], LUTW + h * BORD
-        faff(x, x, w15, 0.0, ["TR", "PWa"], ["TR%d" % h])
-        ts(x, x, 32768, None, AL.bitwise_and, None, ["TR%d" % h], ["TR%d" % h])
+        for cs in ((0, 1), (2,)):
+            pb = tile()
+            for u, c in enumerate(cs): mm([(ps(pb, u * BORD, (u + 1) * BORD), T.BT3[:, 128 * c:128 * c + 128], T.TF[:, h * BORD:(h + 1) * BORD])], ["BT3_%d" % c, "TF%d" % h], [pb])
+            for u, c in enumerate(cs): fcp(T.TR[:, c, h * BORD:(h + 1) * BORD], ps(pb, u * BORD, (u + 1) * BORD), [pb], ["TR%d_%d" % (h, c)])
+        ts(x, x, 32768, None, AL.bitwise_and, None, tk("TR%d" % h, range(3)), ["TR%d" % h])
         for c in range(3):
             faff(T.W0[:, a0 + WN * c:a0 + WN * c + BORD], T.TR[:, c, h * BORD:(h + 1) * BORD], 1 / 32768, 0.0, ["TR%d" % h], tk("W0", (6 * h + c, 6 * h + 3 + c)))
     send_b(0)
     fcp(T.fanU[:], T.fanI[:], ["fanI"], ["fanU"])
-    faff(T.IDf[:], T.IDI[:], -1.0, 2048.0, ["IDI"], ["IDf"])
+    io(T.IDf[:], [[-1, V]], 2048 - V * rank, 0, ["IDf"])
     add({"g": (lambda: g.sem_inc(T.sem.go, 1), 0.05)}, ["sent"], ["go"], 0.0, "go", 1)
-    dma("s", [(T.CE[:, 0:CE0], T.cells[:, 4096 - CE0:]), (T.CE[:, CE0:CE0 + 4096], T.cells[:]),
-              (T.CE[:, CE0 + 4096:], T.cells[:, 0:CEW - CE0 - 4096])], ["go"], ["CE"], 14.0)
+    dma("s", [(T.RQ[:], T.req[:]), (T.CE[:, 0:CE0], T.cells[:, 4096 - CE0:]), (T.CE[:, CE0:CE0 + 4096], T.cells[:]),
+              (T.CE[:, CE0 + 4096:], T.cells[:, 0:CEW - CE0 - 4096])], ["go"], ["CE", "RQ"], 14.0)
     for b in sorted({u * GW // 128 for r, u in folds()}):
         for q in P16:
             o, x = T.RP[:, 2048 * b + q:2048 * (b + 1):16], T.RQ[:, 128 * b:128 * b + 128]
             add({"g": (lambda o=o, x=x: g.affine_select(o, x, [[0, 128]], AL.is_ge, 0.0, 0, 0), 0.39)}, ["RQ"], ["RP%d_%d" % (q, b)])
-    faff(T.IW[:, 0:V], T.IDI[:], 1.0, -1.0 * V * rank, ["IDI"], ["IW0"])
-    for a0 in (V, 2 * V): faff(T.IW[:, a0:min(WN, a0 + V)], T.IW[:, 0:min(V, WN - a0)], 1.0, float(a0), ["IW0"], ["IW%d" % a0])
+    for a0 in (0, V, 2 * V): io(T.IW[:, a0:min(WN, a0 + V)], [[1, min(V, WN - a0)]], a0, 0, ["IW%d" % a0])
     fcp(T.Gc[:], T.IW[:].indirect(T.fanU[:]), ["IW0", "IW512", "IW1024", "fanU"], ["Gc"], GC)
-    bankof["rq"] = 7
-    fcp(ps("rq", 0, V), T.RQ[:], ["RQ"], ["rq"])
+    if SCAN: ms(T.D0[:, 0::2], 0.0, ["D0z"], 0.5)
+    else:
+        bankof["rq"] = 7
+        fcp(ps("rq", 0, V), T.RQ[:], ["RQ"], ["rq"])
 
-    for k, n in enumerate(PN):
+    io(T.PH[:, 0:3, :], [[4, 3], [1, 4], [0, 4]], 0, 0, ["PHSA%d_0" % i for i in range(3)])
+    io(T.PH[:, 3:6, :], [[4, 3], [0, 4], [1, 4]], 0, 0, ["PHSB%d_0" % i for i in range(3)])
+    for k, n in list(enumerate(PN))[6:]:
         for s, x, pat, base in COVER[n]: io(T.PH[:, k, s:s + x], pat, base, 0, ["PH%s_%d" % (n, s)])
 
     def P_(n, a=0, b=16, st=1): return T.PH[:, PN.index(n), a:b:st], ["PH%s_%d" % (n, y[0]) for y in COVER[n]]
@@ -472,9 +518,9 @@ def rank_program(g, core, T, topo):
     eqm(mf("XP", 2, 12, 4), P_("COL", 3, 12, 4), p16, 2048.0); eqm(mf("XP", 3, 12, 4), P_("COL", 3, 12, 4), p16, -2048.0)
     si, sj = (T.PIW[:, 0:16], ["PIW"]), (T.PJW[:, 0:16], ["PJW"])
     eqm(mf("XA"), si, kc, vc("lo2"), vt("lo2")); eqm(mf("XB"), sj, kc, vc("hi2"), vt("hi2")); eqm(mf("I256"), P_("COL"), p16, 256.0)
-    eqm(mf("RMa"), P_("CK"), vc("si"), 16.0, vt("si")); eqm(mf("RMb", 0, 13), P_("CK", 0, 13), vc("sj"), 16.0, vt("sj"))
+    eqm(mf("RMa"), P_("SA0"), vc("si"), 16.0, vt("si")); eqm(mf("RMb", 0, 13), P_("SA0", 0, 13), vc("sj"), 16.0, vt("sj"))
     ms(mf("RMb", 14, 15)[0], -1 / 128, ["MFRMb"])
-    eqm(mf("EA"), P_("CK"), lc, 1 / DL); eqm(tm(0, 16), P_("CL"), lc, vc("le12n"), vt("le12n"))
+    eqm(mf("EA"), P_("SA0"), lc, 1 / DL); eqm(tm(0, 16), P_("SB0"), lc, vc("le12n"), vt("le12n"))
     faff(mf("EB")[0], tm(0, 16)[0], 1.0, vc("is14"), ["TM0"] + vt("is14"), ["MFEB"])
     eqm(mf("HA", 0, 6), P_("HK", 0, 6), lc, 1.0)
     eqm((T.TM[:, 16:22], "TM16"), P_("HK", 0, 6), lc, vc("le12"), vt("le12")); eqm((T.TM[:, 22:26], "TM16"), P_("COL", 0, 4), lc, vc("le12"), vt("le12"))
@@ -485,10 +531,11 @@ def rank_program(g, core, T, topo):
     eqm(mf("He", 12, 16), P_("COL", 0, 4), lc, 4096.0)
     eqm(mf("UH", 8, 11), P_("COL", 0, 3), vc("zrow"), 1.0, vt("zrow")); col(mf("UH", 11, 12), vc("u3"), vt("u3"))
     ms(mf("UA", 11, 12)[0], 1.0, ["MFUA"]); col(mf("UE", 15), vc("is14"), vt("is14"), -65536.0)
-    eqm(mf("E12", 12, 13), P_("RID", 0, 1), p16, 1.0); col(mf("LP", 15), p16, PF, 1 / 256)
+    eqm(mf("E12", 12, 13), P_("RID", 0, 1), p16, 1.0); eqm(mf("LP", 3, 16, 4), P_("RID", 0, 4), 12.0, vc("p16s"), vt("p16s"))
     if "Zc1" in BN: col(mb("Zc1", 15), vc("nwc1"), vt("nwc1")); col(mb("Zc2", 15), vc("w2hi"), vt("w2hi"), -1 / 16)
     col(mb("Zlb", 15), vc("w2lo"), vt("w2lo"), 16.0); col(mb("ZT", 15), w2m, ["PWa"])
-    eqm(mb("IV"), P_("COL"), p16, -524288.0); eqm(mb("ID"), P_("COL"), p16, 1.0); eqm(mb("IDn"), P_("COL"), p16, -1.0)
+    eqm(mb("IV"), P_("COL"), p16, -524288.0)
+    if not SCAN: eqm(mb("ID"), P_("COL"), p16, 1.0); eqm(mb("IDn"), P_("COL"), p16, -1.0)
     for n in NFV: ms(mb("ONE%d" % n, 0, 16 - n)[0], 1.0, ["MBONE%d" % n])
     faff(tm(66, 16)[0], si[0], 4.0, 32.0, si[1], ["TM66"]); plus(tm(66, 16), tm(66, 16), (sj[0], "PJW"))
     faff(mb("KC")[0], tm(66, 16)[0], vc("is1"), vc("is0"), ["TM66"] + vt("is0", "is1"), ["MBKC"])
@@ -503,7 +550,7 @@ def rank_program(g, core, T, topo):
                     continue
                 for base, cm in [(-16 * q, 1)] * (q > 0) + [(16 * q + 15, -1)] * (q < 7):
                     add({"g": (lambda dst=dst, src=src, base=base, cm=cm: g.affine_select(dst, src, [[0, nel(dst)]], AL.is_ge, 0.0, base, cm),
-                               0.17 + 2 * nel(dst) * CY)}, R, Wr)
+                               0.17 + GOV + 2 * nel(dst) * CY)}, R, Wr)
                     src, R = dst, Wr
             TK[tag + str(gi)] = ["B%s%d_%d" % (tag, gi, q) for q in range(8)] + ["B%sz" % tag]
             o += len(ns)
@@ -512,28 +559,31 @@ def rank_program(g, core, T, topo):
 
     def LB(n, s=0): return T.BB[:, BN.index(n), s:s + 128]
     F0, F1, F2, B0, B1 = [TK[x] for x in ("F0", "F1", "F2", "B0", "B1")]
-    for n, x in enumerate(["kA1", "kA2", "A1", "A2", "kN1", "kN2", "N1", "N2"]):
+    for n, x in enumerate(["kA2", "kA1", "A1", "A2", "kN2", "kN1", "N1", "N2"]):
         ts(T.W2[:, 8 * n:8 * n + 8], T.GM[:], vc(x), 1.0 - 2 * (n < 2), AL.mult, AL.mult, ["GM"] + vt(x), ["W2_%d" % n])
     fcp(T.W2[:, 64:72], T.GM[:], ["GM"], ["W2_8"])
     if max(sum(BT, [])):
         co("wlo", p16, 10.0, vc("nwc1"), AL.is_le, AL.mult, PF + vt("nwc1")); co("whi", p16, 10.0, vc("nwc1"), AL.is_gt, AL.mult, PF + vt("nwc1"))
         for n, (x, y) in enumerate((("w2hi", -1 / 16), ("wlo", 1.0), ("whi", 1.0))):
             ts(T.W3[:, 8 * n:8 * n + 8], T.GM[:], vc(x), y, AL.mult, AL.mult, ["GM"] + vt(x), ["W3"])
-    for n, x in enumerate(["nA1", "nA2", 0.5, "N1", "N2", 0.5, 1.0]):
+    for n, x in enumerate(["nA2", "nA1", 0.5, 1, 0, "N2", "N1", 2, 6, 5, 1.0]):
         c_ = isinstance(x, str)
-        ts(T.W9[:, 32 * n:32 * n + 32], T.GI[:], p4, vc(x) if c_ else x, AL.is_equal, AL.mult, ["GI"] + PF + (vt(x) if c_ else []), ["W9_%d" % n])
+        if isinstance(x, int): fcp(T.W9[:, 32 * n:32 * n + 32], T.W9[:, 32 * x:32 * x + 32], ["W9_%d" % x], ["W9_%d" % n])
+        else: ts(T.W9[:, 32 * n:32 * n + 32], T.GI[:], p4, vc(x) if c_ else x, AL.is_equal, AL.mult, ["GI"] + PF + (vt(x) if c_ else []), ["W9_%d" % n])
 
     def wide(n, a0, pn, s, st, x): ts(T[n][:, a0 + s:a0 + 128:st], T[pn][:, s::st], p4, vc(x), AL.is_equal, AL.mult, [pn] + PF + vt(x), [n + str(a0)])
     for a0, x in ((0, "cA"), (128, "cB")):
-        wide("PA", a0, "PIW", 0, 1, x + "f"); wide("PA", a0, "PIW", 3, 4, x + "t")
+        wide("PA", 128 - a0, "PIW", 0, 1, x + "f"); wide("PA", 128 - a0, "PIW", 3, 4, x + "t")
         wide("PB", a0, "PJW", 0, 1, x + "f"); wide("PB", a0, "PJW", 2, 4, x + "t"); wide("PB", a0, "PJW", 14, 16, x + "f")
     for n, pn in (("PAV", "PIW"), ("PBV", "PJW")):
         wide(n, 0, pn, 0, 1, "cV"); ms(T[n][:, 15::16], 0.0, [n + "0"])
-    WT = tk("W2", range(9)) + tk("W9", range(7)) + ["PA0", "PA128", "PB0", "PB128", "PAV0", "PBV0"]
-    ms(T.ON[:], 1.0, ["ON"], 0.5); ms(T.ONH[:], 1.0, ["ONH"], 0.5); ms(T.ONF[:], 1.0, ["ONF"])
+    WT = tk("W2", range(9)) + tk("W9", range(11)) + ["PA0", "PA128", "PB0", "PB128", "PAV0", "PBV0"]
+    for n in ("ON", "ONH", "ONF"): io(T[n][:], [[0, 128]], 1, 0, [n])
     add({"g": (lambda: g.affine_select(T.IDN[:], T.ONF[:], [[-1, 128]], AL.is_equal, 0.0, 0, 1), 0.4)}, ["ONF"], ["IDN"])
     io(T.BCI[:], [[16, 16]], 15, 0, ["BCI"], False); cp(T.BC[:], T.BCI[:], ["BCI"], ["BC"])
-    for w in sorted(set(sum(CH, []))): io(T.CV[0:1, 3 * w // 16:6 * w // 16], [[0, 3], [256, w // 16]], 0, 0, ["CV%d" % w])
+    io(T.CV[0:1, 0:96], [[0, 3], [256, 8], [0, 4]], 0, 0, ["CV"]); io(T.CV[0:4, 96:192], [[0, 96]], 4096, 0, ["CV"])
+    add({"g": (lambda: g.affine_select(T.CV[0:4, 96:192], T.CV[0:4, 96:192], [[0, 24], [1, 4]], AL.is_equal, 0.0, 0, -1), 0.35 + GOV)}, [], ["CV"])
+    add({"g": (lambda: g.affine_select(T.IND[0:4, :], T.ONH[0:4, :], [[0, 8], [1, 4], [0, 4]], AL.is_equal, 0.0, 0, -1), 0.4 + GOV)}, ["ONH"], ["IND"])
 
     faff(T.BYI[:], T.IW[:, 0:256], w15, 0.0, ["IW0", "PWa"], ["BYI"])
     ts(T.BYI[:], T.BYI[:], 32768, None, AL.bitwise_and, None, ["BYI"], ["BYI"])
@@ -543,7 +593,7 @@ def rank_program(g, core, T, topo):
         for u in range(2): mm([(ps(pb, 256 * u, 256 * u + 256), LB("LUT%d" % (2 * q + u)), T.BYB[:])], B0 + ["BYB"], [pb])
         fcp(T.W0[:, 512 * q:512 * q + 512], ps(pb, 0, 512), [pb], ["LUT%d" % q])
     LUT0 = ["LUT%d" % q for q in range(7)]
-    dma("s", [(T.W1[:, 0:LUTW], T.W0[:, 0:LUTW])], LUT0, ["LUTc"], 8.0)
+    dma("s", [(T.W1[:, 0:LUTW], T.W0[:, 0:LUTW])], LUT0 + ["CE", "W0r"], ["LUTc"], 8.0)
 
     def groups(n, w): return [list(range(a, min(n, a + 512 // w))) for a in range(0, n, 512 // w)]
 
@@ -570,14 +620,17 @@ def rank_program(g, core, T, topo):
             ts(Ga, Gw[:].indirect(T.fanU[:, v0 // 16:(v0 + w) // 16]), MG * r, vc("dcol"), AL.subtract, AL.max, gw + vt("dcol"), ga, GC)
             faff(Gb, Gw[:].indirect(T.fanU[:, (V + v0) // 16:(V + v0 + w) // 16]), 1.0, -MG * r, gw, gb, GC)
             ts(blk(T.PP, 2, 0, 2), blk(T.GG, 2, 0, 2), 0.5, None, AL.is_ge, None, ga + gb, pp, 0.5)
-            for bs in groups(11, w):
-                pb = tile() + "a"
+            chain = CHAIN[v0 // 128] and w == 128
+            for bs in ([[9, 10], [0, 1, 2], [3, 4, 5], [6, 7, 8]] if chain else groups(11, w)):
+                if not (chain and bs[0] in (3, 6)): pb = tile() + "a"
                 for u, x in enumerate(bs):
                     l = ("SA%d" % SI[FULL[x]], "SB%d" % SJ[FULL[x]]) if x < 9 else (("I13", "R13") if x == 9 else ("R12", "I12"))
                     o = ps(pb, u * w, u * w + w)
-                    mm([(o, LF(l[0]), Ga), (o, LF(l[1]), Gb)], F0 + ga + gb, [pb])
+                    if chain and 2 < x < 9: mm([(o, LF("SD%d" % (x // 3)), Gb)], F0 + gb, [pb], False, True)
+                    elif chain and x < 3: mm([(o, LF(l[0]), Ga), (o, LF(l[1]), Gb)], F0 + ga + gb, [pb], x == 0, x == 2)
+                    else: mm([(o, LF(l[0]), Ga), (o, LF(l[1]), Gb)], F0 + ga + gb, [pb])
                 sign(blk(T.SG, 11, bs[0], len(bs)), ps(pb, 0, len(bs) * w), [pb], ts_("SG", bs))
-                fne(blk(T.NE, 11, bs[0], len(bs)), blk(T.SG, 11, bs[0], len(bs)), ts_("SG", bs), ts_("NE", bs))
+                fne(blk(T.NE, 11, bs[0], len(bs)), blk(T.SG, 11, bs[0], len(bs)), ts_("SG", bs), ts_("NE", bs), NEA[v0 // 128])
             pb = tile()
             o = ps(pb, 0, w)
             mm([(o, LF("XC", 2), T.Gc[:, v0:v0 + w]), (o, LF("XC"), T.Gc[:, V + v0:V + v0 + w]), (o, LF("XL", 2), Ga), (o, LF("XL"), Gb),
@@ -591,18 +644,17 @@ def rank_program(g, core, T, topo):
 
                 def ne(x): return sub(T.NE, 11, x, b)
                 parts = [([(ps(pb, 0, 256), sub(T.PP, 2, 0, b), T.PA[:, 0:256]), (ps(pb, 256, 512), sub(T.PP, 2, 1, b), T.PB[:])], [])]
-                for xs in ((0, 1, 2, 3), (4, 5, 6, 7), (8,)):
+                for xs in (((0, 1, 2), (3, 4, 5), (6, 7, 8)) if chain else ((0, 1, 2, 3), (4, 5, 6, 7), (8,))):
                     parts.append((sum([[(ps(pb, FULL[x], 512, 16), sg(x), W2[:, 0:32]), (ps(pb, FULL[x], 512, 16), ne(x), W2[:, 32:64])] for x in xs], []), xs))
-                for x, own, oth in ((9, ps(pb, 3, 256, 4), ps(pb, 259, 384, 4)), (10, ps(pb, 258, 512, 4), ps(pb, 2, 128, 4))):
-                    parts[-1] = (parts[-1][0] + [(own, sg(x), W9[:, 0:64]), (oth, sg(x), W9[:, 64:96]), (own, ne(x), W9[:, 96:160]),
-                                                 (oth, ne(x), W9[:, 160:192])], parts[-1][1] + (x,))
+                for x, o, c0 in ((9, ps(pb, 3, 384, 4), 0), (10, ps(pb, 130, 512, 4), 64)):
+                    parts[-1] = (parts[-1][0] + [(o, sg(x), W9[:, c0:c0 + 96]), (o, ne(x), W9[:, 160 + c0:256 + c0])], parts[-1][1] + (x,))
                 parts = [(parts[0][0] + parts[1][0], parts[1][1])] + parts[2:]
                 for n, (tr, xs) in enumerate(parts): mm(tr, WT + pp + ts_("SG", xs) + ts_("NE", xs), [pb], n == 0, n == len(parts) - 1)
                 frelu(T.XT[:, 512 * bl[b]:512 * bl[b] + 512], ps(pb, 0, 512), 0.0, [pb], ["XT_%d" % bl[b]])
                 a0 = 128 * b
                 mm([(ps(pv, a0, a0 + 128), sub(T.PP, 2, 0, b), T.PAV[:]), (ps(pv, a0, a0 + 128), sub(T.PP, 2, 1, b), T.PBV[:])] +
                    [(ps(pv, a0 + FULL[x], a0 + 128, 16), ne(x), W2[:, 64:72]) for x in range(9)] +
-                   [(ps(pv, a0 + 12 - x, a0 + 128, 4), ne(x), W9[:, 192:224]) for x in (9, 10)], WT + pp + ts_("NE", range(11)), [pv])
+                   [(ps(pv, a0 + 12 - x, a0 + 128, 4), ne(x), W9[:, 320:352]) for x in (9, 10)], WT + pp + ts_("NE", range(11)), [pv])
             frelu(blk(T.VT, 1, 0), ps(pv, 0, w), -4.0, [pv], t_("VT"))
             pb = tile()
             mm([(ps(pb, u * w, u * w + w), LF("X" + x), blk(T.XX, 1, 0)) for u, x in enumerate("AB")], F1 + t_("XX"), [pb], True, False)
@@ -618,8 +670,10 @@ def rank_program(g, core, T, topo):
             wt = tk("W%d" % r, range(12)) + ["W%dr" % r] + (LUT0 if r == 0 else ["LUTc"])
             for u in gws:
                 a0 = 2 * v0 + GW * u
-                fcp(T.AG[:, big(u)], Wt[:].indirect(T.IX[:, a0:a0 + GW]), wt + t_("IX"), gt("AG", [u]) + ts_("XM", P16), GC)
-                tt(T.AN[:, big(u)], Wt[:].indirect(T.IX[:, a0 + w:a0 + w + GW]), T.AG[:, big(u)], AL.mult, wt + t_("IX") + gt("AG", [u]), gt("AN", [u]), GC)
+                y = (v0 // GW + u) % (256 // GW)
+                ag, agt = (T.AG[:, 16 * GW * y:16 * GW * (y + 1)], ["AG_%d" % y]) if SCAN else (T.AG[:, big(u)], gt("AG", [u]))
+                fcp(ag, Wt[:].indirect(T.IX[:, a0:a0 + GW]), wt + t_("IX"), agt + ts_("XM", P16), GC)
+                tt(T.AN[:, big(u)], Wt[:].indirect(T.IX[:, a0 + w:a0 + w + GW]), ag, AL.mult, wt + t_("IX") + agt, gt("AN", [u]), GC)
             for b in range(nb):
                 a0, us = 16 * (v0 + 128 * b), range(128 * b // GW, 128 * (b + 1) // GW)
                 if BT[r][bl[b]] == 2:
@@ -634,7 +688,7 @@ def rank_program(g, core, T, topo):
                     pb, ct, c0 = tile(), "CT%d" % (bl[b] % 2), 384 * (bl[b] % 2)
                     for q0 in (0, 8):
                         add({"t": (lambda pb=pb, q0=q0, a0=a0: [ten.matmul(rs(ps(pb, q, 384, 16)), T.AN[:, a0 + q:a0 + 2048:16], T.W3[:], True, True)
-                                                                for q in range(q0, q0 + 8)][-1], 8 * (0.016 + 64 * PEC))}, ["W3"] + gt("AN", us), [pb], 0.05)
+                                                                for q in range(q0, q0 + 8)][-1], 8 * (POV + PMIN * PEC))}, ["W3"] + gt("AN", us), [pb], 0.05)
                     faff(T.CT[:, c0:c0 + 384], ps(pb, 0, 384), 1.0, 2048.0, [pb], [ct])
                     for u, (ys, bi) in enumerate((((0,), 4095.0 + CE0 - 2048), ((1, 2), sum(WC1) + CE0 - 4096.0))):
                         pb = tile()
@@ -648,6 +702,28 @@ def rank_program(g, core, T, topo):
         key = []
 
         def stage_c():
+            if SCAN:
+                pb = tile()
+                key.append(pb)
+                for b in range(nb):
+                    p, us = bl[b] % RD, range(128 * b // GW, 128 * (b + 1) // GW)
+                    c0, rq = 4096 * p, T.RQ[:, v0 + 128 * b:v0 + 128 * b + 128]
+                    for q in (P16 if r == 0 or RD < 4 else []):
+                        o = T.D1[:, c0 + 2 * q + 1:c0 + 4096:32]
+                        add({"g": (lambda o=o, rq=rq: g.affine_select(o, rq, [[0, 128]], AL.is_ge, 0.0, 0, 0), 0.39)}, ["RQ"], ["DR%d_%d" % (p, q)])
+                    for u in us:
+                        a0, y = 2 * v0 + GW * u, (v0 // GW + u) % (256 // GW)
+                        s0, s1 = 32 * GW * y, c0 + 32 * GW * (u - us[0])
+                        dr = tk("DR%d" % p, P16)
+                        fcp(T.D0[:, s0 + 1:s0 + 32 * GW:2], T.CE[:].indirect(T.CX[:, a0:a0 + GW]), ["CE", "D0z"] + gt("CX0", [u]), ["D0_%d" % y], GC)
+                        fcp(T.D1[:, s1:s1 + 32 * GW:2], T.CE[:].indirect(T.CX[:, a0 + w:a0 + w + GW]), ["CE"] + dr + gt("CX1", [u]), ["D1_%d" % (s1 // 32)], GC)
+                        add({"v": (lambda s0=s0, s1=s1: vec.tensor_tensor_scan(T.DO[:, s0:s0 + 32 * GW], T.D0[:, s0:s0 + 32 * GW], T.D1[:, s1:s1 + 32 * GW], 0.0, AL.min, AL.max),
+                                   OVH + 16 * GW * CY)}, ["D0z", "D0_%d" % y, "D1_%d" % (s1 // 32)] + dr, ["DO_%d" % y])
+                    o, c0 = ps(pb, 128 * b, 128 * b + 128), 4096 * (bl[b] % 2)
+                    mm([(o, LB("IV"), sub(T.VT, 1, 0, b)), (o, rq, LB("ONE0"))], B1 + ["RQ"] + t_("VT"), [pb], True, False)
+                    mm([(ps(pb, 128 * b + q, 128 * b + 128, 16), T.DO[:, c0 + 2 * q + 1:c0 + 4096:32], T.GN[:]) for q in P16] + [(o, T.ON[:], LB("KC"))],
+                       B1 + ["GN", "ON"] + ["DO_%d" % ((v0 // GW + u) % (256 // GW)) for u in us], [pb], False, True)
+                return
             for u in gws:
                 a0, b = 2 * v0 + GW * u, (v0 + GW * u) // 128
                 fcp(T.AG[:, big(u)], T.CE[:].indirect(T.CX[:, a0:a0 + GW]), ["CE"] + gt("CX0", [u]), gt("AG", [u]), GC)
@@ -709,19 +785,20 @@ def rank_program(g, core, T, topo):
                 fcp(blk(T.MK, 3, cs[0], len(cs)), ps(pb, 0, len(cs) * w), [pb], ts_("MK", cs))
             for cs in (cgs if last and FINE > 1 else [[0, 1, 2]]):
                 pb, n, a0 = tile(), len(cs) * ns, at(T.MK, 3) + cs[0] * w
-                o = ps(pb, 0, n)
-                for x0 in range(0, 16, 4):
-                    mm([(o, T.ONH[0:1, :], T.CV[0:1, 3 * ns:3 * ns + n])] * (x0 == 0) + [(o, LF("LP", 15 - x), T.MK[:, a0 + x:a0 + len(cs) * w:16]) for x in range(x0, x0 + 4)],
-                       F2 + ["ONH", "CV%d" % w] + ts_("MK", cs), [pb], x0 == 0, x0 == 12)
+                o, ls = ps(pb, 0, 4 * n), blk(T.LS, 1, 0)
+                mm([(o, T.ONH[0:1, :], T.CV[0:1, 0:4 * n]), (o, T.IND[0:4, :], T.CV[0:4, 96:96 + 4 * n])] +
+                   [(o, LF("LP", 3 - x), T.MK[:, a0 + x:a0 + len(cs) * w:4]) for x in range(4)], F2 + ["ONH", "CV", "IND"] + ts_("MK", cs), [pb])
+                scan(T.LS[:, v0:v0 + 4 * n], T.RST[:, 0:16 * n:4], o, 0.0, AL.mult, AL.max, ["RST", pb], t_("LS"))
                 a0 = 3 * v0 // 16 + cs[0] * ns
-                faff(T.LU[:, a0:a0 + n], o, 1.0, vc("p256"), [pb] + vt("p256"), ts_("LU", cs))
+                faff(T.LU[:, a0:a0 + n], T.LS[:, v0 + 3:v0 + 4 * n:4], 1.0, vc("p256"), t_("LS") + vt("p256"), ts_("LU", cs))
             if r == 1:
                 M, s, n = T.SC[:, at(T.SC, 3) + 15:at(T.SC, 3) + 3 * w:16], slice(3 * v0 // 16, 3 * (v0 + w) // 16), 3 * ns
                 faff(T.Q5[:, s], M, 1.0, -524287.0 - MG, ts_("SC", range(3)), t_("Q5"))
                 add({"v": vts(T.Q6[:, s], M, 0.0, 524288.0, AL.is_le, AL.mult), "a": aac(T.Q6[:, s], M, AF.Relu, 524288.0, -524288.0)}, ts_("SC", range(3)), t_("Q6"))
                 pb = tile()
                 o = ps(pb, 0, 128, 1, n)
-                mm([(o, T.Q5[:, s], T.IDN[:]), (o, T.Q6[:, s], T.IDN[:])], t_("Q5") + t_("Q6") + ["IDN"], [pb])
+                tt(T.Q5[:, s], T.Q5[:, s], T.Q6[:, s], AL.add, t_("Q5") + t_("Q6"), t_("Q5"))
+                mm([(o, T.Q5[:, s], T.IDN[:])], t_("Q5") + ["IDN"], [pb])
                 faff(T.YC[0:n, v0:v0 + 128], o, -1.0, -MG, [pb], t_("YC"))
                 dma("s", [(T.yc[:, c * V + 128 * bl[b]:c * V + 128 * bl[b] + 128], T.YC[8 * (c * nb + b):8 * (c * nb + b) + 8, v0:v0 + 128])
                           for c in range(3) for b in range(nb)], t_("YC"), [])
@@ -732,6 +809,7 @@ def rank_program(g, core, T, topo):
             for c in range(3):
                 a0 = 3 * v0 // 16 + c * ns
                 faff(bits[c], T.AN[:, 16 * v0:16 * (v0 + w)].indirect(T.LU[:, a0:a0 + ns]), -1.0, 1.0, gt("AN", gws) + t_("LU", c), wn[c], GC)
+            if r == 0 and v0 + w == BORD: send_b(1)
             for cs in cgs:
                 c0, n = cs[0], len(cs)
                 for R, G, gk, x in ((T.RA, Ga, ga, "a"), (T.RB, Gb, gb, "b")):
@@ -743,7 +821,7 @@ def rank_program(g, core, T, topo):
                 pb = tile()
                 o = ps(pb, 0, n * w)
                 mm([(o, LF("EA"), ra), (o, LF("EB"), rb)], rk, [pb])
-                sign(s2, o, [pb], ts_("S2", cs)); fne(e2, s2, ts_("S2", cs), ts_("E2", cs))
+                sign(s2, o, [pb], ts_("S2", cs)); fne(e2, s2, ts_("S2", cs), ts_("E2", cs), NEA[4])
                 pb = tile()
                 o = ps(pb, 0, n * w)
                 mm([(o, LF("HA"), ra), (o, LF("HB"), rb), (o, LF("Hs"), s2)], rk + ts_("S2", cs), [pb], True, False)
@@ -760,16 +838,17 @@ def rank_program(g, core, T, topo):
                 if not last: parts = [(pr + zz[0] + hh, R + zz[1] + ts_("HH", cs))]
                 else: parts += [(pr, R), zz, (hh, ts_("HH", cs))] if cs[-1] == 2 else [(pr + hh, R + ts_("HH", cs))]
             for n, (pr, R) in enumerate(parts): mm(pr, R, [pb], n == 0, n == len(parts) - 1)
-            ops[-1]["b"] = V - v0 - w
+            ops[-1]["b"] = BV[v0 // 128]
             if r == 0:
                 faff(blk(T.Gw1, 1, 0), o, 1.0, vc("bM"), [pb] + vt("bM"), tk("Gw1", bl))
-                if v0 + w == BORD: send_g(1); send_b(1)
+                if v0 + w == BORD: send_g(1)
             else:
                 Y, YP, y = blk(T.Y, 1, 0), blk(T.YP, 1, 0), t_("Y")
                 faff(Y, o, vc("sY"), vc("bY"), [pb] + vt("bY", "sY"), y)
-                frelu(Y, Y, -MG, y, y)
-                add({"v": vts(YP, Y, 2047.5, vc("thr"), AL.is_ge, AL.mult), "a": aac(YP, Y, AF.Relu, -2049.0 * 2047, vc("thr"))}, y + vt("thr"), t_("YP"))
-                tt(Y, Y, YP, AL.subtract, y + t_("YP"), y)
+                Z = blk(T.NK0, 1, 0)
+                frelu(Z, Y, -MG, y, t_("NK0"))
+                ts(YP, Y, MG + 2048, vc("thr"), AL.is_ge, AL.mult, y + vt("thr"), t_("YP"))
+                tt(Y, Z, YP, AL.subtract, t_("NK0") + t_("YP"), y)
                 if v0 + w in (V - CH[1][-1], V):
                     a0 = 0 if v0 + w < V else v0
                     ys, a1 = ["Y0_%d" % b for b in range(a0 // 128, (v0 + w) // 128)], v0 + w
@@ -782,7 +861,10 @@ def rank_program(g, core, T, topo):
         cs = [chunk(r, sum(CH[r][:h]), CH[r][h]) for h in range(len(CH[r]))]
         for ks in ((0,), (1,), (2, 3, 4)):
             for st in cs:
-                for k in ks: st[k]()
+                for k in ks:
+                    a0 = len(ops)
+                    st[k]()
+                    for o in ops[a0:]: o["r"] = RW[cs.index(st)] * (k >= RK)
 
     if not EST: EST[:] = _plan(ops, users)
     order = EST[1]

import numpy as np
from concourse.bass import DstId, RemoteDMATransfer
from concourse.mybir import AluOpType as AL, ActivationFunctionType as AF

V, NR, BORD, WN = 512, 4, 256, 1280
CH = [[128] * 4, [128] * 4]
SCAN, RD = False, 2
NFS = [[8, 8, 4, 4], [8, 8, 4, 4]]
NFV = sorted({max(x, 0) for x in sum(NFS, [])} - {16})
LATE = ("F2", "B1")
BT = [[1, 1, 1, 1], [1, 1, 1, 1]]
RLAT, RLAT1, FLAT, FINE, LLAT = 5.0, 7.0, 7.0, True, 2.5
NHELP, HENG, LAND = 2, 8, ("AN", "XG")
GW, QS = 64, 4
LUTW = 14 * 256
WW = LUTW + 3 * WN
CEW, CE0 = 7792, 2880
MG, DL = 12582912.0, 1 / 128
N_ = None
P16 = list(range(16))
KK = [p >> 2 for p in P16]
LL = [p & 3 for p in P16]
SI = [0, 0, 3, 0, 1, 1, 3, 1, 2, 2, 3, 2, 0, 1, 2, 3]
SJ = [0, 1, 0, 3, 0, 1, 1, 3, 0, 1, 2, 3, 2, 2, 2, 3]
FULL = sorted((q for q in P16 if SI[q] < 3 and SJ[q] < 3), key=lambda q: (SJ[q], SI[q]))
CHAIN, NEA = (0, 0, 0, 0), (1, 1, 1, 1, 1)
PLACINGS = [7, 11, 13, 3, 14, 5, 6, 9, 10, 12, 1, 2, 4, 8]
POV, PMIN, VF, VO = 0.012, 64, 1.0, 0.0
RUSH, RW, RK = 0.0, (1, 1, 0, 0), 3
EARLY, BV, WAIT, GAP = 8, (384, 256, 128, 0), (0.5, 1.0), 1.0
NBANK, PASSES, MARG2, HALF, HALFA = 7 + SCAN, 4, ((3.0, 0.0), (6.0, 0.005), (10.0, 0.0), (16.0, 0.01)), 0.0, 0.2
MARG, OVH, PEC, GC, HOP, AHEAD, SOON = 20.0, 0.02, 0.43e-3, 1.56, 0.3, (0.004, 0.008, 0.012, 0.016, 0.02, 0.03), 0.6


def _old(s):
    o, k = [0] * 16, 0
    for p in range(4):
        if s >> p & 1:
            o = [o[m] | (((m >> p) & 1) << k) for m in P16]
            k += 1
    return o


WC1 = [((1 << m) + (29 * (1 << (m - 5)) if m >= 5 else 0)) % 4096 for m in P16]
WC1 = [x - 4096 * (x > 2048) for x in WC1]
HZ, HK = [0, 1, 1, 2, 2, 2], [0, 0, 1, 0, 1, 2]
A1, A2, N1, N2 = [.5, 1, 0, 0], [.5, -.5, .5, 0], [2.5, 1, 0, 0], [.5, .5, .5, 0]
TRIV = 10 + 1 / 128
V8 = {"A1": A1 * 2, "A2": A2 * 2, "N1": N1 * 2, "N2": N2 * 2,
      "cA0": [-24, 19, -3, 14, TRIV, 0, 0, 0], "cA1": [-18, 19, -3, 14, -16, 0, 0, 0], "cBf": [6, -26, 16, 0, 0, 0, 0, 0],
      "cBt": [9, -26, 16, 0, TRIV, 0, 0, 0], "cV": [-7, 1, 1, 1, 5, 0, 0, 0], "bU": [0, -4096, -8192, 12288, 0, 0, 0, 0]}
V16 = {"zrow": HZ * 2 + [9] * 4, "nwc1": [-x for x in WC1]}
V2_ = {"mul": (13, -1, 16), "off": (13, -1, 0), "sub": (13, -2047, 0), "dcol": (12, DL, 0), "bRa": (13, -4096, DL - 4096),
       "bRb": (13, -4096, 2), "u3": (12, -1, 1), "sY": (13, -1, 1), "thr": (13, 2049, 0), "tY": (13, 2048 + MG, MG)}
CN = list(V2_) + ["f12", "f13", "c8", "t5", "cAf", "cAt", "bX", "lo2", "hi2", "bY", "le12", "le12n", "is13", "is14", "is0", "is1", "bM",
                  "p256", "w2hi", "w2lo", "nA1", "nA2", "wlo", "whi", "p16s"]
_hc = [2048 * (HZ[c] - HK[c]) + 8192 * HK[c] for c in range(6)]
PHI = {}
for _i in range(6):
    PHI["S" + "AB"[_i // 3] + str(_i % 3)] = [4 * (_i % 3) + x for x in (KK, LL)[_i // 3]]
PHI.update({"COL": P16, "RID": [12] * 16})
for _i, _m in enumerate(PLACINGS):
    PHI["LUT%d" % _i] = _old(_m)
PHI.update({"HK": HK + [N_] * 10, "HC": _hc + [x - 24576 for x in _hc] + [-8192] * 4})
PN = list(PHI)
FM = [["SA0", "SA1", "SA2", "SB0", "SB1", "SB2", "I13", "R13", "I12", "R12"], ["XC", "XL", "XP", "XA", "XB", "I256"],
      ["J13", "RMa", "RMb", "EA", "EB", "HA", "HB", "Hs", "He", "UH", "UA", "UE", "E12", "LP"]]
BM = [["LUT%d" % i for i in range(14)], ["Zc1", "Zc2"] * (set(sum(BT, [])) != {1}) + ["ID", "IDn"] * (not SCAN) + ["IV", "KC", "Zlb", "ZT"] + ["ONE%d" % n for n in NFV]]
FN, BN = sum(FM, []), sum(BM, [])
f32, f16, b16, i32, u16 = "float32", "float16", "bfloat16", "int32", "uint16"
_S = [("fanI", 64, i32), ("fanU", 64, u16), ("LI", V, i32), ("LJ", V, i32), ("TF", V, f32), ("PW", 384, f32), ("BT3", 384, f32), ("IDI", V, i32), ("GNF", 8, f32), ("XF", 128 * 16, f32), ("RP", 16 * 384 if min(sum(NFS, [])) < 0 else 16, b16), ("CE", CEW, b16), ("RQ", V, b16),
      ("Gw0", WN, f32), ("Gw1", WN, f32), ("W0", WW, b16), ("W1", WW, b16), ("IW", WN, f32), ("Gc", 2 * V, f16),
      ("IDf", V, f16), ("PI", 8, i32), ("PJ", 8, i32), ("PF", 8, f32), ("GI", 32, f32), ("GM", 8, f32), ("GN", 8, b16), ("CO", len(CN), f32),
      ("VAL", 112, f32), ("OHI", 80, f32), ("OH", 176, f32), ("PR", 176, f32), ("VC", 176, f32), ("RST", 384, f32),
      ("POWR", 48, f32), ("POWC", 32, f32), ("TWO", 32, f32), ("TM", 128, f32), ("ONF", 128, f32), ("IDN", 128, f32),
      ("ON", 128, b16), ("ONH", 128, f16), ("BYI", 256, i32), ("BYB", 256, b16), ("BCI", 16, i32), ("BC", 16, u16), ("CV", 192, f16), ("IND", 128, f16), ("LS", V, f32),
      ("PIW", 128, f32), ("PJW", 128, f32), ("PA", 512, f16), ("PB", 256, f16), ("PAV", 128, f16), ("PBV", 128, f16),
      ("W2", 72, f16), ("W3", 24, b16), ("CT", 768, f16), ("W9", 352, f16),
      ("GG", 2 * V, f16), ("PP", 2 * V, f16), ("SG", 11 * V, f16), ("NE", 11 * V, f16), ("XX", V, f16), ("XT", 4 * V, f16), ("VT", V, b16),
      ("IX", 2 * V, u16), ("CX", 2 * V, u16), ("AG", 16 * V, b16), ("AN", 16 * V, b16), ("XG", 16 * V, b16),
      ("NK0", V, f32), ("NK1", V, f32), ("NKN", 2 * V, f32), ("KP", 2 * V, f32), ("SC", 3 * V, f32), ("MT", 3 * V, f16), ("MK", 3 * V, f16),
      ("LU", 3 * V // 16, u16), ("RA", 3 * V, f16), ("RB", 3 * V, f16), ("S2", 3 * V, f16), ("E2", 3 * V, f16), ("HH", 3 * V, f16),
      ("Y", V, f32), ("YP", V, f32), ("TT", 96, i32), ("Q5", 96, f32), ("Q6", 96, f32), ("YC", V, f32)]
RING = ("NK0", "NK1", "NKN", "KP", "MT", "RA", "RB", "S2", "E2", "HH", "YP", "SG", "NE")
SCRATCH = {n: ("sbuf", [128, k // 2 if n in RING else k], d) for n, k, d in _S}
if SCAN:
    SCRATCH.update({"D0": ("sbuf", [128, 8192], b16), "D1": ("sbuf", [128, 4096 * RD], b16), "DO": ("sbuf", [128, 8192], b16), "AG": ("sbuf", [128, 4096], b16),
                    "XG": ("sbuf", [128, 16], b16), "XF": ("sbuf", [128, 16], f32)})
SCRATCH.update({"TR": ("sbuf", [128, 3, V], i32), "PH": ("sbuf", [128, len(PN), 16], f32), "MF": ("sbuf", [128, len(FN), 16], f16), "MB": ("sbuf", [128, len(BN), 16], b16),
                "BF": ("sbuf", [128, len(FN), 144], f16), "BB": ("sbuf", [128, len(BN), 144], b16)})
for _b in range(8):
    SCRATCH["ps%d" % _b] = ("psum", [128, 512], f32)
SEMAPHORES = ["sv", "sa", "st", "sg", "loc", "go"] + ["d%d" % i for i in range(32)] + ["ar%d" % i for i in range(4)] + \
    ["h%s%d_%d" % (x, r, u) for x in "fb" for r in range(2) for u in range(V // GW)]
EST = []


def _cover(L):
    def ok(v, x): return (not 0 <= v <= 15) if x is None else v == x
    out, s = [], 0
    while s < len(L):
        base = L[s] if L[s] is not None else -1
        best = (1, [[0, 1]], base)

        def steps(o): return [x for x in ({0, L[s + o] - base} if s + o < len(L) and L[s + o] is not None else {0, 100}) if abs(x) < 32768]
        for n1 in range(1, min(16, len(L) - s) + 1):
            for s1 in (steps(1) if n1 > 1 else [0]):
                if not all(ok(base + j * s1, L[s + j]) for j in range(n1)): continue
                for s2 in steps(n1):
                    n2 = 1
                    while True:
                        m = n1 * n2
                        for s3 in steps(m):
                            n3 = 1
                            while s + (n3 + 1) * m <= len(L) and all(ok(base + n3 * s3 + j // n1 * s2 + j % n1 * s1, L[s + n3 * m + j]) for j in range(m)): n3 += 1
                            if m * n3 > best[0]: best = (m * n3, [[s3, n3], [s2, n2], [s1, n1]], base)
                        if s + (n2 + 1) * n1 <= len(L) and all(ok(base + n2 * s2 + j * s1, L[s + n2 * n1 + j]) for j in range(n1)): n2 += 1
                        else: break
        out.append((s,) + best); s += best[0]
    return out


COVER = {n: _cover(x) for n, x in PHI.items()}


def _runs(L):
    out = []
    for x in sorted(set(L) - {0}):
        rest = {i for i, y in enumerate(L) if y == x}
        while rest:
            best = None
            for a in sorted(rest):
                for st in [1] + [b - a for b in sorted(rest) if b > a]:
                    n = 1
                    while a + n * st in rest and n < 16: n += 1
                    if best is None or n > best[2]: best = (a, st, n)
            out.append(best + (float(x),)); rest -= {best[0] + k * best[1] for k in range(best[2])}
    return out


VRUNS = _runs([x * 128 for y in list(V8.values())[:9] for x in y])
VS, GOV, TLAT, TRA = 1, 0.1, 6.0, 1
VCOVER = [_cover([int(x * 128) for y in list(V8.values())[:9] for x in y]), _cover(V8["bU"]), _cover(sum(V16.values(), []))]


def _plan(ops, users):
    n = len(ops)
    pred = [set(o["d"]) | ({o["o"]} if "o" in o else set()) for o in ops]
    succ, pl = [[] for _ in range(n)], [0.0] * n
    for i in range(n):
        for d in pred[i]: succ[d].append(i)

    shy = [({"v": 1.0} if o["a"]["a"][1] < 1.4 * o["a"]["v"][1] else {"v": HALF, "a": HALFA}) if len(o["a"]) > 1 else {} for o in ops]

    def forward(pr, marg):
        left, free, order, rdy, fin = [len(x) for x in pred], {e: 0.0 for e in "atgsxv"}, [], [0.0] * n, [0.0] * n
        eng, bank, more, early, INF = [None] * n, {}, [set() for _ in range(n)], {}, 1e9
        pool = {i for i in range(n) if left[i] == 0}
        banks, open_ = {b: (0.0, set()) for b in range(NBANK)}, {t: len(u) for t, u in users.items()}
        while pool:
            bt = min([x[0] for x in banks.values()], default=None)
            at = {i: max(rdy[i], bt) if ops[i]["new"] else rdy[i] for i in pool if ops[i]["new"] is None or bt is not None}
            held = sorted(early.values())
            if len(held) >= EARLY:
                for i in [i for i in at if ops[i]["new"] and ops[i]["new"][-1] == "a"]:
                    if held[-EARLY] is INF: del at[i]
                    else: at[i] = max(at[i], held[-EARLY])
            t0, e = min((max(free[e], at[i]), e) for i in at for e in ops[i]["a"])
            mine = {i: (pr[i] - marg * shy[i].get(e, 0.0), -i) for i in at if e in ops[i]["a"]}
            i = max((i for i in mine if at[i] <= t0 + 1e-9), key=mine.get)
            soon = [j for j in mine if at[j] < t0 + min(SOON, WAIT[e == "t"] * ops[i]["a"][e][1]) and mine[j][0] > mine[i][0] + GAP]
            if soon:
                i = max(soon, key=mine.get); t0 = max(free[e], at[i])
            pool.remove(i); order.append(i)
            o = ops[i]
            if o["new"]:
                b = min(banks, key=lambda b: (banks[b][0], b))
                bank[o["new"]] = b; more[i] = banks.pop(b)[1]
                if o["new"][-1] == "a": early[o["new"]] = INF
            eng[i] = e; free[e] = t0 + o["a"][e][1]; fin[i] = free[e] + o["l"] + HOP
            for t in o["ps"]:
                open_[t] -= 1
                if open_[t] == 0:
                    banks[bank[t]] = (max(fin[j] for j in users[t]), users[t])
                    if t in early: early[t] = banks[bank[t]][0]
            for j in succ[i]:
                rdy[j] = max(rdy[j], fin[i]); left[j] -= 1
                if left[j] == 0: pool.add(j)
        return [max(fin), order, eng, bank, more, fin]

    def backward(eng, fin, back):
        left, free, rdy, end = [len(x) for x in succ], {e: 0.0 for e in "atgsxv"}, [o["l"] for o in ops], [0.0] * n
        pool = {i for i in range(n) if left[i] == 0}
        while pool:
            t0, e = min((max(free[eng[i]], rdy[i]), eng[i]) for i in pool)
            i = max((i for i in pool if eng[i] == e and rdy[i] <= t0 + 1e-9), key=lambda i: (fin[i], i))
            pool.remove(i)
            free[e] = end[i] = t0 + ops[i]["a"][e][1]
            for j in pred[i]:
                rdy[j] = max(rdy[j], end[i] + ops[j]["l"] + HOP + back * ops[j].get("b", 0.0)); left[j] -= 1
                if left[j] == 0: pool.add(j)
        return end
    best = None
    for ahead in AHEAD:
        for i in range(n - 1, -1, -1):
            pl[i] = min(c for f, c in ops[i]["a"].values()) + ops[i]["l"] + HOP + max([pl[j] for j in succ[i]], default=0.0) + ahead * ops[i].get("b", 0.0)
        first = forward(pl, MARG)
        for marg, back in MARG2:
            cur = first
            for k in range(PASSES):
                cur = forward([x + RUSH * o.get("r", 0) for x, o in zip(backward(cur[2], cur[5], back), ops)], marg)
                if best is None or cur[0] < best[0]: best = cur
    return best


def helpers(T, topo, core):
    return [c for c in topo.cores_of(core) if topo.die(c) == topo.die(core) and c not in T.cores][:NHELP]


def back(topo, c, core): return topo.engines(c, core)[:HENG]


def folds():
    return [(r, u) for r in range(2) for h, w in enumerate(CH[r]) if NFS[r][h] < 0 for u in range(sum(CH[r][:h]) // GW, sum(CH[r][:h + 1]) // GW)]


def helper_program(g, core, T, topo):
    for c in T.cores:
        if core in helpers(T, topo, c):
            k, es, n = helpers(T, topo, c).index(core), back(topo, core, c), 0
            rid, pid = topo.addr(c, core)
            for r, u in folds():
                if u % NHELP == k:
                    s = slice(16 * GW * u, 16 * GW * (u + 1))
                    g.wait_ge(T.sem["hf%d_%d" % (r, u)], len(topo.engines(c, core)) // NHELP)
                    g.remote_dma(T.AG[:, s], T[LAND[r]][:, s], T.sem["hb%d_%d" % (r, u)], T.sem.loc, pid, rid, sum(1 << e for e in es))
                    n += len(es)
            if n: g.wait_ge(T.sem.loc, n)


def rank_program(g, core, T, topo):
    rank = T.rank_of(core)
    if rank is None:
        return helper_program(g, core, T, topo)
    ops, lastw, readers, users, bankof = [], {}, {}, {}, {}
    vec, act, ten = g.vector, g.scalar, g.tensor
    CY = 0.83e-3

    def add(alts, R, Wr, lat=0.0, sem=None, cnt=1):
        i, deps, eng, new = len(ops), set(), "".join(alts), None
        if "v" in alts: alts["v"] = (alts["v"][0], alts["v"][1] * VF + VO)
        for t in list(R) + list(Wr):
            if t in lastw: deps.add(lastw[t])
            if t[0] == "#":
                deps.update(j for j in readers.get(t, ()) if ops[j]["e"] != eng or len(eng) > 1)
                if t not in users: new = t
                users.setdefault(t, set()).add(i)
        for t in Wr: deps.update(readers.get(t, ()))
        for t in R: readers.setdefault(t, []).append(i)
        for t in Wr: lastw[t] = i; readers[t] = []
        deps.discard(i)
        ops.append({"e": eng, "a": alts, "d": deps, "l": lat, "s": sem, "n": cnt, "new": new, "k": (list(Wr) + ["-"])[0], "ps": [t for t in set(R) | set(Wr) if t[0] == "#"]})
        return i

    def tile():
        return "#%d" % len(ops)

    def ps(t, a, b, st=1, rows=128): return (t, a, b, st, rows)

    def rs(x): return T["ps%d" % bankof[x[0]]][0:x[4], x[1]:x[2]:x[3]] if isinstance(x, tuple) else x

    def nel(x): return len(range(x[1], x[2], x[3])) if isinstance(x, tuple) else int(np.prod(x.shape[1:]))

    def cv(out, cy): return OVH + max(64, nel(out) * cy) * CY

    def vts(out, in0, s1, s2, o0, o1, cy=1.0):
        if o1 is None: return (lambda: vec.tensor_scalar(rs(out), rs(in0), s1, None, o0)), cv(out, cy)
        return (lambda: vec.tensor_scalar(rs(out), rs(in0), s1, s2, o0, o1)), cv(out, cy)

    def vcp(out, a, cy=1.0): return (lambda: vec.tensor_copy(rs(out), rs(a))), cv(out, cy)

    def aac(out, a, fn, bias=0.0, scale=1.0, cy=1.0): return (lambda: act.activation(rs(out), rs(a), fn, bias, scale)), cv(out, cy) + 0.015

    def ts(out, in0, s1, s2, o0, o1, R, Wr, cy=1.0): add({"v": vts(out, in0, s1, s2, o0, o1, cy)}, R, Wr)

    def tt(out, a, b, o, R, Wr, cy=2.0): add({"v": (lambda: vec.tensor_tensor(rs(out), rs(a), rs(b), o), cv(out, cy))}, R, Wr)

    def cp(out, a, R, Wr, cy=1.0): add({"v": vcp(out, a, cy)}, R, Wr)

    def fcp(out, a, R, Wr, cy=1.0): add({"v": vcp(out, a, cy), "a": aac(out, a, AF.Copy, cy=cy)}, R, Wr)

    def faff(out, a, sc, bi, R, Wr, cy=1.0, cyv=None):
        add({"v": vts(out, a, sc, bi, AL.mult, AL.add, cyv or cy), "a": aac(out, a, AF.Identity, bi, sc, cy)}, R, Wr)

    def frelu(out, a, bi, R, Wr): add({"v": vts(out, a, bi, 0.0, AL.add, AL.max), "a": aac(out, a, AF.Relu, bi)}, R, Wr)

    def sign(out, a, R, Wr): add({"v": vts(out, a, -1.0, 1.0, AL.max, AL.min), "a": aac(out, a, AF.Sign)}, R, Wr)

    def fne(out, a, R, Wr, both=True): add({"v": vts(out, a, 0.0, None, AL.not_equal, None, 0.5), **({"a": aac(out, a, AF.Abs)} if both else {})}, R, Wr)

    def ms(out, c, Wr, cy=1.0): add({"v": (lambda: vec.memset(out, c), cv(out, cy))}, [], Wr)

    def scan(out, d0, d1, init, o0, o1, R, Wr): add({"v": (lambda: vec.tensor_tensor_scan(out, d0, rs(d1), init, o0, o1), cv(out, 1))}, R, Wr)

    def ac(out, a, R, Wr, fn=AF.Copy, bias=0.0, cy=1.0): add({"a": aac(out, a, fn, bias, 1.0, cy)}, R, Wr)

    def mm(trips, R, Wr, st=True, sp=True, k=1):
        def f():
            for n, (o, l, r) in enumerate(trips): x = ten.matmul(rs(o), l, r, st and n == 0, sp and n == len(trips) - 1)
            return x
        add({"t": (f, sum(POV + max(PMIN, nel(o)) * (4 if "float32" in str(l.dtype) else 1) * PEC for o, l, r in trips))}, R, Wr, 0.05)

    def io(out, pat, base, cm, Wr, fl=True):
        if fl: f = lambda: g.iota(out, pat, base, cm, allow_small_or_imprecise_dtypes=True)
        else: f = lambda: g.iota(out, pat, base, cm)
        add({"g": (f, 0.13 + GOV + 2 * nel(out) * CY)}, [], Wr)
    nd = [0]

    def dma(q, prs, R, Wr, lat=2.5):
        s, eng = "d%d" % nd[0], {"s": g.sync, "a": g.scalar}[q]
        nd[0] += 1

        def f():
            for o, i in prs: eng.dma_start(o, i).then_inc(T.sem[s], 16)
        add({q: (f, 0.06 * len(prs))}, R, Wr, lat, s, 16 * len(prs))

    def deal(src):
        ds = [c for c in T.cores if c != src]
        far = [c for c in ds if c not in topo.cores_of(src)]
        used, res = set(), {}
        for c in far + [c for c in ds if c not in far]:
            pool = [e for e in topo.engines(src, c) if e not in used]
            share, n = len(pool) // (len([x for x in far if x not in res]) if c in far else 1), 1
            while 2 * n <= min(share, 4): n *= 2
            res[c] = pool[:n]; used.update(pool[:n])
        return res
    mine = deal(core)
    inc_in = sum(len(deal(c)[core]) for c in T.cores if c != core)
    locn = [0]

    def send(buf, offs, sem, R, Wr, lat):
        def f():
            for o in offs:
                trs = []
                for d in range(1, NR):
                    c = T.cores[(rank + d) % NR]
                    rid, pid = topo.addr(c, core)
                    trs.append(RemoteDMATransfer(dst_ids=[DstId(rid=rid, pnc=pid)], dma_engine_mask=sum(1 << e for e in mine[c]), remote_sem=T.sem[sem],
                                                 src=buf[:, o:o + BORD], dst=buf[:, o + V + (d - 1) * BORD:o + V + d * BORD]))
                g.remote_dma_fused(trs, local_sem=T.sem.loc)
        locn[0] += len(offs) * sum(len(x) for x in mine.values())
        i = add({"g": (f, 0.4 * len(offs))}, R, ["sent"], 0.0, "loc", 0)
        ops[add({"x": (None, 0.0)}, [], Wr, lat, sem, inc_in * len(offs))]["o"] = i

    def fold(r, u, R, Wr):
        c, s = helpers(T, topo, core)[u % NHELP], slice(16 * GW * u, 16 * GW * (u + 1))
        es = topo.engines(core, c)
        es = es[u % NHELP * len(es) // NHELP:(u % NHELP + 1) * len(es) // NHELP]
        rid, pid = topo.addr(c, core)
        tr = RemoteDMATransfer(dst_ids=[DstId(rid=rid, pnc=pid)], dma_engine_mask=sum(1 << e for e in es), remote_sem=T.sem["hf%d_%d" % (r, u)],
                               srcs=[T.XG[:, s], T.RP[:, s]], dsts=[T[LAND[r]][:, s]], alu_op=2)
        locn[0] += len(es)
        i = add({"g": (lambda: g.remote_dma_fused([tr], local_sem=T.sem.loc), 0.4)}, R, [], 0.0, "loc", 0)
        ops[add({"x": (None, 0.0)}, [], Wr, FLAT, "hb%d_%d" % (r, u), len(back(topo, c, core)))]["o"] = i

    def tk(n, xs): return ["%s_%d" % (n, x) for x in xs]

    def send_g(r): send(T["Gw%d" % r], [0], "ar%d" % (2 * r), tk("Gw%d" % r, (0, 1)), ["Gw%dr" % r], RLAT1 if r else RLAT)

    def send_b(r): send(T["W%d" % r], [LUTW + WN * c for c in range(3)], "ar%d" % (2 * r + 1), tk("W%d" % r, range(6)), ["W%dr" % r], (RLAT1 if r else RLAT) + 2)

    dma("s", [(T.LI[f::16, :], T.leaf0[:, f * V:(f + 1) * V]) for f in range(8)], [], ["LIa"], LLAT)
    dma("a", [(T.LI[f::16, :], T.leaf0[:, f * V:(f + 1) * V]) for f in range(8, 12)] +
        [(T.LI[13 + c::16, :], T.tab0[:, c * V:(c + 1) * V]) for c in range(3)] + [(T.fanI[:], T.fan[:])], [], ["LIb", "fanI"], LLAT)
    io(T.PI[:, 0:1], [[0, 1]], 0, 1, ["PI"], False)
    for h in range(2):
        io(T.IDI[:, h * BORD:(h + 1) * BORD], [[1, BORD]], V * rank + h * BORD, 0, ["IDI" + "0" * (1 - h)], False)
        dma("s", [(T.LI[12::16, h * BORD:(h + 1) * BORD], T.IDI[12::16, h * BORD:(h + 1) * BORD])], ["IDI" + "0" * (1 - h)], ["LIc%d" % h], LLAT)

    for n, (sh, an) in enumerate([(0, 15), (2, 3), (0, 3), (4, 7), (2, 31), (0, 1)]):
        ts(T.PJ[:, n:n + 1], T.PI[:, 0:1], sh, an, AL.logical_shift_right, AL.bitwise_and, ["PI"], ["PJ%d" % n])
    cp(T.PF[:, 0:1], T.PJ[:, 0:1], ["PJ0"], ["PF0"])
    cp(T.PF[:, 1:6], T.PJ[:, 1:6], ["PJ%d" % n for n in range(1, 6)], ["PF1"])
    p16, kc, lc, gc_, p4, odd = [T.PF[:, n:n + 1] for n in range(6)]
    PF = ["PF0", "PF1"]

    def vc(n):
        if n in CN: return T.CO[:, CN.index(n):CN.index(n) + 1]
        a = 87 + 8 * list(V8).index(n[1:]) if n[0] == "k" else {"si": 127, "sj": 143, "zrow": 159, "nwc1": 175}.get(n) or 8 * list(V8).index(n) + 7
        return T.VC[:, a:a + 1]

    def vt(*ns): return ["c" + n if n in CN else {"k": "VCk", "s": "VCs", "z": "VCs", "n": "VCs", "b": "VCb"}.get(n[0], "VC8") for n in ns]

    def co(n, a, s1, s2, o0, o1, R): ts(vc(n), a, s1, s2, o0, o1, R, vt(n))
    co("f13", p16, 13.0, None, AL.is_ge, None, ["PF0"]); co("f12", p16, 12.0, None, AL.is_ge, None, ["PF0"])
    for n, (at, x, y) in V2_.items(): faff(vc(n), vc("f%d" % at), float(y - x), float(x), vt("f%d" % at), vt(n))
    for n, o, x, y in [("le12", AL.is_le, 12.0, 1.0), ("le12n", AL.is_le, 12.0, -1 / DL), ("is13", AL.is_equal, 13.0, 1.0), ("is14", AL.is_equal, 14.0, 0.5),
                       ("is0", AL.is_equal, 0.0, 524288.0), ("is1", AL.is_equal, 1.0, -1 / 32)]: co(n, p16, x, y, o, AL.mult, ["PF0"])
    faff(vc("p16s"), p16, 1 / 256, 0.0, ["PF0"], vt("p16s"))
    faff(vc("p256"), p16, 16.0, -4096.0, ["PF0"], vt("p256")); faff(vc("bX"), odd, 2048.0, -2048.0, PF, vt("bX"))
    co("lo2", lc, 2.0, None, AL.is_lt, None, PF); co("hi2", lc, 2.0, None, AL.is_ge, None, PF)
    co("c8", kc, 2.0, -4.0, AL.min, AL.mult, PF); co("c8", vc("c8"), p16, None, AL.add, None, PF + vt("c8"))
    io(T.GI[:], [[1, 32]], 0, 0, ["GI"])
    ts(T.GM[:], T.GI[:, 0:8], gc_, None, AL.is_equal, None, ["GI"] + PF, ["GM"])
    faff(T.GN[:], T.GM[:], -1.0, 0.0, ["GM"], ["GN"])
    if not SCAN: faff(T.GNF[:], T.GM[:], -1.0, 0.0, ["GM"], ["GNF"])
    ms(T.RST[:], 1.0, ["RST"]); ms(T.RST[:, 0::16], 0.0, ["RST"])
    ms(T.TWO[:, 0:16], 2.0, ["TWO"]); ms(T.TWO[:, 16:32], 0.5, ["TWO"]); ms(T.POWR[:, 32:48], 0.0, ["ZR"])
    io(T.PIW[:], [[4, 8], [1, 4], [0, 4]], 0, 0, ["PIW"]); io(T.PJW[:], [[4, 8], [0, 4], [1, 4]], 0, 0, ["PJW"])
    fcp(T.PJW[:, 2::4], T.PIW[:, 2::4], ["PIW"], ["PJW"]); fcp(T.PIW[:, 2::4], T.PJW[:, 3::4], ["PJW"], ["PIW"])
    for q in (12, 13, 14):
        faff(T.PIW[:, q::16], T.PIW[:, 0::16], 1.0, float(SI[q]), ["PIW"], ["PIW"]); faff(T.PJW[:, q::16], T.PJW[:, 0::16], 1.0, float(SJ[q]), ["PJW"], ["PJW"])
    vtk = []
    if VS:
        vtk.append(["VAL%d" % y[0] for y in VRUNS])
        ms(T.VAL[:, 0:72], 0.0, ["VAL"])
        for s, st, n, x in VRUNS:
            o = T.VAL[:, s:s + (n - 1) * st + 1:st]
            add({"v": (lambda o=o, x=x: vec.memset(o, x), cv(o, 1)), "a": aac(o, T.TWO[:, 0:n], AF.Identity, x, 0.0)}, ["VAL", "TWO"], ["VAL%d" % s])
    for a0, cov in list(zip((0, 72, 80), VCOVER))[VS:]:
        vtk.append(["VAL%d" % (a0 + y[0]) for y in cov])
        for s, n, pat, base in cov: io(T.VAL[:, a0 + s:a0 + s + n], pat, base, 0, ["VAL%d" % (a0 + s)])
    io(T.OHI[:], [[0, 10], [1, 8]], 0, 0, ["OHI"])
    for a0, n, ft, x, va, R, tok in ((0, 72, vc("c8"), 1 / 128, T.VAL[:, 0:72], vtk[0], "VC8"), (72, 8, vc("c8"), 1.0, T.VAL[:, 72:80], vtk[1], "VCb"),
                                     (80, 32, kc, 1 / 128, T.VAL[:, 0:32], vtk[0], "VCk")):
        ts(T.OH[:, a0:a0 + n], T.OHI[:, 0:n], ft, x, AL.is_equal, AL.mult, ["OHI"] + PF + vt("c8"), ["OH" + tok])
        tt(T.PR[:, a0:a0 + n], T.OH[:, a0:a0 + n], va, AL.mult, ["OH" + tok] + R, ["PR" + tok])
        scan(T.VC[:, a0:a0 + n], T.RST[:, 0:2 * n:2], T.PR[:, a0:a0 + n], 0.0, AL.mult, AL.add, ["PR" + tok, "RST"], [tok])
    for a0 in (112, 128): ts(T.OH[:, a0:a0 + 16], T.GI[:, 0:16], p16, None, AL.is_equal, None, ["GI", "PF0"], ["OH%d" % a0])
    oh, OHT = T.OH[:, 112:144], ["OH112", "OH128"]
    tt(T.PR[:, 112:128], T.OH[:, 112:128], T.PIW[:, 0:16], AL.mult, OHT + ["PIW"], ["PRa"])
    tt(T.PR[:, 128:144], T.OH[:, 112:128], T.PJW[:, 0:16], AL.mult, OHT + ["PJW"], ["PRb"])
    tt(T.PR[:, 144:176], oh, T.VAL[:, 80:112], AL.mult, OHT + vtk[2], ["PRc"])
    scan(T.VC[:, 112:176], T.RST[:, 0:64], T.PR[:, 112:176], 0.0, AL.mult, AL.add, ["PRa", "PRb", "PRc", "RST"], ["VCs"])
    co("t5", vc("c8"), 3.0, kc, AL.is_equal, AL.mult, PF + vt("c8"))
    for n, x in (("cAf", "cA0"), ("cAt", "cA1")): faff(vc(n), vc("t5"), 5.0, vc(x), vt("t5", x), vt(n))
    faff(vc("bM"), vc("bU"), 1.0, MG, vt("bU"), vt("bM")); faff(vc("bY"), vc("bU"), -1.0, vc("tY"), vt("bU", "tY"), vt("bY"))
    for n in ("A1", "A2"): faff(vc("n" + n), vc(n), -1.0, 0.0, vt(n), vt("n" + n))
    scan(T.POWR[:, 0:16], T.TWO[:, 0:16], T.POWR[:, 32:48], 0.5, AL.mult, AL.add, ["TWO", "ZR"], ["PWa"])
    scan(T.POWR[:, 16:32], T.TWO[:, 16:32], T.POWR[:, 32:48], 65536.0, AL.mult, AL.add, ["TWO", "ZR"], ["PWb"])
    tt(T.POWC[:], T.POWR[:, 0:32], oh, AL.mult, ["PWa", "PWb"] + OHT, ["PWc"])
    scan(T.POWR[:, 0:32], T.RST[:, 0:32], T.POWC[:], 0.0, AL.mult, AL.add, ["PWc", "RST"], ["PWa", "PWb"])
    w2m, w15 = T.POWR[:, 15:16], T.POWR[:, 31:32]
    co("w2hi", w2m, 16.0, w2m, AL.is_ge, AL.mult, ["PWa"]); co("w2lo", w2m, 200.0, w2m, AL.is_le, AL.mult, ["PWa"])

    for h in range(2):
        x, y = T.LJ[:, h * BORD:(h + 1) * BORD], T.LI[:, h * BORD:(h + 1) * BORD]
        fcp(T.TF[:, h * BORD:(h + 1) * BORD], y, ["LIa", "LIb", "LIc%d" % h], ["TF%d" % h])
        faff(x, y, vc("mul"), vc("off"), ["LIa", "LIb", "LIc%d" % h] + vt("mul", "off"), ["LI%d" % h])
        ts(x, x, 4095, None, AL.bitwise_and, None, ["LI%d" % h], ["LI%d" % h])
        frelu(T.Gw0[:, h * BORD:(h + 1) * BORD], x, vc("sub"), ["LI%d" % h] + vt("sub"), tk("Gw0", (2 * h, 2 * h + 1)))
    send_g(0)
    faff(T.PW[:, 0:128], T.RST[:, 0:128], 0.5, 0.0, ["RST"], ["PW0"]); faff(T.PW[:, 128:256], T.RST[:, 0:128], -32768.0, 32768.0, ["RST"], ["PW1"])
    scan(T.PW[:, 256:384], T.PW[:, 0:128], T.PW[:, 128:256], 0.0, AL.mult, AL.add, ["PW0", "PW1"], ["PW2"])
    for c in range(3):
        add({"g": (lambda c=c: g.affine_select(T.BT3[:, 128 * c:128 * c + 128], T.PW[:, 256:384], [[16, 8], [0, 16]], AL.is_equal, 0.0, 13 + c, -1), 0.39 + GOV)},
            ["PW2"], ["BT3_%d" % c])
    for h in range(2):
        x, a0 = T.TR[:, :, h * BORD:(h + 1) * BORD], LUTW + h * BORD
        for cs in ((0, 1), (2,)):
            pb = tile()
            for u, c in enumerate(cs): mm([(ps(pb, u * BORD, (u + 1) * BORD), T.BT3[:, 128 * c:128 * c + 128], T.TF[:, h * BORD:(h + 1) * BORD])], ["BT3_%d" % c, "TF%d" % h], [pb])
            for u, c in enumerate(cs): fcp(T.TR[:, c, h * BORD:(h + 1) * BORD], ps(pb, u * BORD, (u + 1) * BORD), [pb], ["TR%d_%d" % (h, c)])
        ts(x, x, 32768, None, AL.bitwise_and, None, tk("TR%d" % h, range(3)), ["TR%d" % h])
        for c in range(3):
            faff(T.W0[:, a0 + WN * c:a0 + WN * c + BORD], T.TR[:, c, h * BORD:(h + 1) * BORD], 1 / 32768, 0.0, ["TR%d" % h], tk("W0", (6 * h + c, 6 * h + 3 + c)))
    send_b(0)
    fcp(T.fanU[:], T.fanI[:], ["fanI"], ["fanU"])
    io(T.IDf[:], [[-1, V]], 2048 - V * rank, 0, ["IDf"])
    add({"g": (lambda: g.sem_inc(T.sem.go, 1), 0.05)}, ["sent"], ["go"], 0.0, "go", 1)
    dma("s", [(T.RQ[:], T.req[:]), (T.CE[:, 0:CE0], T.cells[:, 4096 - CE0:]), (T.CE[:, CE0:CE0 + 4096], T.cells[:]),
              (T.CE[:, CE0 + 4096:], T.cells[:, 0:CEW - CE0 - 4096])], ["go"], ["CE", "RQ"], 14.0)
    for b in sorted({u * GW // 128 for r, u in folds()}):
        for q in P16:
            o, x = T.RP[:, 2048 * b + q:2048 * (b + 1):16], T.RQ[:, 128 * b:128 * b + 128]
            add({"g": (lambda o=o, x=x: g.affine_select(o, x, [[0, 128]], AL.is_ge, 0.0, 0, 0), 0.39)}, ["RQ"], ["RP%d_%d" % (q, b)])
    for a0 in (0, V, 2 * V): io(T.IW[:, a0:min(WN, a0 + V)], [[1, min(V, WN - a0)]], a0, 0, ["IW%d" % a0])
    fcp(T.Gc[:], T.IW[:].indirect(T.fanU[:]), ["IW0", "IW512", "IW1024", "fanU"], ["Gc"], GC)
    if SCAN: ms(T.D0[:, 0::2], 0.0, ["D0z"], 0.5)
    else:
        bankof["rq"] = 7
        fcp(ps("rq", 0, V), T.RQ[:], ["RQ"], ["rq"])

    io(T.PH[:, 0:3, :], [[4, 3], [1, 4], [0, 4]], 0, 0, ["PHSA%d_0" % i for i in range(3)])
    io(T.PH[:, 3:6, :], [[4, 3], [0, 4], [1, 4]], 0, 0, ["PHSB%d_0" % i for i in range(3)])
    for k, n in list(enumerate(PN))[6:]:
        for s, x, pat, base in COVER[n]: io(T.PH[:, k, s:s + x], pat, base, 0, ["PH%s_%d" % (n, s)])

    def P_(n, a=0, b=16, st=1): return T.PH[:, PN.index(n), a:b:st], ["PH%s_%d" % (n, y[0]) for y in COVER[n]]

    def mf(n, a=0, b=16, st=1): return T.MF[:, FN.index(n), a:b:st], "MF" + n

    def mb(n, a=0, b=16, st=1): return T.MB[:, BN.index(n), a:b:st], "MB" + n

    def tm(a, n): return T.TM[:, a:a + n], "TM%d" % a

    def eqm(dst, phi, feat, x, tok=()): ts(dst[0], phi[0], feat, x, AL.is_equal, AL.mult, phi[1] + PF + list(tok), [dst[1]])

    def col(dst, z, tok, sc=1.0): faff(dst[0], z, sc, 0.0, tok, [dst[1]])

    def plus(dst, a, b): tt(dst[0], a[0], b[0], AL.add, [a[1], b[1]], [dst[1]])

    def ramp(dst, phi, feat, tmp, top):
        ts(tmp[0], phi[0], feat, 1.0, AL.subtract, AL.add, phi[1] + PF, [tmp[1]])
        ts(tmp[0], tmp[0], -top / 2, 0.0, AL.mult, AL.min, [tmp[1]], [tmp[1]])
        ts(dst[0], tmp[0], -top, None, AL.max, None, [tmp[1]], [dst[1]])
    add({"v": (lambda: vec.memset(T.MF[:], 0.0), 0.3)}, [], ["MF" + n for n in FN])
    add({"v": (lambda: vec.memset(T.MB[:], 0.0), 0.3)}, [], ["MB" + n for n in BN])
    ms(T.BF[:, :, 128:144], 0.0, ["BFz"], 0.5); ms(T.BB[:, :, 128:144], 0.0, ["BBz"], 0.5)
    for M, N, ns, x in ((T.MF, FN, FM[0][:3], 1 / DL), (T.MF, FN, FM[0][3:6], -1 / DL), (T.MB, BN, BM[0], 1.0)):
        a0, b0 = N.index(ns[0]), PN.index(ns[0])
        ts(M[:, a0:a0 + len(ns), :], T.PH[:, b0:b0 + len(ns), :], p16, x, AL.is_equal, AL.mult, sum([P_(n)[1] for n in ns], ["PF0"]),
           [("MF" if N is FN else "MB") + n for n in ns])
    for n in (13, 12):
        eqm(mf("I%d" % n, 0, n), P_("COL", 0, n), p16, 1 / DL); eqm(mf("R%d" % n, 0, n), P_("RID", 0, n), p16, -1 / DL)
    eqm(mf("J13", 0, 13), P_("COL", 0, 13), p16, 1.0)
    eqm(mf("XC", 2, 12, 4), P_("RID", 0, 3), p16, 1.0); eqm(mf("XL", 3, 12, 4), P_("COL", 13, 16), p16, 1 / 16)
    eqm(mf("XP", 2, 12, 4), P_("COL", 3, 12, 4), p16, 2048.0); eqm(mf("XP", 3, 12, 4), P_("COL", 3, 12, 4), p16, -2048.0)
    si, sj = (T.PIW[:, 0:16], ["PIW"]), (T.PJW[:, 0:16], ["PJW"])
    eqm(mf("XA"), si, kc, vc("lo2"), vt("lo2")); eqm(mf("XB"), sj, kc, vc("hi2"), vt("hi2")); eqm(mf("I256"), P_("COL"), p16, 256.0)
    eqm(mf("RMa"), P_("SA0"), vc("si"), 16.0, vt("si")); eqm(mf("RMb", 0, 13), P_("SA0", 0, 13), vc("sj"), 16.0, vt("sj"))
    ms(mf("RMb", 14, 15)[0], -1 / 128, ["MFRMb"])
    eqm(mf("EA"), P_("SA0"), lc, 1 / DL); eqm(tm(0, 16), P_("SB0"), lc, vc("le12n"), vt("le12n"))
    faff(mf("EB")[0], tm(0, 16)[0], 1.0, vc("is14"), ["TM0"] + vt("is14"), ["MFEB"])
    eqm(mf("HA", 0, 6), P_("HK", 0, 6), lc, 1.0)
    eqm((T.TM[:, 16:22], "TM16"), P_("HK", 0, 6), lc, vc("le12"), vt("le12")); eqm((T.TM[:, 22:26], "TM16"), P_("COL", 0, 4), lc, vc("le12"), vt("le12"))
    faff(mf("HB")[0], P_("HC")[0], vc("is13"), 0.0, P_("HC")[1] + vt("is13"), ["MFHB"]); plus(mf("HB", 6, 16), mf("HB", 6, 16), tm(16, 10))
    eqm(mf("Hs", 0, 6), P_("HK", 0, 6), kc, 2048.0); eqm(mf("Hs", 6, 12), P_("HK", 0, 6), lc, -2048.0)
    ramp(mf("He", 0, 6), P_("HK", 0, 6), kc, tm(48, 6), 4096.0); ramp(tm(54, 6), P_("HK", 0, 6), lc, tm(54, 6), 4096.0)
    eqm(tm(60, 6), P_("HK", 0, 6), lc, 12288.0); plus(mf("He", 6, 12), tm(54, 6), tm(60, 6))
    eqm(mf("He", 12, 16), P_("COL", 0, 4), lc, 4096.0)
    eqm(mf("UH", 8, 11), P_("COL", 0, 3), vc("zrow"), 1.0, vt("zrow")); col(mf("UH", 11, 12), vc("u3"), vt("u3"))
    ms(mf("UA", 11, 12)[0], 1.0, ["MFUA"]); col(mf("UE", 15), vc("is14"), vt("is14"), -65536.0)
    eqm(mf("E12", 12, 13), P_("RID", 0, 1), p16, 1.0); eqm(mf("LP", 3, 16, 4), P_("RID", 0, 4), 12.0, vc("p16s"), vt("p16s"))
    if "Zc1" in BN: col(mb("Zc1", 15), vc("nwc1"), vt("nwc1")); col(mb("Zc2", 15), vc("w2hi"), vt("w2hi"), -1 / 16)
    col(mb("Zlb", 15), vc("w2lo"), vt("w2lo"), 16.0); col(mb("ZT", 15), w2m, ["PWa"])
    eqm(mb("IV"), P_("COL"), p16, -524288.0)
    if not SCAN: eqm(mb("ID"), P_("COL"), p16, 1.0); eqm(mb("IDn"), P_("COL"), p16, -1.0)
    for n in NFV: ms(mb("ONE%d" % n, 0, 16 - n)[0], 1.0, ["MBONE%d" % n])
    faff(tm(66, 16)[0], si[0], 4.0, 32.0, si[1], ["TM66"]); plus(tm(66, 16), tm(66, 16), (sj[0], "PJW"))
    faff(mb("KC")[0], tm(66, 16)[0], vc("is1"), vc("is0"), ["TM66"] + vt("is0", "is1"), ["MBKC"])
    TK = {}
    for tag, grp, M, B in (("F", FM, T.MF, T.BF), ("B", BM, T.MB, T.BB)):
        o = 0
        for gi, ns in enumerate(grp):
            for q in range(8):
                dst, src, R, Wr = B[:, o:o + len(ns), 16 * q:16 * q + 16], M[:, o:o + len(ns), :], ["M" + tag + n for n in ns], ["B%s%d_%d" % (tag, gi, q)]
                if tag + str(gi) not in LATE:
                    faff(dst, src, T.GM[:, q:q + 1], 0.0, ["GM"] + R, Wr, 1.0, 0.5)
                    continue
                for base, cm in [(-16 * q, 1)] * (q > 0) + [(16 * q + 15, -1)] * (q < 7):
                    add({"g": (lambda dst=dst, src=src, base=base, cm=cm: g.affine_select(dst, src, [[0, nel(dst)]], AL.is_ge, 0.0, base, cm),
                               0.17 + GOV + 2 * nel(dst) * CY)}, R, Wr)
                    src, R = dst, Wr
            TK[tag + str(gi)] = ["B%s%d_%d" % (tag, gi, q) for q in range(8)] + ["B%sz" % tag]
            o += len(ns)

    def LF(n, s=0): return T.BF[:, FN.index(n), s:s + 128]

    def LB(n, s=0): return T.BB[:, BN.index(n), s:s + 128]
    F0, F1, F2, B0, B1 = [TK[x] for x in ("F0", "F1", "F2", "B0", "B1")]
    for n, x in enumerate(["kA2", "kA1", "A1", "A2", "kN2", "kN1", "N1", "N2"]):
        ts(T.W2[:, 8 * n:8 * n + 8], T.GM[:], vc(x), 1.0 - 2 * (n < 2), AL.mult, AL.mult, ["GM"] + vt(x), ["W2_%d" % n])
    fcp(T.W2[:, 64:72], T.GM[:], ["GM"], ["W2_8"])
    if max(sum(BT, [])):
        co("wlo", p16, 10.0, vc("nwc1"), AL.is_le, AL.mult, PF + vt("nwc1")); co("whi", p16, 10.0, vc("nwc1"), AL.is_gt, AL.mult, PF + vt("nwc1"))
        for n, (x, y) in enumerate((("w2hi", -1 / 16), ("wlo", 1.0), ("whi", 1.0))):
            ts(T.W3[:, 8 * n:8 * n + 8], T.GM[:], vc(x), y, AL.mult, AL.mult, ["GM"] + vt(x), ["W3"])
    for n, x in enumerate(["nA2", "nA1", 0.5, 1, 0, "N2", "N1", 2, 6, 5, 1.0]):
        c_ = isinstance(x, str)
        if isinstance(x, int): fcp(T.W9[:, 32 * n:32 * n + 32], T.W9[:, 32 * x:32 * x + 32], ["W9_%d" % x], ["W9_%d" % n])
        else: ts(T.W9[:, 32 * n:32 * n + 32], T.GI[:], p4, vc(x) if c_ else x, AL.is_equal, AL.mult, ["GI"] + PF + (vt(x) if c_ else []), ["W9_%d" % n])

    def wide(n, a0, pn, s, st, x): ts(T[n][:, a0 + s:a0 + 128:st], T[pn][:, s::st], p4, vc(x), AL.is_equal, AL.mult, [pn] + PF + vt(x), [n + str(a0)])
    for a0, x in ((0, "cA"), (128, "cB")):
        wide("PA", 128 - a0, "PIW", 0, 1, x + "f"); wide("PA", 128 - a0, "PIW", 3, 4, x + "t")
        wide("PB", a0, "PJW", 0, 1, x + "f"); wide("PB", a0, "PJW", 2, 4, x + "t"); wide("PB", a0, "PJW", 14, 16, x + "f")
    for n, pn in (("PAV", "PIW"), ("PBV", "PJW")):
        wide(n, 0, pn, 0, 1, "cV"); ms(T[n][:, 15::16], 0.0, [n + "0"])
    WT = tk("W2", range(9)) + tk("W9", range(11)) + ["PA0", "PA128", "PB0", "PB128", "PAV0", "PBV0"]
    for n in ("ON", "ONH", "ONF"): io(T[n][:], [[0, 128]], 1, 0, [n])
    add({"g": (lambda: g.affine_select(T.IDN[:], T.ONF[:], [[-1, 128]], AL.is_equal, 0.0, 0, 1), 0.4)}, ["ONF"], ["IDN"])
    io(T.BCI[:], [[16, 16]], 15, 0, ["BCI"], False); cp(T.BC[:], T.BCI[:], ["BCI"], ["BC"])
    io(T.CV[0:1, 0:96], [[0, 3], [256, 8], [0, 4]], 0, 0, ["CV"]); io(T.CV[0:4, 96:192], [[0, 96]], 4096, 0, ["CV"])
    add({"g": (lambda: g.affine_select(T.CV[0:4, 96:192], T.CV[0:4, 96:192], [[0, 24], [1, 4]], AL.is_equal, 0.0, 0, -1), 0.35 + GOV)}, [], ["CV"])
    add({"g": (lambda: g.affine_select(T.IND[0:4, :], T.ONH[0:4, :], [[0, 8], [1, 4], [0, 4]], AL.is_equal, 0.0, 0, -1), 0.4 + GOV)}, ["ONH"], ["IND"])

    faff(T.BYI[:], T.IW[:, 0:256], w15, 0.0, ["IW0", "PWa"], ["BYI"])
    ts(T.BYI[:], T.BYI[:], 32768, None, AL.bitwise_and, None, ["BYI"], ["BYI"])
    faff(T.BYB[:], T.BYI[:], 1 / 32768, 0.0, ["BYI"], ["BYB"])
    for q in range(7):
        pb = tile()
        for u in range(2): mm([(ps(pb, 256 * u, 256 * u + 256), LB("LUT%d" % (2 * q + u)), T.BYB[:])], B0 + ["BYB"], [pb])
        fcp(T.W0[:, 512 * q:512 * q + 512], ps(pb, 0, 512), [pb], ["LUT%d" % q])
    LUT0 = ["LUT%d" % q for q in range(7)]
    dma("s", [(T.W1[:, 0:LUTW], T.W0[:, 0:LUTW])], LUT0 + ["CE", "W0r"], ["LUTc"], 8.0)

    def groups(n, w): return [list(range(a, min(n, a + 512 // w))) for a in range(0, n, 512 // w)]

    def chunk(r, v0, w):
        bl, nb, ns = list(range(v0 // 128, (v0 + w) // 128)), w // 128, w // 16

        def t_(n, x=0): return ["%s%d_%d" % (n, x, b % 2 if n.upper() in RING else b) for b in bl]

        def ts_(n, xs): return sum([t_(n, x) for x in xs], [])

        def at(buf, k): return k * (v0 % 256 if buf.name in RING else v0)

        def blk(buf, k, x, n=1): return buf[:, at(buf, k) + x * w:at(buf, k) + (x + n) * w]

        def sub(buf, k, x, b): return buf[:, at(buf, k) + x * w + 128 * b:at(buf, k) + x * w + 128 * (b + 1)]
        Gw, Wt, Wn = T["Gw%d" % r], T["W%d" % r], T["W%d" % (1 - r)]
        Ga, Gb, Pa, Pb = blk(T.GG, 2, 0), blk(T.GG, 2, 1), blk(T.PP, 2, 0), blk(T.PP, 2, 1)
        ga, gb, pp = t_("GG", 0), t_("GG", 1), t_("PP")
        gws, last = range(w // GW), v0 + w == V and FINE
        cgs = [[0, 1], [2]] if last else groups(3, w)

        def stage_a():
            gw = tk("Gw%d" % r, range(4)) + ["Gw%dr" % r, "fanU"]
            ts(Ga, Gw[:].indirect(T.fanU[:, v0 // 16:(v0 + w) // 16]), MG * r, vc("dcol"), AL.subtract, AL.max, gw + vt("dcol"), ga, GC)
            faff(Gb, Gw[:].indirect(T.fanU[:, (V + v0) // 16:(V + v0 + w) // 16]), 1.0, -MG * r, gw, gb, GC)
            ts(blk(T.PP, 2, 0, 2), blk(T.GG, 2, 0, 2), 0.5, None, AL.is_ge, None, ga + gb, pp, 0.5)
            chain = CHAIN[v0 // 128] and w == 128
            for bs in ([[9, 10], [0, 1, 2], [3, 4, 5], [6, 7, 8]] if chain else groups(11, w)):
                if not (chain and bs[0] in (3, 6)): pb = tile() + "a"
                for u, x in enumerate(bs):
                    l = ("SA%d" % SI[FULL[x]], "SB%d" % SJ[FULL[x]]) if x < 9 else (("I13", "R13") if x == 9 else ("R12", "I12"))
                    o = ps(pb, u * w, u * w + w)
                    if chain and 2 < x < 9: mm([(o, LF("SD%d" % (x // 3)), Gb)], F0 + gb, [pb], False, True)
                    elif chain and x < 3: mm([(o, LF(l[0]), Ga), (o, LF(l[1]), Gb)], F0 + ga + gb, [pb], x == 0, x == 2)
                    else: mm([(o, LF(l[0]), Ga), (o, LF(l[1]), Gb)], F0 + ga + gb, [pb])
                sign(blk(T.SG, 11, bs[0], len(bs)), ps(pb, 0, len(bs) * w), [pb], ts_("SG", bs))
                fne(blk(T.NE, 11, bs[0], len(bs)), blk(T.SG, 11, bs[0], len(bs)), ts_("SG", bs), ts_("NE", bs), NEA[v0 // 128])
            pb = tile()
            o = ps(pb, 0, w)
            mm([(o, LF("XC", 2), T.Gc[:, v0:v0 + w]), (o, LF("XC"), T.Gc[:, V + v0:V + v0 + w]), (o, LF("XL", 2), Ga), (o, LF("XL"), Gb),
                (o, LF("XP", 2), Pa), (o, LF("XP"), Pb)], F1 + ["Gc"] + ga + gb + pp, [pb])
            frelu(blk(T.XX, 1, 0), o, vc("bX"), [pb] + vt("bX"), t_("XX"))
            W2, W9, pv = T.W2, T.W9, tile() + "v"
            for b in range(nb):
                pb = tile()

                def sg(x): return sub(T.SG, 11, x, b)

                def ne(x): return sub(T.NE, 11, x, b)
                parts = [([(ps(pb, 0, 256), sub(T.PP, 2, 0, b), T.PA[:, 0:256]), (ps(pb, 256, 512), sub(T.PP, 2, 1, b), T.PB[:])], [])]
                for xs in (((0, 1, 2), (3, 4, 5), (6, 7, 8)) if chain else ((0, 1, 2, 3), (4, 5, 6, 7), (8,))):
                    parts.append((sum([[(ps(pb, FULL[x], 512, 16), sg(x), W2[:, 0:32]), (ps(pb, FULL[x], 512, 16), ne(x), W2[:, 32:64])] for x in xs], []), xs))
                for x, o, c0 in ((9, ps(pb, 3, 384, 4), 0), (10, ps(pb, 130, 512, 4), 64)):
                    parts[-1] = (parts[-1][0] + [(o, sg(x), W9[:, c0:c0 + 96]), (o, ne(x), W9[:, 160 + c0:256 + c0])], parts[-1][1] + (x,))
                parts = [(parts[0][0] + parts[1][0], parts[1][1])] + parts[2:]
                for n, (tr, xs) in enumerate(parts): mm(tr, WT + pp + ts_("SG", xs) + ts_("NE", xs), [pb], n == 0, n == len(parts) - 1)
                frelu(T.XT[:, 512 * bl[b]:512 * bl[b] + 512], ps(pb, 0, 512), 0.0, [pb], ["XT_%d" % bl[b]])
                a0 = 128 * b
                mm([(ps(pv, a0, a0 + 128), sub(T.PP, 2, 0, b), T.PAV[:]), (ps(pv, a0, a0 + 128), sub(T.PP, 2, 1, b), T.PBV[:])] +
                   [(ps(pv, a0 + FULL[x], a0 + 128, 16), ne(x), W2[:, 64:72]) for x in range(9)] +
                   [(ps(pv, a0 + 12 - x, a0 + 128, 4), ne(x), W9[:, 320:352]) for x in (9, 10)], WT + pp + ts_("NE", range(11)), [pv])
            frelu(blk(T.VT, 1, 0), ps(pv, 0, w), -4.0, [pv], t_("VT"))
            pb = tile()
            mm([(ps(pb, u * w, u * w + w), LF("X" + x), blk(T.XX, 1, 0)) for u, x in enumerate("AB")], F1 + t_("XX"), [pb], True, False)
            mm([(ps(pb, y // 2 * w + 128 * b, y // 2 * w + 128 * b + 128), T.XT[:, 512 * bl[b] + 128 * y:512 * bl[b] + 128 * y + 128], LF("I256"))
                for b in range(nb) for y in range(4)], F1 + tk("XT", bl), [pb], False, True)
            ts(blk(T.IX, 2, 0, 2), ps(pb, 0, 2 * w), float(WW - 1), None, AL.min, None, [pb], t_("IX"))

        def big(u): return slice(16 * (v0 + GW * u), 16 * (v0 + GW * (u + 1)))

        def gt(n, us): return ["%s_%d" % (n, v0 // GW + u) for u in us]

        def stage_b():
            wt = tk("W%d" % r, range(12)) + ["W%dr" % r] + (LUT0 if r == 0 else ["LUTc"])
            for u in gws:
                a0 = 2 * v0 + GW * u
                y = (v0 // GW + u) % (256 // GW)
                ag, agt = (T.AG[:, 16 * GW * y:16 * GW * (y + 1)], ["AG_%d" % y]) if SCAN else (T.AG[:, big(u)], gt("AG", [u]))
                fcp(ag, Wt[:].indirect(T.IX[:, a0:a0 + GW]), wt + t_("IX"), agt + ts_("XM", P16), GC)
                tt(T.AN[:, big(u)], Wt[:].indirect(T.IX[:, a0 + w:a0 + w + GW]), ag, AL.mult, wt + t_("IX") + agt, gt("AN", [u]), GC)
            for b in range(nb):
                a0, us = 16 * (v0 + 128 * b), range(128 * b // GW, 128 * (b + 1) // GW)
                if BT[r][bl[b]] == 2:
                    for y in us:
                        for u, (zm, bi) in enumerate((("Zc2", 4095.0 + CE0), ("Zc1", sum(WC1) + float(CE0)))):
                            pb, c0 = tile(), 16 * (v0 + GW * y)
                            mm([(ps(pb, 0, GW), LB(zm, 15 - q), T.AN[:, c0 + q:c0 + 16 * GW:16]) for q in P16], B1 + gt("AN", [y]), [pb])
                            c0 = 2 * v0 + u * w + GW * y
                            faff(T.CX[:, c0:c0 + GW], ps(pb, 0, GW), 1.0, bi, [pb], gt("CX%d" % u, [y]))
                    continue
                if BT[r][bl[b]]:
                    pb, ct, c0 = tile(), "CT%d" % (bl[b] % 2), 384 * (bl[b] % 2)
                    for q0 in (0, 8):
                        add({"t": (lambda pb=pb, q0=q0, a0=a0: [ten.matmul(rs(ps(pb, q, 384, 16)), T.AN[:, a0 + q:a0 + 2048:16], T.W3[:], True, True)
                                                                for q in range(q0, q0 + 8)][-1], 8 * (POV + PMIN * PEC))}, ["W3"] + gt("AN", us), [pb], 0.05)
                    faff(T.CT[:, c0:c0 + 384], ps(pb, 0, 384), 1.0, 2048.0, [pb], [ct])
                    for u, (ys, bi) in enumerate((((0,), 4095.0 + CE0 - 2048), ((1, 2), sum(WC1) + CE0 - 4096.0))):
                        pb = tile()
                        mm([(ps(pb, 0, 128), T.CT[:, c0 + 128 * y:c0 + 128 * y + 128], LF("I256")) for y in ys], F1 + [ct], [pb])
                        faff(sub(T.CX, 2, u, b), ps(pb, 0, 128), 1 / 256, bi, [pb], gt("CX%d" % u, us))
                    continue
                for u, (zm, bi) in enumerate((("Zc2", 4095.0 + CE0), ("Zc1", sum(WC1) + float(CE0)))):
                    pb = tile()
                    mm([(ps(pb, 0, 128), LB(zm, 15 - q), T.AN[:, a0 + q:a0 + 2048:16]) for q in P16], B1 + gt("AN", us), [pb])
                    faff(sub(T.CX, 2, u, b), ps(pb, 0, 128), 1.0, bi, [pb], gt("CX%d" % u, us))
        key = []

        def stage_c():
            if SCAN:
                pb = tile()
                key.append(pb)
                for b in range(nb):
                    p, us = bl[b] % RD, range(128 * b // GW, 128 * (b + 1) // GW)
                    c0, rq = 4096 * p, T.RQ[:, v0 + 128 * b:v0 + 128 * b + 128]
                    for q in (P16 if r == 0 or RD < 4 else []):
                        o = T.D1[:, c0 + 2 * q + 1:c0 + 4096:32]
                        add({"g": (lambda o=o, rq=rq: g.affine_select(o, rq, [[0, 128]], AL.is_ge, 0.0, 0, 0), 0.39)}, ["RQ"], ["DR%d_%d" % (p, q)])
                    for u in us:
                        a0, y = 2 * v0 + GW * u, (v0 // GW + u) % (256 // GW)
                        s0, s1 = 32 * GW * y, c0 + 32 * GW * (u - us[0])
                        dr = tk("DR%d" % p, P16)
                        fcp(T.D0[:, s0 + 1:s0 + 32 * GW:2], T.CE[:].indirect(T.CX[:, a0:a0 + GW]), ["CE", "D0z"] + gt("CX0", [u]), ["D0_%d" % y], GC)
                        fcp(T.D1[:, s1:s1 + 32 * GW:2], T.CE[:].indirect(T.CX[:, a0 + w:a0 + w + GW]), ["CE"] + dr + gt("CX1", [u]), ["D1_%d" % (s1 // 32)], GC)
                        add({"v": (lambda s0=s0, s1=s1: vec.tensor_tensor_scan(T.DO[:, s0:s0 + 32 * GW], T.D0[:, s0:s0 + 32 * GW], T.D1[:, s1:s1 + 32 * GW], 0.0, AL.min, AL.max),
                                   OVH + 16 * GW * CY)}, ["D0z", "D0_%d" % y, "D1_%d" % (s1 // 32)] + dr, ["DO_%d" % y])
                    o, c0 = ps(pb, 128 * b, 128 * b + 128), 4096 * (bl[b] % 2)
                    mm([(o, LB("IV"), sub(T.VT, 1, 0, b)), (o, rq, LB("ONE0"))], B1 + ["RQ"] + t_("VT"), [pb], True, False)
                    mm([(ps(pb, 128 * b + q, 128 * b + 128, 16), T.DO[:, c0 + 2 * q + 1:c0 + 4096:32], T.GN[:]) for q in P16] + [(o, T.ON[:], LB("KC"))],
                       B1 + ["GN", "ON"] + ["DO_%d" % ((v0 // GW + u) % (256 // GW)) for u in us], [pb], False, True)
                return
            for u in gws:
                a0, b = 2 * v0 + GW * u, (v0 + GW * u) // 128
                fcp(T.AG[:, big(u)], T.CE[:].indirect(T.CX[:, a0:a0 + GW]), ["CE"] + gt("CX0", [u]), gt("AG", [u]), GC)
                tt(T.XG[:, big(u)], T.CE[:].indirect(T.CX[:, a0 + w:a0 + w + GW]), T.AG[:, big(u)], AL.min,
                   ["CE"] + gt("CX1", [u]) + gt("AG", [u]), gt("XG", [u]), GC)
            NF = NFS[r][sum(1 for x in range(len(CH[r])) if sum(CH[r][:x]) < v0)]
            if NF < 0:
                for u in gws: fold(r, v0 // GW + u, gt("XG", [u]) + ["RP%d_%d" % (q, (v0 + GW * u) // 128) for q in P16], gt("AG", [u]))
                pb = tile()
                key.append(pb)
                for b in range(nb):
                    a0, c0 = 128 * b, 16 * (v0 + 128 * b)
                    o = ps(pb, a0, a0 + 128)
                    mm([(o, LB("IV"), sub(T.VT, 1, 0, b)), (o, T.RQ[:, v0 + a0:v0 + a0 + 128], LB("ONE0"))] +
                       [(ps(pb, a0 + q, a0 + 128, 16), T.AG[:, c0 + q:c0 + 2048:16], T.GN[:]) for q in P16] + [(o, T.ON[:], LB("KC"))],
                       B1 + ["GN", "ON", "RQ"] + t_("VT") + gt("AG", range(128 * b // GW, 128 * (b + 1) // GW)), [pb])
                return

            def xg(q): return T.XG[:, 16 * v0 + q:16 * (v0 + w):16]

            def xf(q, a, n): return T.XF[:, (q - 16 + NF) * w + a:(q - 16 + NF) * w + a + n]

            def xt(qs): return [("XM%d_%d" % (q, b) if q < 16 - NF else "XF%d" % ((q - 16 + NF) * w // 512)) for q in qs for b in bl]
            for q in range(16 - NF):
                tt(blk(T.AG, 16, q), xg(q), ps("rq", v0, v0 + w), AL.max, ["rq"] + gt("XG", gws), xt([q]), 1.0)
            for qs in groups(NF, w):
                qs, pb = [16 - NF + q for q in qs], tile()
                for u, q in enumerate(qs):
                    o = ps(pb, u * w, u * w + w)
                    mm([(o, LB("IDn"), T.RQ[:, v0:v0 + w]), (o, LB("ID"), xg(q))], B1 + ["RQ"] + gt("XG", gws), [pb])
                frelu(xf(qs[0], 0, len(qs) * w), ps(pb, 0, len(qs) * w), 0.0, [pb], xt(qs))
            pb = tile()
            key.append(pb)
            for b in range(nb):
                a0 = 128 * b
                o = ps(pb, a0, a0 + 128)
                for q0 in range(0, 16, QS):
                    mm([(o, LB("IV"), sub(T.VT, 1, 0, b))] * (q0 == 0) + [(o, T.RQ[:, v0 + a0:v0 + a0 + 128], LB("ONE%d" % min(NF, NFV[-1])))] * (q0 == 0 and NF < 16) +
                       [(ps(pb, a0 + q, a0 + 128, 16), sub(T.AG, 16, q, b), T.GN[:]) if q < 16 - NF else (ps(pb, a0 + q, a0 + 128, 16), xf(q, a0, 128), T.GNF[:])
                        for q in range(q0, q0 + QS)] + [(o, T.ON[:], LB("KC"))] * (q0 + QS == 16),
                       B1 + ["GN", "GNF", "ON", "RQ"] + t_("VT") + xt(range(q0, q0 + QS)), [pb], q0 == 0, q0 + QS == 16)

        def stage_d():
            pb = key[0]
            K, K0, K1, bc = ps(pb, 0, w), blk(T.NK0, 1, 0), blk(T.NK1, 1, 0), T.BC[:, 0:ns]
            ac(K0, K, [pb], t_("NK0"))
            ac(K1, K0, t_("NK0"), t_("NK1"), AF.Identity, 0.5)
            for c in range(3):
                sc = blk(T.SC, 3, c)
                scan(sc, T.RST[:, 0:w], blk(T.NKN, 2, c - 1) if c else K, 0.0, AL.mult, AL.max, ["RST"] + (t_("NKN", c - 1) if c else [pb]), t_("SC", c))
                if c < 2:
                    tt(blk(T.KP, 2, c), sc.indirect(bc), K1, AL.is_gt, t_("SC", c) + t_("NK1") + ["BC"], t_("KP", c), GC)
                    tt(blk(T.NKN, 2, c), blk(T.KP, 2, c), K, AL.mult, t_("KP", c) + [pb], t_("NKN", c), 1.0)
                tt(blk(T.MT, 3, c), sc.indirect(bc), K0, AL.is_equal, t_("SC", c) + t_("NK0") + ["BC"], t_("MT", c), GC)
            for cs in cgs:
                pb = tile()
                for u, c in enumerate(cs):
                    for b in range(nb): mm([(ps(pb, u * w + 128 * b, u * w + 128 * b + 128), sub(T.MT, 3, c, b), LF("I256"))], F1 + t_("MT", c), [pb])
                fcp(blk(T.MK, 3, cs[0], len(cs)), ps(pb, 0, len(cs) * w), [pb], ts_("MK", cs))
            for cs in (cgs if last and FINE > 1 else [[0, 1, 2]]):
                pb, n, a0 = tile(), len(cs) * ns, at(T.MK, 3) + cs[0] * w
                o, ls = ps(pb, 0, 4 * n), blk(T.LS, 1, 0)
                mm([(o, T.ONH[0:1, :], T.CV[0:1, 0:4 * n]), (o, T.IND[0:4, :], T.CV[0:4, 96:96 + 4 * n])] +
                   [(o, LF("LP", 3 - x), T.MK[:, a0 + x:a0 + len(cs) * w:4]) for x in range(4)], F2 + ["ONH", "CV", "IND"] + ts_("MK", cs), [pb])
                scan(T.LS[:, v0:v0 + 4 * n], T.RST[:, 0:16 * n:4], o, 0.0, AL.mult, AL.max, ["RST", pb], t_("LS"))
                a0 = 3 * v0 // 16 + cs[0] * ns
                faff(T.LU[:, a0:a0 + n], T.LS[:, v0 + 3:v0 + 4 * n:4], 1.0, vc("p256"), t_("LS") + vt("p256"), ts_("LU", cs))
            if r == 1:
                M, s, n = T.SC[:, at(T.SC, 3) + 15:at(T.SC, 3) + 3 * w:16], slice(3 * v0 // 16, 3 * (v0 + w) // 16), 3 * ns
                faff(T.Q5[:, s], M, 1.0, -524287.0 - MG, ts_("SC", range(3)), t_("Q5"))
                add({"v": vts(T.Q6[:, s], M, 0.0, 524288.0, AL.is_le, AL.mult), "a": aac(T.Q6[:, s], M, AF.Relu, 524288.0, -524288.0)}, ts_("SC", range(3)), t_("Q6"))
                pb = tile()
                o = ps(pb, 0, 128, 1, n)
                tt(T.Q5[:, s], T.Q5[:, s], T.Q6[:, s], AL.add, t_("Q5") + t_("Q6"), t_("Q5"))
                mm([(o, T.Q5[:, s], T.IDN[:])], t_("Q5") + ["IDN"], [pb])
                faff(T.YC[0:n, v0:v0 + 128], o, -1.0, -MG, [pb], t_("YC"))
                dma("s", [(T.yc[:, c * V + 128 * bl[b]:c * V + 128 * bl[b] + 128], T.YC[8 * (c * nb + b):8 * (c * nb + b) + 8, v0:v0 + 128])
                          for c in range(3) for b in range(nb)], t_("YC"), [])

        def stage_e():
            wn = [tk("W%d" % (1 - r), [3 * b + c for b in bl]) for c in range(3)]
            bits = [Wn[:, LUTW + WN * c + v0:LUTW + WN * c + v0 + w] for c in range(3)]
            for c in range(3):
                a0 = 3 * v0 // 16 + c * ns
                faff(bits[c], T.AN[:, 16 * v0:16 * (v0 + w)].indirect(T.LU[:, a0:a0 + ns]), -1.0, 1.0, gt("AN", gws) + t_("LU", c), wn[c], GC)
            if r == 0 and v0 + w == BORD: send_b(1)
            for cs in cgs:
                c0, n = cs[0], len(cs)
                for R, G, gk, x in ((T.RA, Ga, ga, "a"), (T.RB, Gb, gb, "b")):
                    pb = tile()
                    mm([(ps(pb, 0, n * w), LF("RM" + x), blk(T.MK, 3, c0, n))] + [(ps(pb, u * w, u * w + w), LF("J13"), G) for u in range(n)],
                       F2 + gk + ts_("MK", cs), [pb])
                    frelu(blk(R, 3, c0, n), ps(pb, 0, n * w), vc("bR" + x), [pb] + vt("bR" + x), ts_("R" + x, cs))
                ra, rb, s2, e2, rk = blk(T.RA, 3, c0, n), blk(T.RB, 3, c0, n), blk(T.S2, 3, c0, n), blk(T.E2, 3, c0, n), F2 + ts_("Ra", cs) + ts_("Rb", cs)
                pb = tile()
                o = ps(pb, 0, n * w)
                mm([(o, LF("EA"), ra), (o, LF("EB"), rb)], rk, [pb])
                sign(s2, o, [pb], ts_("S2", cs)); fne(e2, s2, ts_("S2", cs), ts_("E2", cs), NEA[4])
                pb = tile()
                o = ps(pb, 0, n * w)
                mm([(o, LF("HA"), ra), (o, LF("HB"), rb), (o, LF("Hs"), s2)], rk + ts_("S2", cs), [pb], True, False)
                mm([(o, LF("He"), e2)], ts_("E2", cs), [pb], False, True)
                ts(blk(T.HH, 3, c0, n), o, 0.0, 4096.0, AL.max, AL.min, [pb], ts_("HH", cs))
            pb = tile()
            o = ps(pb, 0, w)
            parts = []
            for cs in (cgs if last else [[0, 1, 2]]):
                pr = [(o, LF("E12"), blk(T.IDf, 1, 0))] * (r == 0 and cs[0] == 0)
                for c in cs: pr += [(o, LF("UA", 8 - 4 * c), blk(T.RA, 3, c))] + [(o, LF("UE", 2 - c), blk(T.RB, 3, c))] * r
                hh, R = [(o, LF("UH", 8 - 4 * c), blk(T.HH, 3, c)) for c in cs], F2 + B1 + ["IDf"] + ts_("Ra", cs) + ts_("Rb", cs)
                zz = ([(o, LB("ZT" if r else "Zlb", 2 - c), bits[c]) for c in range(3)], sum(wn, []))
                if not last: parts = [(pr + zz[0] + hh, R + zz[1] + ts_("HH", cs))]
                else: parts += [(pr, R), zz, (hh, ts_("HH", cs))] if cs[-1] == 2 else [(pr + hh, R + ts_("HH", cs))]
            for n, (pr, R) in enumerate(parts): mm(pr, R, [pb], n == 0, n == len(parts) - 1)
            ops[-1]["b"] = BV[v0 // 128]
            if r == 0:
                faff(blk(T.Gw1, 1, 0), o, 1.0, vc("bM"), [pb] + vt("bM"), tk("Gw1", bl))
                if v0 + w == BORD: send_g(1)
            else:
                Y, YP, y = blk(T.Y, 1, 0), blk(T.YP, 1, 0), t_("Y")
                faff(Y, o, vc("sY"), vc("bY"), [pb] + vt("bY", "sY"), y)
                Z = blk(T.NK0, 1, 0)
                frelu(Z, Y, -MG, y, t_("NK0"))
                ts(YP, Y, MG + 2048, vc("thr"), AL.is_ge, AL.mult, y + vt("thr"), t_("YP"))
                tt(Y, Z, YP, AL.subtract, t_("NK0") + t_("YP"), y)
                if v0 + w in (V - CH[1][-1], V):
                    a0 = 0 if v0 + w < V else v0
                    ys, a1 = ["Y0_%d" % b for b in range(a0 // 128, (v0 + w) // 128)], v0 + w
                    prs = [(T.yl[:, f * V + a0:f * V + a1], T.Y[f::16, a0:a1]) for f in range(12)] + \
                          [(T.yt[:, c * V + a0:c * V + a1], T.Y[13 + c::16, a0:a1]) for c in range(3)]
                    if a1 < V: dma("s", prs, ys, [])
                    else: dma("s", prs[:8], ys, []); dma("a", prs[8:], ys, [])
        return [stage_a, stage_b, stage_c, stage_d, stage_e]
    for r in range(2):
        cs = [chunk(r, sum(CH[r][:h]), CH[r][h]) for h in range(len(CH[r]))]
        for ks in ((0,), (1,), (2, 3, 4)):
            for st in cs:
                for k in ks:
                    a0 = len(ops)
                    st[k]()
                    for o in ops[a0:]: o["r"] = RW[cs.index(st)] * (k >= RK)

    if not EST: EST[:] = _plan(ops, users)
    order = EST[1]
    bankof.update(EST[3])
    for o, e, d in zip(ops, EST[2], EST[4]): o.update({"e": e, "d": o["d"] | d})
    qs = {"v": vec, "a": act, "t": ten, "g": g, "s": g.sync}
    cnt, seen, final = {"v": 0, "a": 0, "t": 0, "g": 0}, {}, {}
    for i in order:
        o = ops[i]
        e = o["e"]
        if o["s"] is None:
            cnt[e] += 1; o["w"] = ("s" + e, cnt[e])
        else:
            o["w"] = (o["s"], o["n"])
        if o["s"] != "loc": final[o["w"][0]] = o["w"][1]
        if e == "x": continue
        need = {}
        for d in o["d"]:
            if e == "t" and ops[d]["e"] == "t": continue
            s, c = ops[d]["w"]
            need[s] = max(need.get(s, 0), c)
        for s, c in need.items():
            if seen.get((e, s), 0) < c:
                qs[e].wait_ge(T.sem[s], c); seen[(e, s)] = c
        x = o["a"][e][0]()
        if o["s"] is None: x.then_inc(T.sem[o["w"][0]], 1)
    final["loc"] = locn[0]
    for s, c in final.items(): g.wait_ge(T.sem[s], c)
